import numpy as np
import ml_dtypes


def mxq(x, axis, fmt="e4m3"):
    dtype, down = {"e4m3": (ml_dtypes.float8_e4m3fn, 7), "e5m2": (ml_dtypes.float8_e5m2, 14)}[fmt]
    v = np.moveaxis(np.asarray(x, np.float32).astype(ml_dtypes.bfloat16).astype(np.float64), axis, -1)
    blocks = v.reshape(v.shape[:-1] + (-1, 32))
    amax = np.abs(blocks).max(-1, keepdims=True)
    byte = np.maximum(np.where(amax > 0, np.frexp(amax)[1] - 1 + 127, 0) - down, 1)
    scale = np.exp2(byte - 127.0)
    codes = (blocks / scale).astype(np.float32).astype(dtype).astype(np.float64)
    return np.moveaxis((codes * scale).reshape(v.shape), -1, axis)


WIDE = False


def mx_kscale(k):
    if not WIDE:
        return np.ones(k)
    levels = np.array([24, -24, 12, -12, 0])
    if k % 512:
        return np.exp2(np.random.permutation(np.resize(levels, k // 32))).repeat(32)
    a = np.empty((k // 512, 16))
    for p in range(k // 512):
        a[p, :8] = np.random.permutation(np.resize(levels, 8))
        for g in range(8):
            far = levels[np.abs(levels - a[p, g]) >= 10]
            a[p, g + 8] = far[np.random.randint(len(far))]
    return np.exp2(a.ravel()).repeat(32)


def f64(x):
    return np.asarray(x).astype(np.float64)


def striped(idx):
    return np.tile(idx.reshape(-1, 16).T, (8, 1)).astype(np.uint16)


def unstriped(offs):
    return offs[:16].T.reshape(-1).astype(np.int64)


E2M1 = np.array([0.0, 0.5, 1.0, 1.5, 2.0, 3.0, 4.0, 6.0, -0.0, -0.5, -1.0, -1.5, -2.0, -3.0, -4.0, -6.0])


def pack_weight(w, fmt):
    k, n = w.shape
    w = f64(np.asarray(w, np.float32).astype(ml_dtypes.bfloat16)).reshape(k // 32, 32, n)
    amax = np.abs(w).max(1)
    if fmt == "e4m3":
        byte = np.frexp(amax)[1] - 1 + 127 - 7
    else:
        mant, ex = np.frexp(amax / 6.0)
        byte = np.where(mant > 0.5, ex, ex - 1) + 127
    byte = np.clip(np.where(amax > 0, byte, 1), 1, 254)
    scaled = (w * np.exp2(127.0 - byte)[:, None, :]).reshape(k, n).astype(np.float32)
    by_word = np.ascontiguousarray(scaled.reshape(k // 512, 128, 4, n).transpose(0, 1, 3, 2))
    if fmt == "e4m3":
        words = by_word.astype(ml_dtypes.float8_e4m3fn).view(np.uint8)
    else:
        c = by_word.astype(ml_dtypes.float4_e2m1fn).view(np.uint8) & 0xF
        words = (c[..., 0::2] | (c[..., 1::2] << 4)).reshape(k // 512, 128, 2 * n)
    return np.ascontiguousarray(words), np.ascontiguousarray(byte.astype(np.uint8).reshape(k // 512, 16, n))


def unpack_weight(words, scales, fmt):
    g, _, n = scales.shape
    words = np.ascontiguousarray(words).reshape(g, 128, n, -1)
    if fmt == "e4m3":
        vals = words.view(ml_dtypes.float8_e4m3fn).astype(np.float64)
    else:
        nib = np.empty((g, 128, n, 4), np.uint8)
        nib[..., 0::2] = words & 0xF
        nib[..., 1::2] = words >> 4
        vals = E2M1[nib]
    vals = vals * np.repeat(np.exp2(scales.astype(np.float64) - 127.0), 8, axis=1)[..., None]
    return vals.transpose(0, 1, 3, 2).reshape(g * 512, n)


def pack_table4(v):
    words, scales = pack_weight(v, "e2m1")
    g, t = words.shape[0] // 2, v.shape[1]
    return np.ascontiguousarray(words.reshape(g, 2, 128, t, 2).transpose(0, 2, 3, 1, 4).reshape(g, 128, t, 4)), scales


def unpack_table4(words, scales):
    g, _, t, _ = words.shape
    return unpack_weight(words.reshape(g, 128, t, 2, 2).transpose(0, 3, 1, 2, 4).reshape(2 * g, 128, 2 * t), scales, "e2m1")


def sigm(f):
    return 1.0 / (1.0 + np.exp(-np.maximum(f, -700.0)))


K, N, T, J = 1024, 512, 2048, 1024


def setup_inputs():
    n = np.random.standard_normal
    s = mx_kscale(K)[:, None]
    p_tab = pack_table4(n((K, T)) * s)
    p_wb = pack_weight(n((K, N)) / np.sqrt(2 * K) / s, "e2m1")
    p_wc = pack_weight(n((K, N)) / np.sqrt(K) / s, "e4m3")
    return {
        "tab_words": p_tab[0],
        "tab_scales": p_tab[1],
        "wa": (n((K, N)) / np.sqrt(2 * K) / s).astype(np.float32),
        "wb_words": p_wb[0],
        "wb_scales": p_wb[1],
        "wc_words": p_wc[0],
        "wc_scales": p_wc[1],
        "wgo": np.tile(np.random.uniform(0.5, 2.0, J), (128, 1)).astype(np.float32),
        "offs": striped(np.random.permutation(T)[:J]),
        "offs2": striped(np.random.permutation(T)[:J]),
    }


def reference(tab_words, tab_scales, wa, wb_words, wb_scales, wc_words, wc_scales, wgo, offs, offs2):
    idx = unstriped(offs)
    idx2 = unstriped(offs2)
    tab_ = unpack_table4(tab_words, tab_scales)[:, idx]
    tabb_ = unpack_table4(tab_words, tab_scales)[:, idx2]
    wa_ = mxq(f64(wa), 0, "e4m3")
    wb_ = unpack_weight(wb_words, wb_scales, "e2m1")
    za = wa_.T @ tabb_ + wb_.T @ tab_
    eta = sigm(za)
    wc_ = unpack_weight(wc_words, wc_scales, "e4m3")
    ms = wc_.T @ tab_
    out = np.zeros((N, T))
    out[:, idx2] = f64(wgo)[0] * (np.maximum(eta * ms, 0.0))
    return out

@@ -1,0 +1,203 @@
+from contextlib import ExitStack
+
+import concourse.mybir as mybir
+from concourse.masks import make_identity
+
+K, N, T, J = 1024, 512, 2048, 1024
+FLOPS = 3 * 2 * K * N * J
+
+F32 = mybir.dt.float32
+BF16 = mybir.dt.bfloat16
+I32 = mybir.dt.int32
+U32 = mybir.dt.uint32
+U16 = mybir.dt.uint16
+U8 = mybir.dt.uint8
+FP8X4 = mybir.dt.float8_e4m3fn_x4
+FP4X4 = mybir.dt.float4_e2m1fn_x4
+ACT = mybir.ActivationFunctionType
+MULT = mybir.AluOpType.mult
+
+P = 128
+PASSES = K // 512
+HALF = J // 2
+TILES = N // P
+BLOCKS = HALF // P
+SPARE = 8
+
+
+def tile_list_rgg_relu_kernel(
+    tc, tab_words, tab_scales, wa, wb_words, wb_scales, wc_words, wc_scales, wgo, offs, offs2, out
+):
+    nc = tc.nc
+    with ExitStack() as ctx:
+        keep = ctx.enter_context(tc.tile_pool(name="keep", bufs=1))
+        ring = ctx.enter_context(tc.tile_pool(name="ring", bufs=2))
+        psum = ctx.enter_context(tc.psum_pool(name="psum", bufs=1))
+
+        src_list = keep.tile([P, J // 16], U16, name="src_list")
+        dst_list = keep.tile([P, J // 16], U16, name="dst_list")
+        tab_w = keep.tile([P, T], I32, name="tab_w", align_bytes=64)
+        tab_s = keep.tile([P, T // 4], I32, name="tab_s", align_bytes=64)
+        wb_w = keep.tile([P, PASSES, N // 2], I32, name="wb_w", align_bytes=64)
+        wc_w = keep.tile([P, PASSES, N], I32, name="wc_w", align_bytes=64)
+        wb_s = keep.tile([P, PASSES * N // 4], I32, name="wb_s", align_bytes=64)
+        wc_s = keep.tile([P, PASSES * N // 4], I32, name="wc_s", align_bytes=64)
+        picked_s = keep.tile([P, 2 * J], U8, name="picked_s", align_bytes=64)
+        moved_s = keep.tile([P, 2 * J // 4], I32, name="moved_s", align_bytes=64)
+        wa_raw = [keep.tile([P, 4, N], F32, name=f"wa_raw{a}") for a in range(PASSES)]
+        wa_w = [keep.tile([P, N], U32, name=f"wa_w{a}", align_bytes=64) for a in range(PASSES)]
+        wa_s = [keep.tile([P, N], U8, name=f"wa_s{a}", align_bytes=64) for a in range(PASSES)]
+        pages = [keep.tile([P, T], F32, name="page0")]
+        ident = keep.tile([P, P], F32, name="ident")
+        wgo_rows = keep.tile([P, P], F32, name="wgo_rows")
+        wgo_cols = keep.tile([P, J // P], F32, name="wgo_cols")
+        warm = keep.tile([P, 1], F32, name="warm")
+
+        nc.vector.memset(tab_s[:], 0)
+        nc.vector.memset(wc_s[:], 0)
+        nc.vector.memset(wb_s[:], 0)
+        nc.vector.memset(moved_s[:], 0)
+        nc.vector.memset(pages[0][:], 0.0)
+        nc.gpsimd.memset(wgo_rows[:], 0.0)
+        nc.gpsimd.dma_start(out=wgo_rows[0 : J // P, :], in_=wgo[0:1, :].rearrange("o (c p) -> (o c) p", p=P))
+        make_identity(nc, ident[:])
+        nc.scalar.activation(warm[:], ident[:, 0:1], ACT.Sigmoid)
+
+        def load_wa(a):
+            nc.sync.dma_start(out=wa_raw[a][:], in_=wa[512 * a : 512 * (a + 1), :].rearrange("(p i) n -> p i n", i=4))
+
+        def load_weight_scales(plane, scales, q):
+            nc.scalar.dma_start(
+                out=plane[32 * q : 32 * q + 4, :].rearrange("r (a n) -> r a n", a=PASSES),
+                in_=scales[:, 4 * q : 4 * q + 4, :].rearrange("a r n -> r a n").bitcast(I32),
+            )
+
+        nc.sync.dma_start(src_list[:], offs)
+        for q in range(4):
+            nc.sync.dma_start(out=tab_s[32 * q : 32 * q + 4, :], in_=tab_scales[0, 4 * q : 4 * q + 4, :].bitcast(I32))
+        nc.sync.dma_start(out=tab_s[SPARE : SPARE + 16, :], in_=tab_scales[1].bitcast(I32))
+        nc.sync.dma_start(dst_list[:], offs2)
+        nc.sync.dma_start(out=tab_w[:], in_=tab_words[0].rearrange("p t b -> p (t b)").bitcast(I32))
+        load_wa(0)
+        for q in range(4):
+            load_weight_scales(wc_s, wc_scales, q)
+        for q in range(2):
+            load_weight_scales(wb_s, wb_scales, q)
+        load_wa(1)
+        nc.sync.dma_start(out=wc_w[:], in_=wc_words.rearrange("a p n i -> p a (n i)").bitcast(I32))
+        for q in range(2, 4):
+            load_weight_scales(wb_s, wb_scales, q)
+
+        lists = (src_list, dst_list)
+        for e in range(2):
+            nc.vector.tensor_copy(picked_s[:, e * J : (e + 1) * J], tab_s[:].bitcast(U8).indirect(lists[e][:]))
+        for q in range(4):
+            nc.sync.dma_start(
+                out=moved_s[32 * q : 32 * q + 4, :],
+                in_=picked_s[SPARE + 4 * q : SPARE + 4 * q + 4, :].bitcast(I32),
+            )
+        nc.sync.dma_start(out=wb_w[:], in_=wb_words.rearrange("a p n -> p a n").bitcast(I32))
+
+        wgo_bank = psum.tile([P, HALF], F32, name="wgo_bank", tag="turned", bufs=3)
+        nc.tensor.transpose(wgo_bank[:, 0:P], wgo_rows[:], ident[:])
+        nc.scalar.copy(wgo_cols[:], wgo_bank[:, 0 : J // P])
+
+        def picked_scales(e, a, cols):
+            plane = picked_s[:] if a == 0 else moved_s[:].bitcast(U8)
+            return plane[:, e * J + cols.start : e * J + cols.stop]
+
+        parted = {}
+
+        def pick_words(e, h, tag):
+            both = keep.tile([P, HALF], U32, name=f"both{e}{h}", tag=tag, align_bytes=64)
+            cols = slice(h * HALF // 16, (h + 1) * HALF // 16)
+            nc.vector.tensor_copy(both[:], tab_w[:].bitcast(U32).indirect(lists[e][:, cols]))
+            parted[e, h] = keep.tile([P, PASSES, HALF], U16, name=f"parted{e}{h}", align_bytes=64)
+            nc.vector.tensor_copy(parted[e, h][:], both[:].bitcast(U16).rearrange("p (j d) -> p d j", d=PASSES))
+
+        def quantise_wa(a):
+            rounded = keep.tile([P, N, 4], BF16, name=f"rounded{a}", tag=f"stage{a}", align_bytes=64)
+            nc.scalar.copy(
+                rounded[:].rearrange("p (c u) i -> p c i u", u=4),
+                wa_raw[a][:].rearrange("p i (c u) -> p c i u", u=4),
+            )
+            nc.vector.quantize_mx(
+                out=wa_w[a][:].bitcast(FP8X4), scales=wa_s[a][:], in_=rounded[:].rearrange("p n i -> p (n i)")
+            )
+
+        pick_words(0, 0, "first0")
+        pick_words(1, 0, "first1")
+        quantise_wa(0)
+        pick_words(0, 1, "stage0")
+        quantise_wa(1)
+        pick_words(1, 1, "stage1")
+        pages.append(keep.tile([P, T], F32, name="page1", tag="stage1", align_bytes=64))
+        nc.gpsimd.memset(pages[1][:], 0.0)
+
+        def half_unit(t, h, gate, message):
+            n_cols = slice(t * P, (t + 1) * P)
+            j_cols = slice(h * HALF, (h + 1) * HALF)
+            ms_bank = psum.tile([P, HALF], F32, name="ms_bank", tag="ms", bufs=2)
+            for b in range(BLOCKS):
+                for a in range(PASSES):
+                    nc.tensor.matmul_mx(
+                        out=ms_bank[:, b * P : (b + 1) * P],
+                        lhsT=parted[0, h][:, a, b * P : (b + 1) * P].bitcast(FP4X4),
+                        lhsT_scale=picked_scales(0, a, slice(h * HALF + b * P, h * HALF + (b + 1) * P)),
+                        rhs=wc_w[:, a, n_cols].bitcast(FP8X4),
+                        rhs_scale=wc_s[:].bitcast(U8)[:, a * N + t * P : a * N + (t + 1) * P],
+                        start=(a == 0),
+                        stop=(a == PASSES - 1),
+                    )
+            positive = ring.tile([P, HALF], F32, name="positive")
+            nc.scalar.activation(positive[:], ms_bank[:], ACT.Relu)
+            weighted = ring.tile([P, HALF], F32, name="weighted")
+            for b in range(BLOCKS):
+                c = h * BLOCKS + b
+                nc.scalar.activation(
+                    weighted[:, b * P : (b + 1) * P], positive[:, b * P : (b + 1) * P], ACT.Copy,
+                    scale=wgo_cols[:, c : c + 1],
+                )
+            za_bank = psum.tile([P, HALF], F32, name="za_bank", tag="za", bufs=3)
+            for a in range(PASSES):
+                nc.tensor.matmul_mx(
+                    out=za_bank[:],
+                    lhsT=wb_w[:, a, t * P // 2 : (t + 1) * P // 2].bitcast(FP4X4),
+                    lhsT_scale=wb_s[:].bitcast(U8)[:, a * N + t * P : a * N + (t + 1) * P],
+                    rhs=parted[0, h][:, a, :].bitcast(FP4X4),
+                    rhs_scale=picked_scales(0, a, j_cols),
+                    start=(a == 0),
+                    stop=False,
+                )
+            for a in range(PASSES):
+                nc.tensor.matmul_mx(
+                    out=za_bank[:],
+                    lhsT=wa_w[a][:, n_cols].bitcast(FP8X4),
+                    lhsT_scale=wa_s[a][:, n_cols],
+                    rhs=parted[1, h][:, a, :].bitcast(FP4X4),
+                    rhs_scale=picked_scales(1, a, j_cols),
+                    start=False,
+                    stop=(a == PASSES - 1),
+                )
+            turned = psum.tile([P, HALF], F32, name="turned", tag="turned", bufs=3)
+            for b in range(BLOCKS):
+                nc.tensor.transpose(turned[:, b * P : (b + 1) * P], weighted[:, b * P : (b + 1) * P], ident[:])
+            nc.scalar.activation(gate, za_bank[:], ACT.Sigmoid)
+            nc.scalar.copy(message, turned[:])
+
+        for t in range(TILES):
+            page = pages[t % 2]
+            if t < 2:
+                for h in range(2):
+                    gate = ring.tile([P, HALF], F32, name="gate_half", bufs=3)
+                    message = ring.tile([P, HALF], F32, name="message_half", bufs=3)
+                    half_unit(t, h, gate[:], message[:])
+                    cols = slice(h * HALF // 16, (h + 1) * HALF // 16)
+                    nc.vector.tensor_tensor(page[:].indirect(dst_list[:, cols]), gate[:], message[:], MULT)
+            else:
+                gate = ring.tile([P, J], F32, name="gate")
+                message = ring.tile([P, J], F32, name="message")
+                for h in range(2):
+                    half_unit(t, h, gate[:, h * HALF : (h + 1) * HALF], message[:, h * HALF : (h + 1) * HALF])
+                nc.vector.tensor_tensor(page[:].indirect(dst_list[:]), gate[:], message[:], MULT)
+            nc.sync.dma_start(out=out[t * P : (t + 1) * P, :], in_=page[:])

@@ -22,7 +22,11 @@ PASSES = K // 512
 HALF = J // 2
 TILES = N // P
 BLOCKS = HALF // P
-SPARE = 8
+ROWS = K // 32
+WB_AT = 2 * J
+WC_AT = WB_AT + N
+PLANE = WC_AT + N
+WIDE = N // 2
 
 
 def tile_list_rgg_relu_kernel(
@@ -40,71 +44,65 @@ def tile_list_rgg_relu_kernel(
         tab_s = keep.tile([P, T // 4], I32, name="tab_s", align_bytes=64)
         wb_w = keep.tile([P, PASSES, N // 2], I32, name="wb_w", align_bytes=64)
         wc_w = keep.tile([P, PASSES, N], I32, name="wc_w", align_bytes=64)
-        wb_s = keep.tile([P, PASSES * N // 4], I32, name="wb_s", align_bytes=64)
-        wc_s = keep.tile([P, PASSES * N // 4], I32, name="wc_s", align_bytes=64)
-        picked_s = keep.tile([P, 2 * J], U8, name="picked_s", align_bytes=64)
-        moved_s = keep.tile([P, 2 * J // 4], I32, name="moved_s", align_bytes=64)
-        wa_raw = [keep.tile([P, 4, N], F32, name=f"wa_raw{a}") for a in range(PASSES)]
-        wa_w = [keep.tile([P, N], U32, name=f"wa_w{a}", align_bytes=64) for a in range(PASSES)]
-        wa_s = [keep.tile([P, N], U8, name=f"wa_s{a}", align_bytes=64) for a in range(PASSES)]
+        picked_s = keep.tile([P, 2 * J], U8, name="picked_s", tag="picked", align_bytes=64)
+        rows_s = keep.tile([P, PLANE // 4], I32, name="rows_s", align_bytes=64)
+        second_s = keep.tile([P, PLANE // 4], I32, name="second_s", align_bytes=64)
+        planes = (rows_s, second_s)
+        wa_raw = {(0, a): keep.tile([P, 4, WIDE], F32, name=f"wa_raw{a}", tag=f"early{a}") for a in range(PASSES)}
+        wa_w = {(g, a): keep.tile([P, WIDE], U32, name=f"wa_w{g}{a}", align_bytes=64) for g in range(2) for a in range(PASSES)}
+        wa_s = {(g, a): keep.tile([P, WIDE], U8, name=f"wa_s{g}{a}", align_bytes=64) for g in range(2) for a in range(PASSES)}
         pages = [keep.tile([P, T], F32, name="page0")]
         ident = keep.tile([P, P], F32, name="ident")
         wgo_rows = keep.tile([P, P], F32, name="wgo_rows")
-        wgo_cols = keep.tile([P, J // P], F32, name="wgo_cols")
         warm = keep.tile([P, 1], F32, name="warm")
 
-        nc.vector.memset(tab_s[:], 0)
-        nc.vector.memset(wc_s[:], 0)
-        nc.vector.memset(wb_s[:], 0)
-        nc.vector.memset(moved_s[:], 0)
+        nc.gpsimd.memset(tab_s[32:64, :], 0)
+        nc.gpsimd.memset(tab_s[64:128, :], 0)
         nc.vector.memset(pages[0][:], 0.0)
+        make_identity(nc, ident[:])
         nc.gpsimd.memset(wgo_rows[:], 0.0)
         nc.gpsimd.dma_start(out=wgo_rows[0 : J // P, :], in_=wgo[0:1, :].rearrange("o (c p) -> (o c) p", p=P))
-        make_identity(nc, ident[:])
+        nc.gpsimd.memset(rows_s[32:64, WB_AT // 4 :], 0)
+        nc.gpsimd.memset(rows_s[64:128, WB_AT // 4 :], 0)
+        nc.gpsimd.memset(second_s[:], 0)
         nc.scalar.activation(warm[:], ident[:, 0:1], ACT.Sigmoid)
 
-        def load_wa(a):
-            nc.sync.dma_start(out=wa_raw[a][:], in_=wa[512 * a : 512 * (a + 1), :].rearrange("(p i) n -> p i n", i=4))
+        def load_wa(g, a):
+            rows = wa[512 * a : 512 * (a + 1), g * WIDE : (g + 1) * WIDE]
+            nc.sync.dma_start(out=wa_raw[g, a][:], in_=rows.rearrange("(p i) n -> p i n", i=4))
 
-        def load_weight_scales(plane, scales, q):
-            nc.scalar.dma_start(
-                out=plane[32 * q : 32 * q + 4, :].rearrange("r (a n) -> r a n", a=PASSES),
-                in_=scales[:, 4 * q : 4 * q + 4, :].rearrange("a r n -> r a n").bitcast(I32),
-            )
+        def scale_rows(scales):
+            return scales.rearrange("a q n -> (a q) n").bitcast(I32)
 
         nc.sync.dma_start(src_list[:], offs)
-        for q in range(4):
-            nc.sync.dma_start(out=tab_s[32 * q : 32 * q + 4, :], in_=tab_scales[0, 4 * q : 4 * q + 4, :].bitcast(I32))
-        nc.sync.dma_start(out=tab_s[SPARE : SPARE + 16, :], in_=tab_scales[1].bitcast(I32))
+        nc.sync.dma_start(out=tab_s[0:ROWS, :], in_=scale_rows(tab_scales))
         nc.sync.dma_start(dst_list[:], offs2)
         nc.sync.dma_start(out=tab_w[:], in_=tab_words[0].rearrange("p t b -> p (t b)").bitcast(I32))
-        load_wa(0)
-        for q in range(4):
-            load_weight_scales(wc_s, wc_scales, q)
-        for q in range(2):
-            load_weight_scales(wb_s, wb_scales, q)
-        load_wa(1)
+        nc.sync.dma_start(out=rows_s[0:ROWS, WB_AT // 4 : WC_AT // 4], in_=scale_rows(wb_scales))
+        nc.sync.dma_start(out=rows_s[0:ROWS, WC_AT // 4 : PLANE // 4], in_=scale_rows(wc_scales))
+        load_wa(0, 0)
+        load_wa(0, 1)
         nc.sync.dma_start(out=wc_w[:], in_=wc_words.rearrange("a p n i -> p a (n i)").bitcast(I32))
-        for q in range(2, 4):
-            load_weight_scales(wb_s, wb_scales, q)
+        nc.sync.dma_start(out=wb_w[:], in_=wb_words.rearrange("a p n -> p a n").bitcast(I32))
 
         lists = (src_list, dst_list)
         for e in range(2):
             nc.vector.tensor_copy(picked_s[:, e * J : (e + 1) * J], tab_s[:].bitcast(U8).indirect(lists[e][:]))
-        for q in range(4):
-            nc.sync.dma_start(
-                out=moved_s[32 * q : 32 * q + 4, :],
-                in_=picked_s[SPARE + 4 * q : SPARE + 4 * q + 4, :].bitcast(I32),
-            )
-        nc.sync.dma_start(out=wb_w[:], in_=wb_words.rearrange("a p n -> p a n").bitcast(I32))
+        nc.vector.tensor_copy(rows_s[:, 0 : WB_AT // 4], picked_s[:].bitcast(I32))
+        for a in range(PASSES):
+            for q in range(1 - a, 4):
+                nc.sync.dma_start(
+                    out=planes[a][32 * q : 32 * q + 4, :],
+                    in_=rows_s[16 * a + 4 * q : 16 * a + 4 * q + 4, :],
+                )
+        late = keep.tile([P, PASSES * 4, WIDE], F32, name="wa_late", tag="picked", align_bytes=64)
+        for a in range(PASSES):
+            wa_raw[1, a] = late[:, 4 * a : 4 * a + 4, :]
+            load_wa(1, a)
 
-        wgo_bank = psum.tile([P, HALF], F32, name="wgo_bank", tag="turned", bufs=3)
-        nc.tensor.transpose(wgo_bank[:, 0:P], wgo_rows[:], ident[:])
-        nc.scalar.copy(wgo_cols[:], wgo_bank[:, 0 : J // P])
 
-        def picked_scales(e, a, cols):
-            plane = picked_s[:] if a == 0 else moved_s[:].bitcast(U8)
-            return plane[:, e * J + cols.start : e * J + cols.stop]
+        def scales_of(a, first, width):
+            return planes[a][:].bitcast(U8)[:, first : first + width]
 
         parted = {}
 
@@ -115,67 +113,74 @@ def tile_list_rgg_relu_kernel(
             parted[e, h] = keep.tile([P, PASSES, HALF], U16, name=f"parted{e}{h}", align_bytes=64)
             nc.vector.tensor_copy(parted[e, h][:], both[:].bitcast(U16).rearrange("p (j d) -> p d j", d=PASSES))
 
-        def quantise_wa(a):
-            rounded = keep.tile([P, N, 4], BF16, name=f"rounded{a}", tag=f"stage{a}", align_bytes=64)
+        def quantise_wa(g, a):
+            rounded = keep.tile([P, WIDE, 4], BF16, name=f"rounded{g}{a}", tag=f"stage{g}{a}", align_bytes=64)
             nc.scalar.copy(
                 rounded[:].rearrange("p (c u) i -> p c i u", u=4),
-                wa_raw[a][:].rearrange("p i (c u) -> p c i u", u=4),
+                wa_raw[g, a][:].rearrange("p i (c u) -> p c i u", u=4),
             )
             nc.vector.quantize_mx(
-                out=wa_w[a][:].bitcast(FP8X4), scales=wa_s[a][:], in_=rounded[:].rearrange("p n i -> p (n i)")
+                out=wa_w[g, a][:].bitcast(FP8X4), scales=wa_s[g, a][:], in_=rounded[:].rearrange("p n i -> p (n i)")
             )
 
         pick_words(0, 0, "first0")
         pick_words(1, 0, "first1")
-        quantise_wa(0)
-        pick_words(0, 1, "stage0")
-        quantise_wa(1)
-        pick_words(1, 1, "stage1")
-        pages.append(keep.tile([P, T], F32, name="page1", tag="stage1", align_bytes=64))
+        quantise_wa(0, 0)
+        quantise_wa(0, 1)
+        pick_words(0, 1, "stage01")
+        pick_words(1, 1, "stage01")
+        pages.append(keep.tile([P, T], F32, name="page1", tag="stage01", align_bytes=64))
         nc.gpsimd.memset(pages[1][:], 0.0)
+
+        wgo_bank = psum.tile([P, HALF], F32, name="wgo_bank", tag="turned", bufs=3)
+        nc.tensor.transpose(wgo_bank[:, 0:P], wgo_rows[:], ident[:])
+        wgo_cols = keep.tile([P, J // P], F32, name="wgo_cols", tag="early1")
+        nc.scalar.copy(wgo_cols[:], wgo_bank[:, 0 : J // P])
 
         def half_unit(t, h, gate, message):
             n_cols = slice(t * P, (t + 1) * P)
-            j_cols = slice(h * HALF, (h + 1) * HALF)
-            ms_bank = psum.tile([P, HALF], F32, name="ms_bank", tag="ms", bufs=2)
-            for b in range(BLOCKS):
-                for a in range(PASSES):
+            ms_bank = psum.tile([P, HALF], F32, name="ms_bank", tag="ms", bufs=1)
+            for a in range(PASSES):
+                for b in range(BLOCKS):
                     nc.tensor.matmul_mx(
                         out=ms_bank[:, b * P : (b + 1) * P],
                         lhsT=parted[0, h][:, a, b * P : (b + 1) * P].bitcast(FP4X4),
-                        lhsT_scale=picked_scales(0, a, slice(h * HALF + b * P, h * HALF + (b + 1) * P)),
+                        lhsT_scale=scales_of(a, h * HALF + b * P, P),
                         rhs=wc_w[:, a, n_cols].bitcast(FP8X4),
-                        rhs_scale=wc_s[:].bitcast(U8)[:, a * N + t * P : a * N + (t + 1) * P],
-                        start=(a == 0),
-                        stop=(a == PASSES - 1),
+                        rhs_scale=scales_of(a, WC_AT + t * P, P),
+                        start=(a == 0 and b == 0),
+                        stop=(a == PASSES - 1 and b == BLOCKS - 1),
                     )
             positive = ring.tile([P, HALF], F32, name="positive")
             nc.scalar.activation(positive[:], ms_bank[:], ACT.Relu)
-            weighted = ring.tile([P, HALF], F32, name="weighted")
+            if t == 0:
+                weighted = keep.tile([P, HALF], F32, name=f"weighted{h}", tag=f"stage1{h}", align_bytes=64)
+            else:
+                weighted = ring.tile([P, HALF], F32, name="weighted")
             for b in range(BLOCKS):
                 c = h * BLOCKS + b
                 nc.scalar.activation(
                     weighted[:, b * P : (b + 1) * P], positive[:, b * P : (b + 1) * P], ACT.Copy,
                     scale=wgo_cols[:, c : c + 1],
                 )
-            za_bank = psum.tile([P, HALF], F32, name="za_bank", tag="za", bufs=3)
+            za_bank = psum.tile([P, HALF], F32, name="za_bank", tag="za", bufs=1)
+            g, own = divmod(t * P, WIDE)
             for a in range(PASSES):
                 nc.tensor.matmul_mx(
                     out=za_bank[:],
-                    lhsT=wb_w[:, a, t * P // 2 : (t + 1) * P // 2].bitcast(FP4X4),
-                    lhsT_scale=wb_s[:].bitcast(U8)[:, a * N + t * P : a * N + (t + 1) * P],
-                    rhs=parted[0, h][:, a, :].bitcast(FP4X4),
-                    rhs_scale=picked_scales(0, a, j_cols),
+                    lhsT=wa_w[g, a][:, own : own + P].bitcast(FP8X4),
+                    lhsT_scale=wa_s[g, a][:, own : own + P],
+                    rhs=parted[1, h][:, a, :].bitcast(FP4X4),
+                    rhs_scale=scales_of(a, J + h * HALF, HALF),
                     start=(a == 0),
                     stop=False,
                 )
-            for a in range(PASSES):
                 nc.tensor.matmul_mx(
                     out=za_bank[:],
-                    lhsT=wa_w[a][:, n_cols].bitcast(FP8X4),
-                    lhsT_scale=wa_s[a][:, n_cols],
-                    rhs=parted[1, h][:, a, :].bitcast(FP4X4),
-                    rhs_scale=picked_scales(1, a, j_cols),
+                    lhsT=wb_w[:, a, t * P // 2 : (t + 1) * P // 2].bitcast(FP4X4),
+                    lhsT_scale=scales_of(a, WB_AT + t * P, P),
+                    rhs=parted[0, h][:, a, :].bitcast(FP4X4),
+                    rhs_scale=scales_of(a, h * HALF, HALF),
                     start=False,
                     stop=(a == PASSES - 1),
                 )
@@ -187,17 +192,12 @@ def tile_list_rgg_relu_kernel(
 
         for t in range(TILES):
             page = pages[t % 2]
-            if t < 2:
-                for h in range(2):
-                    gate = ring.tile([P, HALF], F32, name="gate_half", bufs=3)
-                    message = ring.tile([P, HALF], F32, name="message_half", bufs=3)
-                    half_unit(t, h, gate[:], message[:])
-                    cols = slice(h * HALF // 16, (h + 1) * HALF // 16)
-                    nc.vector.tensor_tensor(page[:].indirect(dst_list[:, cols]), gate[:], message[:], MULT)
-            else:
-                gate = ring.tile([P, J], F32, name="gate")
-                message = ring.tile([P, J], F32, name="message")
-                for h in range(2):
-                    half_unit(t, h, gate[:, h * HALF : (h + 1) * HALF], message[:, h * HALF : (h + 1) * HALF])
-                nc.vector.tensor_tensor(page[:].indirect(dst_list[:]), gate[:], message[:], MULT)
+            for h in range(2):
+                gate = ring.tile([P, HALF], F32, name="gate", bufs=3)
+                message = ring.tile([P, HALF], F32, name="message", bufs=3)
+                half_unit(t, h, gate[:], message[:])
+                cols = slice(h * HALF // 16, (h + 1) * HALF // 16)
+                nc.vector.tensor_tensor(page[:].indirect(dst_list[:, cols]), gate[:], message[:], MULT)
+                if t == 0:
+                    quantise_wa(1, h)
             nc.sync.dma_start(out=out[t * P : (t + 1) * P, :], in_=page[:])

@@ -20,10 +20,9 @@ MULT = mybir.AluOpType.mult
 P = 128
 PASSES = K // 512
 HALF = J // 2
-TILES = N // P
 BLOCKS = HALF // P
 ROWS = K // 32
-WB_AT = 2 * J
+WB_AT = 2 * HALF
 WC_AT = WB_AT + N
 PLANE = WC_AT + N
 WIDE = N // 2
@@ -40,31 +39,34 @@ def tile_list_rgg_relu_kernel(
 
         src_list = keep.tile([P, J // 16], U16, name="src_list")
         dst_list = keep.tile([P, J // 16], U16, name="dst_list")
+        lists = (src_list, dst_list)
         tab_w = keep.tile([P, T], I32, name="tab_w", align_bytes=64)
         tab_s = keep.tile([P, T // 4], I32, name="tab_s", align_bytes=64)
         wb_w = keep.tile([P, PASSES, N // 2], I32, name="wb_w", align_bytes=64)
         wc_w = keep.tile([P, PASSES, N], I32, name="wc_w", align_bytes=64)
-        picked_s = keep.tile([P, 2 * J], U8, name="picked_s", tag="picked", align_bytes=64)
-        rows_s = keep.tile([P, PLANE // 4], I32, name="rows_s", align_bytes=64)
-        second_s = keep.tile([P, PLANE // 4], I32, name="second_s", align_bytes=64)
-        planes = (rows_s, second_s)
-        wa_raw = {(0, a): keep.tile([P, 4, WIDE], F32, name=f"wa_raw{a}", tag=f"early{a}") for a in range(PASSES)}
-        wa_w = {(g, a): keep.tile([P, WIDE], U32, name=f"wa_w{g}{a}", align_bytes=64) for g in range(2) for a in range(PASSES)}
-        wa_s = {(g, a): keep.tile([P, WIDE], U8, name=f"wa_s{g}{a}", align_bytes=64) for g in range(2) for a in range(PASSES)}
+        planes = {
+            (h, a): keep.tile([P, (PLANE, WB_AT)[h] // 4], I32, name=f"plane{h}{a}", align_bytes=64)
+            for h in range(2)
+            for a in range(PASSES)
+        }
+        rows_s = planes[0, 0]
+        wa_raw = {(0, a): keep.tile([P, 4, WIDE], F32, name=f"wa_raw{a}", tag=f"early{a}", align_bytes=64) for a in range(PASSES)}
+        wa_w = [keep.tile([P, PASSES * WIDE], U32, name=f"wa_w{g}", align_bytes=64) for g in range(2)]
+        wa_s = [keep.tile([P, PASSES * WIDE], U8, name=f"wa_s{g}", align_bytes=64) for g in range(2)]
         pages = [keep.tile([P, T], F32, name="page0")]
         ident = keep.tile([P, P], F32, name="ident")
         wgo_rows = keep.tile([P, P], F32, name="wgo_rows")
         warm = keep.tile([P, 1], F32, name="warm")
 
-        nc.gpsimd.memset(tab_s[32:64, :], 0)
-        nc.gpsimd.memset(tab_s[64:128, :], 0)
+        nc.vector.memset(tab_s[32:64, :], 0)
+        nc.vector.memset(tab_s[64:128, :], 0)
+        nc.vector.memset(rows_s[32:64, WB_AT // 4 :], 0)
+        nc.vector.memset(rows_s[64:128, WB_AT // 4 :], 0)
+        for key in ((0, 1), (1, 0), (1, 1)):
+            nc.vector.memset(planes[key][:], 0)
         nc.vector.memset(pages[0][:], 0.0)
-        make_identity(nc, ident[:])
         nc.gpsimd.memset(wgo_rows[:], 0.0)
-        nc.gpsimd.dma_start(out=wgo_rows[0 : J // P, :], in_=wgo[0:1, :].rearrange("o (c p) -> (o c) p", p=P))
-        nc.gpsimd.memset(rows_s[32:64, WB_AT // 4 :], 0)
-        nc.gpsimd.memset(rows_s[64:128, WB_AT // 4 :], 0)
-        nc.gpsimd.memset(second_s[:], 0)
+        make_identity(nc, ident[:])
         nc.scalar.activation(warm[:], ident[:, 0:1], ACT.Sigmoid)
 
         def load_wa(g, a):
@@ -84,120 +86,141 @@ def tile_list_rgg_relu_kernel(
         load_wa(0, 1)
         nc.sync.dma_start(out=wc_w[:], in_=wc_words.rearrange("a p n i -> p a (n i)").bitcast(I32))
         nc.sync.dma_start(out=wb_w[:], in_=wb_words.rearrange("a p n -> p a n").bitcast(I32))
+        nc.sync.dma_start(out=wgo_rows[0 : J // P, :], in_=wgo[0:1, :].rearrange("o (c p) -> (o c) p", p=P))
 
-        lists = (src_list, dst_list)
-        for e in range(2):
-            nc.vector.tensor_copy(picked_s[:, e * J : (e + 1) * J], tab_s[:].bitcast(U8).indirect(lists[e][:]))
-        nc.vector.tensor_copy(rows_s[:, 0 : WB_AT // 4], picked_s[:].bitcast(I32))
-        for a in range(PASSES):
-            for q in range(1 - a, 4):
-                nc.sync.dma_start(
-                    out=planes[a][32 * q : 32 * q + 4, :],
-                    in_=rows_s[16 * a + 4 * q : 16 * a + 4 * q + 4, :],
+        def half_list(e, h):
+            return lists[e][:, h * HALF // 16 : (h + 1) * HALF // 16]
+
+        def pick_scales(h, tag):
+            picked = keep.tile([P, 2 * HALF], U8, name=f"picked{h}", tag=tag, align_bytes=64)
+            for e in range(2):
+                nc.vector.tensor_copy(
+                    picked[:, e * HALF : (e + 1) * HALF], tab_s[:].bitcast(U8).indirect(half_list(e, h))
                 )
-        late = keep.tile([P, PASSES * 4, WIDE], F32, name="wa_late", tag="picked", align_bytes=64)
+            return picked[:].bitcast(I32)
+
+        def spread_rows(h, rows, first):
+            for r in range(first, ROWS // 4):
+                a, q = divmod(r, 4)
+                nc.sync.dma_start(out=planes[h, a][32 * q : 32 * q + 4, :], in_=rows[4 * r : 4 * r + 4, :])
+
+        nc.vector.tensor_copy(rows_s[:, 0 : WB_AT // 4], pick_scales(0, "picked0"))
+        spread_rows(0, rows_s[:], 1)
+        late = keep.tile([P, PASSES * 4, WIDE], F32, name="wa_late", tag="picked0", align_bytes=64)
         for a in range(PASSES):
             wa_raw[1, a] = late[:, 4 * a : 4 * a + 4, :]
             load_wa(1, a)
 
-
-        def scales_of(a, first, width):
-            return planes[a][:].bitcast(U8)[:, first : first + width]
+        def scales_of(h, a, first, width):
+            return planes[h, a][:].bitcast(U8)[:, first : first + width]
 
         parted = {}
 
-        def pick_words(e, h, tag):
-            both = keep.tile([P, HALF], U32, name=f"both{e}{h}", tag=tag, align_bytes=64)
-            cols = slice(h * HALF // 16, (h + 1) * HALF // 16)
-            nc.vector.tensor_copy(both[:], tab_w[:].bitcast(U32).indirect(lists[e][:, cols]))
-            parted[e, h] = keep.tile([P, PASSES, HALF], U16, name=f"parted{e}{h}", align_bytes=64)
-            nc.vector.tensor_copy(parted[e, h][:], both[:].bitcast(U16).rearrange("p (j d) -> p d j", d=PASSES))
+        def pick_words(h, tag):
+            both = keep.tile([P, 2, HALF], U32, name=f"both{h}", tag=tag, align_bytes=64)
+            for e in range(2):
+                nc.vector.tensor_copy(both[:, e, :], tab_w[:].bitcast(U32).indirect(half_list(e, h)))
+            for e in range(2):
+                parted[e, h] = keep.tile([P, PASSES, HALF], U16, name=f"parted{e}{h}", align_bytes=64)
+                nc.vector.tensor_copy(
+                    parted[e, h][:], both[:, e, :].bitcast(U16).rearrange("p (j d) -> p d j", d=PASSES)
+                )
 
-        def quantise_wa(g, a):
-            rounded = keep.tile([P, WIDE, 4], BF16, name=f"rounded{g}{a}", tag=f"stage{g}{a}", align_bytes=64)
+        def round_wa(g, a, rounded):
             nc.scalar.copy(
-                rounded[:].rearrange("p (c u) i -> p c i u", u=4),
+                rounded.rearrange("p (c u) i -> p c i u", u=4),
                 wa_raw[g, a][:].rearrange("p i (c u) -> p c i u", u=4),
             )
+
+        def quantise_wa(g, first, rounded):
+            cols = slice(first, first + rounded.shape[1])
             nc.vector.quantize_mx(
-                out=wa_w[g, a][:].bitcast(FP8X4), scales=wa_s[g, a][:], in_=rounded[:].rearrange("p n i -> p (n i)")
+                out=wa_w[g][:, cols].bitcast(FP8X4), scales=wa_s[g][:, cols], in_=rounded.rearrange("p n i -> p (n i)")
             )
 
-        pick_words(0, 0, "first0")
-        pick_words(1, 0, "first1")
-        quantise_wa(0, 0)
-        quantise_wa(0, 1)
-        pick_words(0, 1, "stage01")
-        pick_words(1, 1, "stage01")
-        pages.append(keep.tile([P, T], F32, name="page1", tag="stage01", align_bytes=64))
-        nc.gpsimd.memset(pages[1][:], 0.0)
+        def clear_page(tag):
+            pages.append(keep.tile([P, T], F32, name=f"page{len(pages)}", tag=tag, align_bytes=64))
+            nc.gpsimd.memset(pages[-1][:], 0.0)
 
-        wgo_bank = psum.tile([P, HALF], F32, name="wgo_bank", tag="turned", bufs=3)
+        pick_words(0, "first")
+        early = keep.tile([P, PASSES * WIDE, 4], BF16, name="early", tag="rounded", align_bytes=64)
+        for a in range(PASSES):
+            round_wa(0, a, early[:, a * WIDE : (a + 1) * WIDE, :])
+        quantise_wa(0, 0, early[:])
+        spread_rows(1, pick_scales(1, "rounded"), 0)
+        pick_words(1, "early1")
+        clear_page("early1")
+
+        wgo_bank = psum.tile([P, HALF], F32, name="wgo_bank", tag="bank2")
         nc.tensor.transpose(wgo_bank[:, 0:P], wgo_rows[:], ident[:])
-        wgo_cols = keep.tile([P, J // P], F32, name="wgo_cols", tag="early1")
+        wgo_cols = keep.tile([P, J // P], F32, name="wgo_cols", tag="early0", align_bytes=64)
         nc.scalar.copy(wgo_cols[:], wgo_bank[:, 0 : J // P])
 
-        def half_unit(t, h, gate, message):
+        def half_unit(u, t, h, weighted):
             n_cols = slice(t * P, (t + 1) * P)
-            ms_bank = psum.tile([P, HALF], F32, name="ms_bank", tag="ms", bufs=1)
+            ms_bank = psum.tile([P, HALF], F32, name="ms_bank", tag=f"bank{u % 3}")
             for a in range(PASSES):
                 for b in range(BLOCKS):
                     nc.tensor.matmul_mx(
                         out=ms_bank[:, b * P : (b + 1) * P],
                         lhsT=parted[0, h][:, a, b * P : (b + 1) * P].bitcast(FP4X4),
-                        lhsT_scale=scales_of(a, h * HALF + b * P, P),
+                        lhsT_scale=scales_of(h, a, b * P, P),
                         rhs=wc_w[:, a, n_cols].bitcast(FP8X4),
-                        rhs_scale=scales_of(a, WC_AT + t * P, P),
+                        rhs_scale=scales_of(0, a, WC_AT + t * P, P),
                         start=(a == 0 and b == 0),
                         stop=(a == PASSES - 1 and b == BLOCKS - 1),
                     )
             positive = ring.tile([P, HALF], F32, name="positive")
             nc.scalar.activation(positive[:], ms_bank[:], ACT.Relu)
-            if t == 0:
-                weighted = keep.tile([P, HALF], F32, name=f"weighted{h}", tag=f"stage1{h}", align_bytes=64)
-            else:
-                weighted = ring.tile([P, HALF], F32, name="weighted")
             for b in range(BLOCKS):
                 c = h * BLOCKS + b
                 nc.scalar.activation(
                     weighted[:, b * P : (b + 1) * P], positive[:, b * P : (b + 1) * P], ACT.Copy,
                     scale=wgo_cols[:, c : c + 1],
                 )
-            za_bank = psum.tile([P, HALF], F32, name="za_bank", tag="za", bufs=1)
+            za_bank = psum.tile([P, HALF], F32, name="za_bank", tag=f"bank{(u + 1) % 3}")
             g, own = divmod(t * P, WIDE)
             for a in range(PASSES):
                 nc.tensor.matmul_mx(
                     out=za_bank[:],
-                    lhsT=wa_w[g, a][:, own : own + P].bitcast(FP8X4),
-                    lhsT_scale=wa_s[g, a][:, own : own + P],
+                    lhsT=wa_w[g][:, a * WIDE + own : a * WIDE + own + P].bitcast(FP8X4),
+                    lhsT_scale=wa_s[g][:, a * WIDE + own : a * WIDE + own + P],
                     rhs=parted[1, h][:, a, :].bitcast(FP4X4),
-                    rhs_scale=scales_of(a, J + h * HALF, HALF),
+                    rhs_scale=scales_of(h, a, HALF, HALF),
                     start=(a == 0),
                     stop=False,
                 )
                 nc.tensor.matmul_mx(
                     out=za_bank[:],
                     lhsT=wb_w[:, a, t * P // 2 : (t + 1) * P // 2].bitcast(FP4X4),
-                    lhsT_scale=scales_of(a, WB_AT + t * P, P),
+                    lhsT_scale=scales_of(0, a, WB_AT + t * P, P),
                     rhs=parted[0, h][:, a, :].bitcast(FP4X4),
-                    rhs_scale=scales_of(a, h * HALF, HALF),
+                    rhs_scale=scales_of(h, a, 0, HALF),
                     start=False,
                     stop=(a == PASSES - 1),
                 )
-            turned = psum.tile([P, HALF], F32, name="turned", tag="turned", bufs=3)
+            turned = psum.tile([P, HALF], F32, name="turned", tag=f"bank{(u + 2) % 3}")
             for b in range(BLOCKS):
                 nc.tensor.transpose(turned[:, b * P : (b + 1) * P], weighted[:, b * P : (b + 1) * P], ident[:])
-            nc.scalar.activation(gate, za_bank[:], ACT.Sigmoid)
-            nc.scalar.copy(message, turned[:])
+            gate = ring.tile([P, HALF], F32, name="gate", bufs=3)
+            message = ring.tile([P, HALF], F32, name="message", bufs=3)
+            nc.scalar.activation(gate[:], za_bank[:], ACT.Sigmoid)
+            nc.scalar.copy(message[:], turned[:])
+            page = pages[t % 3]
+            nc.vector.tensor_tensor(page[:].indirect(half_list(1, h)), gate[:], message[:], MULT)
+            if h == 1:
+                nc.sync.dma_start(out=out[n_cols, :], in_=page[:])
 
-        for t in range(TILES):
-            page = pages[t % 2]
-            for h in range(2):
-                gate = ring.tile([P, HALF], F32, name="gate", bufs=3)
-                message = ring.tile([P, HALF], F32, name="message", bufs=3)
-                half_unit(t, h, gate[:], message[:])
-                cols = slice(h * HALF // 16, (h + 1) * HALF // 16)
-                nc.vector.tensor_tensor(page[:].indirect(dst_list[:, cols]), gate[:], message[:], MULT)
-                if t == 0:
-                    quantise_wa(1, h)
-            nc.sync.dma_start(out=out[t * P : (t + 1) * P, :], in_=page[:])
+        units = [(2 * g + i, h) for g in range(2) for h in range(2) for i in range(2)]
+        for u, (t, h) in enumerate(units):
+            if u in (1, 2):
+                weighted = keep.tile([P, HALF], F32, name=f"weighted{u}", tag=f"stage1{u - 1}", align_bytes=64)
+            else:
+                weighted = ring.tile([P, HALF], F32, name="weighted")
+            half_unit(u, t, h, weighted)
+            if u in (1, 2):
+                rounded = keep.tile([P, WIDE, 4], BF16, name=f"rounded{u}", tag=f"stage1{u - 1}", align_bytes=64)
+                round_wa(1, u - 1, rounded[:])
+                quantise_wa(1, (u - 1) * WIDE, rounded[:])
+            if u == 1:
+                clear_page("stage10")

@@ -151,15 +151,15 @@ def tile_list_rgg_relu_kernel(
         pick_words(1, "early1")
         clear_page("early1")
 
-        wgo_bank = psum.tile([P, HALF], F32, name="wgo_bank", tag="bank2")
+        wgo_bank = psum.tile([P, HALF], F32, name="wgo_bank", tag="za1")
         nc.tensor.transpose(wgo_bank[:, 0:P], wgo_rows[:], ident[:])
         wgo_cols = keep.tile([P, J // P], F32, name="wgo_cols", tag="early0", align_bytes=64)
         nc.scalar.copy(wgo_cols[:], wgo_bank[:, 0 : J // P])
 
         def half_unit(u, t, h, weighted):
             n_cols = slice(t * P, (t + 1) * P)
-            ms_bank = psum.tile([P, HALF], F32, name="ms_bank", tag=f"bank{u % 3}")
-            for a in range(PASSES):
+            ms_bank = psum.tile([P, HALF], F32, name="ms_bank", tag=f"ms{u % 2}")
+            for a in reversed(range(PASSES)):
                 for b in range(BLOCKS):
                     nc.tensor.matmul_mx(
                         out=ms_bank[:, b * P : (b + 1) * P],
@@ -167,10 +167,13 @@ def tile_list_rgg_relu_kernel(
                         lhsT_scale=scales_of(h, a, b * P, P),
                         rhs=wc_w[:, a, n_cols].bitcast(FP8X4),
                         rhs_scale=scales_of(0, a, WC_AT + t * P, P),
-                        start=(a == 0 and b == 0),
-                        stop=(a == PASSES - 1 and b == BLOCKS - 1),
+                        start=(a == PASSES - 1 and b == 0),
+                        stop=(a == 0 and b == BLOCKS - 1),
                     )
-            positive = ring.tile([P, HALF], F32, name="positive")
+            if u == 2:
+                positive = keep.tile([P, HALF], F32, name="positive2", tag="picked0", align_bytes=64)
+            else:
+                positive = ring.tile([P, HALF], F32, name="positive")
             nc.scalar.activation(positive[:], ms_bank[:], ACT.Relu)
             for b in range(BLOCKS):
                 c = h * BLOCKS + b
@@ -178,16 +181,16 @@ def tile_list_rgg_relu_kernel(
                     weighted[:, b * P : (b + 1) * P], positive[:, b * P : (b + 1) * P], ACT.Copy,
                     scale=wgo_cols[:, c : c + 1],
                 )
-            za_bank = psum.tile([P, HALF], F32, name="za_bank", tag=f"bank{(u + 1) % 3}")
+            za_bank = psum.tile([P, HALF], F32, name="za_bank", tag=f"za{u % 2}")
             g, own = divmod(t * P, WIDE)
-            for a in range(PASSES):
+            for a in reversed(range(PASSES)):
                 nc.tensor.matmul_mx(
                     out=za_bank[:],
                     lhsT=wa_w[g][:, a * WIDE + own : a * WIDE + own + P].bitcast(FP8X4),
                     lhsT_scale=wa_s[g][:, a * WIDE + own : a * WIDE + own + P],
                     rhs=parted[1, h][:, a, :].bitcast(FP4X4),
                     rhs_scale=scales_of(h, a, HALF, HALF),
-                    start=(a == 0),
+                    start=(a == PASSES - 1),
                     stop=False,
                 )
                 nc.tensor.matmul_mx(
@@ -197,13 +200,13 @@ def tile_list_rgg_relu_kernel(
                     rhs=parted[0, h][:, a, :].bitcast(FP4X4),
                     rhs_scale=scales_of(h, a, 0, HALF),
                     start=False,
-                    stop=(a == PASSES - 1),
+                    stop=(a == 0),
                 )
-            turned = psum.tile([P, HALF], F32, name="turned", tag=f"bank{(u + 2) % 3}")
+            turned = psum.tile([P, HALF], F32, name="turned", tag=f"ms{u % 2}")
             for b in range(BLOCKS):
                 nc.tensor.transpose(turned[:, b * P : (b + 1) * P], weighted[:, b * P : (b + 1) * P], ident[:])
-            gate = ring.tile([P, HALF], F32, name="gate", bufs=3)
-            message = ring.tile([P, HALF], F32, name="message", bufs=3)
+            gate = ring.tile([P, HALF], F32, name="gate", bufs=8)
+            message = ring.tile([P, HALF], F32, name="message", bufs=8)
             nc.scalar.activation(gate[:], za_bank[:], ACT.Sigmoid)
             nc.scalar.copy(message[:], turned[:])
             page = pages[t % 3]
@@ -213,14 +216,14 @@ def tile_list_rgg_relu_kernel(
 
         units = [(2 * g + i, h) for g in range(2) for h in range(2) for i in range(2)]
         for u, (t, h) in enumerate(units):
-            if u in (1, 2):
-                weighted = keep.tile([P, HALF], F32, name=f"weighted{u}", tag=f"stage1{u - 1}", align_bytes=64)
+            if u == 1:
+                weighted = keep.tile([P, HALF], F32, name="weighted1", tag="stage1", align_bytes=64)
             else:
                 weighted = ring.tile([P, HALF], F32, name="weighted")
             half_unit(u, t, h, weighted)
-            if u in (1, 2):
-                rounded = keep.tile([P, WIDE, 4], BF16, name=f"rounded{u}", tag=f"stage1{u - 1}", align_bytes=64)
-                round_wa(1, u - 1, rounded[:])
-                quantise_wa(1, (u - 1) * WIDE, rounded[:])
             if u == 1:
-                clear_page("stage10")
+                rounded = keep.tile([P, PASSES * WIDE, 4], BF16, name="rounded1", tag="stage1", align_bytes=64)
+                for a in range(PASSES):
+                    round_wa(1, a, rounded[:, a * WIDE : (a + 1) * WIDE, :])
+                quantise_wa(1, 0, rounded[:])
+                clear_page("stage1")

@@ -35,6 +35,7 @@ def tile_list_rgg_relu_kernel(
     with ExitStack() as ctx:
         keep = ctx.enter_context(tc.tile_pool(name="keep", bufs=1))
         ring = ctx.enter_context(tc.tile_pool(name="ring", bufs=2))
+        shared = ctx.enter_context(tc.tile_pool(name="shared", bufs=1))
         psum = ctx.enter_context(tc.psum_pool(name="psum", bufs=1))
 
         src_list = keep.tile([P, J // 16], U16, name="src_list")
@@ -42,18 +43,16 @@ def tile_list_rgg_relu_kernel(
         lists = (src_list, dst_list)
         tab_w = keep.tile([P, T], I32, name="tab_w", align_bytes=64)
         tab_s = keep.tile([P, T // 4], I32, name="tab_s", align_bytes=64)
-        wb_w = keep.tile([P, PASSES, N // 2], I32, name="wb_w", align_bytes=64)
-        wc_w = keep.tile([P, PASSES, N], I32, name="wc_w", align_bytes=64)
         planes = {
             (h, a): keep.tile([P, (PLANE, WB_AT)[h] // 4], I32, name=f"plane{h}{a}", align_bytes=64)
             for h in range(2)
             for a in range(PASSES)
         }
         rows_s = planes[0, 0]
-        wa_raw = {(0, a): keep.tile([P, 4, WIDE], F32, name=f"wa_raw{a}", tag=f"early{a}", align_bytes=64) for a in range(PASSES)}
+        wa_raw = {(0, a): keep.tile([P, 4, WIDE], F32, name=f"wa_raw{a}", align_bytes=64) for a in range(PASSES)}
         wa_w = [keep.tile([P, PASSES * WIDE], U32, name=f"wa_w{g}", align_bytes=64) for g in range(2)]
         wa_s = [keep.tile([P, PASSES * WIDE], U8, name=f"wa_s{g}", align_bytes=64) for g in range(2)]
-        pages = [keep.tile([P, T], F32, name="page0")]
+        pages = []
         ident = keep.tile([P, P], F32, name="ident")
         wgo_rows = keep.tile([P, P], F32, name="wgo_rows")
         warm = keep.tile([P, 1], F32, name="warm")
@@ -64,7 +63,6 @@ def tile_list_rgg_relu_kernel(
         nc.vector.memset(rows_s[64:128, WB_AT // 4 :], 0)
         for key in ((0, 1), (1, 0), (1, 1)):
             nc.vector.memset(planes[key][:], 0)
-        nc.vector.memset(pages[0][:], 0.0)
         nc.gpsimd.memset(wgo_rows[:], 0.0)
         make_identity(nc, ident[:])
         nc.scalar.activation(warm[:], ident[:, 0:1], ACT.Sigmoid)
@@ -82,17 +80,14 @@ def tile_list_rgg_relu_kernel(
         nc.sync.dma_start(out=tab_w[:], in_=tab_words[0].rearrange("p t b -> p (t b)").bitcast(I32))
         nc.sync.dma_start(out=rows_s[0:ROWS, WB_AT // 4 : WC_AT // 4], in_=scale_rows(wb_scales))
         nc.sync.dma_start(out=rows_s[0:ROWS, WC_AT // 4 : PLANE // 4], in_=scale_rows(wc_scales))
+        nc.sync.dma_start(out=wgo_rows[0 : J // P, :], in_=wgo[0:1, :].rearrange("o (c p) -> (o c) p", p=P))
         load_wa(0, 0)
         load_wa(0, 1)
-        nc.sync.dma_start(out=wc_w[:], in_=wc_words.rearrange("a p n i -> p a (n i)").bitcast(I32))
-        nc.sync.dma_start(out=wb_w[:], in_=wb_words.rearrange("a p n -> p a n").bitcast(I32))
-        nc.sync.dma_start(out=wgo_rows[0 : J // P, :], in_=wgo[0:1, :].rearrange("o (c p) -> (o c) p", p=P))
 
         def half_list(e, h):
             return lists[e][:, h * HALF // 16 : (h + 1) * HALF // 16]
 
-        def pick_scales(h, tag):
-            picked = keep.tile([P, 2 * HALF], U8, name=f"picked{h}", tag=tag, align_bytes=64)
+        def pick_scales(h, picked):
             for e in range(2):
                 nc.vector.tensor_copy(
                     picked[:, e * HALF : (e + 1) * HALF], tab_s[:].bitcast(U8).indirect(half_list(e, h))
@@ -104,26 +99,29 @@ def tile_list_rgg_relu_kernel(
                 a, q = divmod(r, 4)
                 nc.sync.dma_start(out=planes[h, a][32 * q : 32 * q + 4, :], in_=rows[4 * r : 4 * r + 4, :])
 
-        nc.vector.tensor_copy(rows_s[:, 0 : WB_AT // 4], pick_scales(0, "picked0"))
+        picked0 = shared.tile([P, 2 * HALF], U8, name="picked0", align_bytes=64, offset=12 * N - 64)
+        nc.vector.tensor_copy(rows_s[:, 0 : WB_AT // 4], pick_scales(0, picked0))
         spread_rows(0, rows_s[:], 1)
-        late = keep.tile([P, PASSES * 4, WIDE], F32, name="wa_late", tag="picked0", align_bytes=64)
-        for a in range(PASSES):
-            wa_raw[1, a] = late[:, 4 * a : 4 * a + 4, :]
-            load_wa(1, a)
+        weights = shared.tile([P, 3 * N], I32, name="weights", align_bytes=64, offset=0)
+        wc_w = weights[:, 0 : 2 * N].rearrange("p (a n) -> p a n", a=PASSES)
+        wb_w = weights[:, 2 * N : 3 * N].rearrange("p (a n) -> p a n", a=PASSES)
+        nc.sync.dma_start(out=wc_w, in_=wc_words.rearrange("a p n i -> p a (n i)").bitcast(I32))
+        nc.sync.dma_start(out=wb_w, in_=wb_words.rearrange("a p n -> p a n").bitcast(I32))
+        pages.append(shared.tile([P, T], F32, name="page0", align_bytes=64, offset=12 * N + 2 * HALF - 128))
+        nc.gpsimd.memset(pages[0][:], 0.0)
 
         def scales_of(h, a, first, width):
             return planes[h, a][:].bitcast(U8)[:, first : first + width]
 
         parted = {}
 
-        def pick_words(h, tag):
-            both = keep.tile([P, 2, HALF], U32, name=f"both{h}", tag=tag, align_bytes=64)
+        def pick_words(h, both):
             for e in range(2):
-                nc.vector.tensor_copy(both[:, e, :], tab_w[:].bitcast(U32).indirect(half_list(e, h)))
+                nc.vector.tensor_copy(both[e], tab_w[:].bitcast(U32).indirect(half_list(e, h)))
             for e in range(2):
                 parted[e, h] = keep.tile([P, PASSES, HALF], U16, name=f"parted{e}{h}", align_bytes=64)
                 nc.vector.tensor_copy(
-                    parted[e, h][:], both[:, e, :].bitcast(U16).rearrange("p (j d) -> p d j", d=PASSES)
+                    parted[e, h][:], both[e].bitcast(U16).rearrange("p (j d) -> p d j", d=PASSES)
                 )
 
         def round_wa(g, a, rounded):
@@ -142,18 +140,28 @@ def tile_list_rgg_relu_kernel(
             pages.append(keep.tile([P, T], F32, name=f"page{len(pages)}", tag=tag, align_bytes=64))
             nc.gpsimd.memset(pages[-1][:], 0.0)
 
-        pick_words(0, "first")
-        early = keep.tile([P, PASSES * WIDE, 4], BF16, name="early", tag="rounded", align_bytes=64)
+        at = 12 * N + 2 * HALF + 4 * T
+        both_src = keep.tile([P, HALF], U32, name="both_src", align_bytes=64)
+        both_dst = keep.tile([P, HALF], U32, name="both_dst", tag="first1", align_bytes=64)
+        pick_words(0, [both_src[:], both_dst[:]])
+        late = keep.tile([P, PASSES * 4, WIDE], F32, name="wa_late", tag="first1", align_bytes=64)
+        for a in range(PASSES):
+            wa_raw[1, a] = late[:, 4 * a : 4 * a + 4, :]
+            load_wa(1, a)
+        early = shared.tile([P, PASSES * WIDE, 4], BF16, name="early", align_bytes=64, offset=at + 2 * HALF - 64)
         for a in range(PASSES):
             round_wa(0, a, early[:, a * WIDE : (a + 1) * WIDE, :])
         quantise_wa(0, 0, early[:])
-        spread_rows(1, pick_scales(1, "rounded"), 0)
-        pick_words(1, "early1")
-        clear_page("early1")
+        picked1 = shared.tile([P, 2 * HALF], U8, name="picked1", align_bytes=64, offset=at)
+        spread_rows(1, pick_scales(1, picked1), 0)
+        both1 = shared.tile([P, 2, HALF], U32, name="both1", align_bytes=64, offset=at + 2 * HALF)
+        pick_words(1, [both1[:, 0, :], both1[:, 1, :]])
+        pages.append(shared.tile([P, T], F32, name="page1", align_bytes=64, offset=at + 2 * HALF))
+        nc.gpsimd.memset(pages[1][:], 0.0)
 
         wgo_bank = psum.tile([P, HALF], F32, name="wgo_bank", tag="za1")
         nc.tensor.transpose(wgo_bank[:, 0:P], wgo_rows[:], ident[:])
-        wgo_cols = keep.tile([P, J // P], F32, name="wgo_cols", tag="early0", align_bytes=64)
+        wgo_cols = keep.tile([P, J // P], F32, name="wgo_cols")
         nc.scalar.copy(wgo_cols[:], wgo_bank[:, 0 : J // P])
 
         def half_unit(u, t, h, weighted):
@@ -171,7 +179,7 @@ def tile_list_rgg_relu_kernel(
                         stop=(a == 0 and b == BLOCKS - 1),
                     )
             if u == 2:
-                positive = keep.tile([P, HALF], F32, name="positive2", tag="picked0", align_bytes=64)
+                positive = keep.tile([P, HALF], F32, name="positive2", tag="first1", align_bytes=64)
             else:
                 positive = ring.tile([P, HALF], F32, name="positive")
             nc.scalar.activation(positive[:], ms_bank[:], ACT.Relu)
@@ -186,19 +194,19 @@ def tile_list_rgg_relu_kernel(
             for a in reversed(range(PASSES)):
                 nc.tensor.matmul_mx(
                     out=za_bank[:],
-                    lhsT=wa_w[g][:, a * WIDE + own : a * WIDE + own + P].bitcast(FP8X4),
-                    lhsT_scale=wa_s[g][:, a * WIDE + own : a * WIDE + own + P],
-                    rhs=parted[1, h][:, a, :].bitcast(FP4X4),
-                    rhs_scale=scales_of(h, a, HALF, HALF),
+                    lhsT=wb_w[:, a, t * P // 2 : (t + 1) * P // 2].bitcast(FP4X4),
+                    lhsT_scale=scales_of(0, a, WB_AT + t * P, P),
+                    rhs=parted[0, h][:, a, :].bitcast(FP4X4),
+                    rhs_scale=scales_of(h, a, 0, HALF),
                     start=(a == PASSES - 1),
                     stop=False,
                 )
                 nc.tensor.matmul_mx(
                     out=za_bank[:],
-                    lhsT=wb_w[:, a, t * P // 2 : (t + 1) * P // 2].bitcast(FP4X4),
-                    lhsT_scale=scales_of(0, a, WB_AT + t * P, P),
-                    rhs=parted[0, h][:, a, :].bitcast(FP4X4),
-                    rhs_scale=scales_of(h, a, 0, HALF),
+                    lhsT=wa_w[g][:, a * WIDE + own : a * WIDE + own + P].bitcast(FP8X4),
+                    lhsT_scale=wa_s[g][:, a * WIDE + own : a * WIDE + own + P],
+                    rhs=parted[1, h][:, a, :].bitcast(FP4X4),
+                    rhs_scale=scales_of(h, a, HALF, HALF),
                     start=False,
                     stop=(a == 0),
                 )

@@ -49,7 +49,8 @@ def tile_list_rgg_relu_kernel(
             for a in range(PASSES)
         }
         rows_s = planes[0, 0]
-        wa_raw = {(0, a): keep.tile([P, 4, WIDE], F32, name=f"wa_raw{a}", align_bytes=64) for a in range(PASSES)}
+        wa_raw = {(0, a): keep.tile([P, 4, WIDE], F32, name=f"wa_raw{a}", tag=f"early{a}", align_bytes=64) for a in range(PASSES)}
+        wc_w = [keep.tile([P, PASSES, WIDE], I32, name="wc_w0", align_bytes=64)]
         wa_w = [keep.tile([P, PASSES * WIDE], U32, name=f"wa_w{g}", align_bytes=64) for g in range(2)]
         wa_s = [keep.tile([P, PASSES * WIDE], U8, name=f"wa_s{g}", align_bytes=64) for g in range(2)]
         pages = []
@@ -71,6 +72,10 @@ def tile_list_rgg_relu_kernel(
             rows = wa[512 * a : 512 * (a + 1), g * WIDE : (g + 1) * WIDE]
             nc.sync.dma_start(out=wa_raw[g, a][:], in_=rows.rearrange("(p i) n -> p i n", i=4))
 
+        def load_wc(g):
+            cols = wc_words[:, :, g * WIDE : (g + 1) * WIDE, :]
+            nc.sync.dma_start(out=wc_w[g][:], in_=cols.rearrange("a p n i -> p a (n i)").bitcast(I32))
+
         def scale_rows(scales):
             return scales.rearrange("a q n -> (a q) n").bitcast(I32)
 
@@ -82,32 +87,28 @@ def tile_list_rgg_relu_kernel(
         nc.sync.dma_start(out=rows_s[0:ROWS, WC_AT // 4 : PLANE // 4], in_=scale_rows(wc_scales))
         nc.sync.dma_start(out=wgo_rows[0 : J // P, :], in_=wgo[0:1, :].rearrange("o (c p) -> (o c) p", p=P))
         load_wa(0, 0)
+        load_wc(0)
         load_wa(0, 1)
 
         def half_list(e, h):
             return lists[e][:, h * HALF // 16 : (h + 1) * HALF // 16]
 
-        def pick_scales(h, picked):
-            for e in range(2):
-                nc.vector.tensor_copy(
-                    picked[:, e * HALF : (e + 1) * HALF], tab_s[:].bitcast(U8).indirect(half_list(e, h))
-                )
-            return picked[:].bitcast(I32)
+        def pick_scales(e, h, picked):
+            nc.vector.tensor_copy(picked, tab_s[:].bitcast(U8).indirect(half_list(e, h)))
 
         def spread_rows(h, rows, first):
             for r in range(first, ROWS // 4):
                 a, q = divmod(r, 4)
                 nc.sync.dma_start(out=planes[h, a][32 * q : 32 * q + 4, :], in_=rows[4 * r : 4 * r + 4, :])
 
-        picked0 = shared.tile([P, 2 * HALF], U8, name="picked0", align_bytes=64, offset=12 * N - 64)
-        nc.vector.tensor_copy(rows_s[:, 0 : WB_AT // 4], pick_scales(0, picked0))
+        picked0 = shared.tile([P, 2 * HALF], U8, name="picked0", align_bytes=64, offset=4 * N - 64)
+        pick_scales(0, 0, picked0[:, 0:HALF])
+        pick_scales(1, 0, picked0[:, HALF : 2 * HALF])
+        nc.vector.tensor_copy(rows_s[:, 0 : WB_AT // 4], picked0[:].bitcast(I32))
         spread_rows(0, rows_s[:], 1)
-        weights = shared.tile([P, 3 * N], I32, name="weights", align_bytes=64, offset=0)
-        wc_w = weights[:, 0 : 2 * N].rearrange("p (a n) -> p a n", a=PASSES)
-        wb_w = weights[:, 2 * N : 3 * N].rearrange("p (a n) -> p a n", a=PASSES)
-        nc.sync.dma_start(out=wc_w, in_=wc_words.rearrange("a p n i -> p a (n i)").bitcast(I32))
-        nc.sync.dma_start(out=wb_w, in_=wb_words.rearrange("a p n -> p a n").bitcast(I32))
-        pages.append(shared.tile([P, T], F32, name="page0", align_bytes=64, offset=12 * N + 2 * HALF - 128))
+        wb_w = shared.tile([P, PASSES, N // 2], I32, name="wb_w", align_bytes=64, offset=0)
+        nc.sync.dma_start(out=wb_w[:], in_=wb_words.rearrange("a p n -> p a n").bitcast(I32))
+        pages.append(shared.tile([P, T], F32, name="page0", align_bytes=64, offset=4 * N))
         nc.gpsimd.memset(pages[0][:], 0.0)
 
         def scales_of(h, a, first, width):
@@ -115,14 +116,15 @@ def tile_list_rgg_relu_kernel(
 
         parted = {}
 
-        def pick_words(h, both):
-            for e in range(2):
-                nc.vector.tensor_copy(both[e], tab_w[:].bitcast(U32).indirect(half_list(e, h)))
-            for e in range(2):
+        def pick_words(e, h, both):
+            nc.vector.tensor_copy(both[:], tab_w[:].bitcast(U32).indirect(half_list(e, h)))
+
+        def part_words(e, h, both):
+            if (e, h) == (0, 1):
+                parted[e, h] = shared.tile([P, PASSES, HALF], U16, name="parted01", align_bytes=64, offset=at + 2 * HALF)
+            else:
                 parted[e, h] = keep.tile([P, PASSES, HALF], U16, name=f"parted{e}{h}", align_bytes=64)
-                nc.vector.tensor_copy(
-                    parted[e, h][:], both[e].bitcast(U16).rearrange("p (j d) -> p d j", d=PASSES)
-                )
+            nc.vector.tensor_copy(parted[e, h][:], both[:].bitcast(U16).rearrange("p (j d) -> p d j", d=PASSES))
 
         def round_wa(g, a, rounded):
             nc.scalar.copy(
@@ -140,23 +142,34 @@ def tile_list_rgg_relu_kernel(
             pages.append(keep.tile([P, T], F32, name=f"page{len(pages)}", tag=tag, align_bytes=64))
             nc.gpsimd.memset(pages[-1][:], 0.0)
 
-        at = 12 * N + 2 * HALF + 4 * T
-        both_src = keep.tile([P, HALF], U32, name="both_src", align_bytes=64)
+        at = 4 * N + 4 * T
+        both_src = keep.tile([P, HALF], U32, name="both_src", tag="src", align_bytes=64)
         both_dst = keep.tile([P, HALF], U32, name="both_dst", tag="first1", align_bytes=64)
-        pick_words(0, [both_src[:], both_dst[:]])
+        pick_words(0, 0, both_src)
+        pick_words(1, 0, both_dst)
+        part_words(0, 0, both_src)
+        part_words(1, 0, both_dst)
         late = keep.tile([P, PASSES * 4, WIDE], F32, name="wa_late", tag="first1", align_bytes=64)
         for a in range(PASSES):
             wa_raw[1, a] = late[:, 4 * a : 4 * a + 4, :]
             load_wa(1, a)
-        early = shared.tile([P, PASSES * WIDE, 4], BF16, name="early", align_bytes=64, offset=at + 2 * HALF - 64)
+        next_src = keep.tile([P, HALF], U32, name="next_src", tag="src", align_bytes=64)
+        pick_words(0, 1, next_src)
+        early = shared.tile([P, PASSES * WIDE, 4], BF16, name="early", align_bytes=64, offset=at)
         for a in range(PASSES):
             round_wa(0, a, early[:, a * WIDE : (a + 1) * WIDE, :])
         quantise_wa(0, 0, early[:])
         picked1 = shared.tile([P, 2 * HALF], U8, name="picked1", align_bytes=64, offset=at)
-        spread_rows(1, pick_scales(1, picked1), 0)
-        both1 = shared.tile([P, 2, HALF], U32, name="both1", align_bytes=64, offset=at + 2 * HALF)
-        pick_words(1, [both1[:, 0, :], both1[:, 1, :]])
-        pages.append(shared.tile([P, T], F32, name="page1", align_bytes=64, offset=at + 2 * HALF))
+        next_dst = shared.tile([P, HALF], U32, name="next_dst", align_bytes=64, offset=at + 6 * HALF)
+        pick_scales(0, 1, picked1[:, 0:HALF])
+        pick_scales(1, 1, picked1[:, HALF : 2 * HALF])
+        spread_rows(1, picked1[:].bitcast(I32), 0)
+        pick_words(1, 1, next_dst)
+        part_words(0, 1, next_src)
+        part_words(1, 1, next_dst)
+        wc_w.append(keep.tile([P, PASSES, WIDE], I32, name="wc_w1", tag="src", align_bytes=64))
+        load_wc(1)
+        pages.append(shared.tile([P, T], F32, name="page1", align_bytes=64, offset=at + 6 * HALF))
         nc.gpsimd.memset(pages[1][:], 0.0)
 
         wgo_bank = psum.tile([P, HALF], F32, name="wgo_bank", tag="za1")
@@ -166,6 +179,7 @@ def tile_list_rgg_relu_kernel(
 
         def half_unit(u, t, h, weighted):
             n_cols = slice(t * P, (t + 1) * P)
+            g, own = divmod(t * P, WIDE)
             ms_bank = psum.tile([P, HALF], F32, name="ms_bank", tag=f"ms{u % 2}")
             for a in reversed(range(PASSES)):
                 for b in range(BLOCKS):
@@ -173,12 +187,14 @@ def tile_list_rgg_relu_kernel(
                         out=ms_bank[:, b * P : (b + 1) * P],
                         lhsT=parted[0, h][:, a, b * P : (b + 1) * P].bitcast(FP4X4),
                         lhsT_scale=scales_of(h, a, b * P, P),
-                        rhs=wc_w[:, a, n_cols].bitcast(FP8X4),
+                        rhs=wc_w[g][:, a, own : own + P].bitcast(FP8X4),
                         rhs_scale=scales_of(0, a, WC_AT + t * P, P),
                         start=(a == PASSES - 1 and b == 0),
                         stop=(a == 0 and b == BLOCKS - 1),
                     )
-            if u == 2:
+            if u == 0:
+                positive = keep.tile([P, HALF], F32, name="positive0", tag="early1", align_bytes=64)
+            elif u == 2:
                 positive = keep.tile([P, HALF], F32, name="positive2", tag="first1", align_bytes=64)
             else:
                 positive = ring.tile([P, HALF], F32, name="positive")
@@ -190,7 +206,6 @@ def tile_list_rgg_relu_kernel(
                     scale=wgo_cols[:, c : c + 1],
                 )
             za_bank = psum.tile([P, HALF], F32, name="za_bank", tag=f"za{u % 2}")
-            g, own = divmod(t * P, WIDE)
             for a in reversed(range(PASSES)):
                 nc.tensor.matmul_mx(
                     out=za_bank[:],

@@ -26,6 +26,7 @@ WB_AT = 2 * HALF
 WC_AT = WB_AT + N
 PLANE = WC_AT + N
 WIDE = N // 2
+SPLIT = 3 * P
 
 
 def tile_list_rgg_relu_kernel(
@@ -121,7 +122,7 @@ def tile_list_rgg_relu_kernel(
 
         def part_words(e, h, both):
             if (e, h) == (0, 1):
-                parted[e, h] = shared.tile([P, PASSES, HALF], U16, name="parted01", align_bytes=64, offset=at + 2 * HALF)
+                parted[e, h] = shared.tile([P, PASSES, HALF], U16, name="parted01", align_bytes=64, offset=at + 2 * HALF + 64)
             else:
                 parted[e, h] = keep.tile([P, PASSES, HALF], U16, name=f"parted{e}{h}", align_bytes=64)
             nc.vector.tensor_copy(parted[e, h][:], both[:].bitcast(U16).rearrange("p (j d) -> p d j", d=PASSES))
@@ -138,11 +139,7 @@ def tile_list_rgg_relu_kernel(
                 out=wa_w[g][:, cols].bitcast(FP8X4), scales=wa_s[g][:, cols], in_=rounded.rearrange("p n i -> p (n i)")
             )
 
-        def clear_page(tag):
-            pages.append(keep.tile([P, T], F32, name=f"page{len(pages)}", tag=tag, align_bytes=64))
-            nc.gpsimd.memset(pages[-1][:], 0.0)
-
-        at = 4 * N + 4 * T
+        at = 4 * N + 8 * T
         both_src = keep.tile([P, HALF], U32, name="both_src", tag="src", align_bytes=64)
         both_dst = keep.tile([P, HALF], U32, name="both_dst", tag="first1", align_bytes=64)
         pick_words(0, 0, both_src)
@@ -159,8 +156,10 @@ def tile_list_rgg_relu_kernel(
         for a in range(PASSES):
             round_wa(0, a, early[:, a * WIDE : (a + 1) * WIDE, :])
         quantise_wa(0, 0, early[:])
-        picked1 = shared.tile([P, 2 * HALF], U8, name="picked1", align_bytes=64, offset=at)
-        next_dst = shared.tile([P, HALF], U32, name="next_dst", align_bytes=64, offset=at + 6 * HALF)
+        pages.append(shared.tile([P, T], F32, name="page1", align_bytes=64, offset=at - 4 * T + 64))
+        nc.gpsimd.memset(pages[1][:], 0.0)
+        picked1 = shared.tile([P, 2 * HALF], U8, name="picked1", align_bytes=64, offset=at + 64)
+        next_dst = shared.tile([P, HALF], U32, name="next_dst", align_bytes=64, offset=at + 6 * HALF + 64)
         pick_scales(0, 1, picked1[:, 0:HALF])
         pick_scales(1, 1, picked1[:, HALF : 2 * HALF])
         spread_rows(1, picked1[:].bitcast(I32), 0)
@@ -169,8 +168,6 @@ def tile_list_rgg_relu_kernel(
         part_words(1, 1, next_dst)
         wc_w.append(keep.tile([P, PASSES, WIDE], I32, name="wc_w1", tag="src", align_bytes=64))
         load_wc(1)
-        pages.append(shared.tile([P, T], F32, name="page1", align_bytes=64, offset=at + 6 * HALF))
-        nc.gpsimd.memset(pages[1][:], 0.0)
 
         wgo_bank = psum.tile([P, HALF], F32, name="wgo_bank", tag="za1")
         nc.tensor.transpose(wgo_bank[:, 0:P], wgo_rows[:], ident[:])
@@ -178,7 +175,6 @@ def tile_list_rgg_relu_kernel(
         nc.scalar.copy(wgo_cols[:], wgo_bank[:, 0 : J // P])
 
         def half_unit(u, t, h, weighted):
-            n_cols = slice(t * P, (t + 1) * P)
             g, own = divmod(t * P, WIDE)
             ms_bank = psum.tile([P, HALF], F32, name="ms_bank", tag=f"ms{u % 2}")
             for a in reversed(range(PASSES)):
@@ -228,25 +224,32 @@ def tile_list_rgg_relu_kernel(
             turned = psum.tile([P, HALF], F32, name="turned", tag=f"ms{u % 2}")
             for b in range(BLOCKS):
                 nc.tensor.transpose(turned[:, b * P : (b + 1) * P], weighted[:, b * P : (b + 1) * P], ident[:])
-            gate = ring.tile([P, HALF], F32, name="gate", bufs=8)
-            message = ring.tile([P, HALF], F32, name="message", bufs=8)
-            nc.scalar.activation(gate[:], za_bank[:], ACT.Sigmoid)
-            nc.scalar.copy(message[:], turned[:])
-            page = pages[t % 3]
-            nc.vector.tensor_tensor(page[:].indirect(half_list(1, h)), gate[:], message[:], MULT)
-            if h == 1:
-                nc.sync.dma_start(out=out[n_cols, :], in_=page[:])
+            edges = slice(h * HALF, (h + 1) * HALF)
+            nc.scalar.activation(gates[t][:, edges], za_bank[:], ACT.Sigmoid)
+            nc.scalar.copy(messages[t][:, edges], turned[:])
 
-        units = [(2 * g + i, h) for g in range(2) for h in range(2) for i in range(2)]
-        for u, (t, h) in enumerate(units):
-            if u == 1:
-                weighted = keep.tile([P, HALF], F32, name="weighted1", tag="stage1", align_bytes=64)
+        def place(t, first, last):
+            page = pages[t % 2]
+            nc.vector.tensor_tensor(
+                page[:].indirect(dst_list[:, first // 16 : last // 16]), gates[t][:, first:last], messages[t][:, first:last], MULT
+            )
+            if last == J:
+                nc.sync.dma_start(out=out[t * P : (t + 1) * P, :], in_=page[:])
+
+        gates = [keep.tile([P, J], F32, name=f"gate{t}") for t in range(N // P)]
+        messages = [keep.tile([P, J], F32, name=f"message{t}") for t in range(N // P)]
+        units = [(0, 0, 0, HALF), (1, 0, 0, SPLIT), (0, 1, HALF, J), (1, 1, SPLIT, J)]
+        units = units + [(2, 0, 0, 0), (2, 1, 0, J), (3, 0, 0, 0), (3, 1, 0, J)]
+        for u, (t, h, first, last) in enumerate(units):
+            if u == 0:
+                weighted = keep.tile([P, HALF], F32, name="weighted0", tag="stage1", align_bytes=64)
             else:
                 weighted = ring.tile([P, HALF], F32, name="weighted")
             half_unit(u, t, h, weighted)
+            if last > first:
+                place(t, first, last)
             if u == 1:
                 rounded = keep.tile([P, PASSES * WIDE, 4], BF16, name="rounded1", tag="stage1", align_bytes=64)
                 for a in range(PASSES):
                     round_wa(1, a, rounded[:, a * WIDE : (a + 1) * WIDE, :])
                 quantise_wa(1, 0, rounded[:])
-                clear_page("stage1")

@@ -26,7 +26,6 @@ WB_AT = 2 * HALF
 WC_AT = WB_AT + N
 PLANE = WC_AT + N
 WIDE = N // 2
-SPLIT = 3 * P
 
 
 def tile_list_rgg_relu_kernel(
@@ -37,6 +36,7 @@ def tile_list_rgg_relu_kernel(
         keep = ctx.enter_context(tc.tile_pool(name="keep", bufs=1))
         ring = ctx.enter_context(tc.tile_pool(name="ring", bufs=2))
         shared = ctx.enter_context(tc.tile_pool(name="shared", bufs=1))
+        behind = ctx.enter_context(tc.tile_pool(name="behind", bufs=1))
         psum = ctx.enter_context(tc.psum_pool(name="psum", bufs=1))
 
         src_list = keep.tile([P, J // 16], U16, name="src_list")
@@ -44,30 +44,26 @@ def tile_list_rgg_relu_kernel(
         lists = (src_list, dst_list)
         tab_w = keep.tile([P, T], I32, name="tab_w", align_bytes=64)
         tab_s = keep.tile([P, T // 4], I32, name="tab_s", align_bytes=64)
-        planes = {
-            (h, a): keep.tile([P, (PLANE, WB_AT)[h] // 4], I32, name=f"plane{h}{a}", align_bytes=64)
-            for h in range(2)
-            for a in range(PASSES)
-        }
+        planes = {(0, a): keep.tile([P, PLANE // 4], I32, name=f"plane0{a}", align_bytes=64) for a in range(PASSES)}
         rows_s = planes[0, 0]
         wa_raw = {(0, a): keep.tile([P, 4, WIDE], F32, name=f"wa_raw{a}", tag=f"early{a}", align_bytes=64) for a in range(PASSES)}
         wc_w = [keep.tile([P, PASSES, WIDE], I32, name="wc_w0", align_bytes=64)]
         wa_w = [keep.tile([P, PASSES * WIDE], U32, name=f"wa_w{g}", align_bytes=64) for g in range(2)]
         wa_s = [keep.tile([P, PASSES * WIDE], U8, name=f"wa_s{g}", align_bytes=64) for g in range(2)]
         pages = []
-        ident = keep.tile([P, P], F32, name="ident")
         wgo_rows = keep.tile([P, P], F32, name="wgo_rows")
-        warm = keep.tile([P, 1], F32, name="warm")
+        warm = keep.tile([P, 1], F32, name="warm", tag="to_ident")
 
         nc.vector.memset(tab_s[32:64, :], 0)
         nc.vector.memset(tab_s[64:128, :], 0)
         nc.vector.memset(rows_s[32:64, WB_AT // 4 :], 0)
         nc.vector.memset(rows_s[64:128, WB_AT // 4 :], 0)
-        for key in ((0, 1), (1, 0), (1, 1)):
-            nc.vector.memset(planes[key][:], 0)
+        nc.vector.memset(planes[0, 1][:], 0)
         nc.gpsimd.memset(wgo_rows[:], 0.0)
+        nc.scalar.dma_start(out=tab_s[0:ROWS, :], in_=tab_scales.rearrange("a q n -> (a q) n").bitcast(I32))
+        nc.scalar.activation(warm[:], wgo_rows[:, 0:1], ACT.Sigmoid)
+        ident = keep.tile([P, P], F32, name="ident", tag="to_ident")
         make_identity(nc, ident[:])
-        nc.scalar.activation(warm[:], ident[:, 0:1], ACT.Sigmoid)
 
         def load_wa(g, a):
             rows = wa[512 * a : 512 * (a + 1), g * WIDE : (g + 1) * WIDE]
@@ -81,12 +77,11 @@ def tile_list_rgg_relu_kernel(
             return scales.rearrange("a q n -> (a q) n").bitcast(I32)
 
         nc.sync.dma_start(src_list[:], offs)
-        nc.sync.dma_start(out=tab_s[0:ROWS, :], in_=scale_rows(tab_scales))
         nc.sync.dma_start(dst_list[:], offs2)
         nc.sync.dma_start(out=tab_w[:], in_=tab_words[0].rearrange("p t b -> p (t b)").bitcast(I32))
         nc.sync.dma_start(out=rows_s[0:ROWS, WB_AT // 4 : WC_AT // 4], in_=scale_rows(wb_scales))
         nc.sync.dma_start(out=rows_s[0:ROWS, WC_AT // 4 : PLANE // 4], in_=scale_rows(wc_scales))
-        nc.sync.dma_start(out=wgo_rows[0 : J // P, :], in_=wgo[0:1, :].rearrange("o (c p) -> (o c) p", p=P))
+        nc.gpsimd.dma_start(out=wgo_rows[0 : J // P, :], in_=wgo[0:1, :].rearrange("o (c p) -> (o c) p", p=P))
         load_wa(0, 0)
         load_wc(0)
         load_wa(0, 1)
@@ -141,12 +136,16 @@ def tile_list_rgg_relu_kernel(
 
         at = 4 * N + 8 * T
         both_src = keep.tile([P, HALF], U32, name="both_src", tag="src", align_bytes=64)
-        both_dst = keep.tile([P, HALF], U32, name="both_dst", tag="first1", align_bytes=64)
+        both_dst = behind.tile([P, HALF], U32, name="both_dst", align_bytes=64, offset=4 * HALF - 64)
         pick_words(0, 0, both_src)
         pick_words(1, 0, both_dst)
         part_words(0, 0, both_src)
         part_words(1, 0, both_dst)
-        late = keep.tile([P, PASSES * 4, WIDE], F32, name="wa_late", tag="first1", align_bytes=64)
+        late_planes = behind.tile([P, PASSES * WB_AT // 4], I32, name="late_planes", align_bytes=64, offset=0)
+        nc.gpsimd.memset(late_planes[:], 0)
+        for a in range(PASSES):
+            planes[1, a] = late_planes[:, a * WB_AT // 4 : (a + 1) * WB_AT // 4]
+        late = behind.tile([P, PASSES * 4, WIDE], F32, name="wa_late", align_bytes=64, offset=4 * HALF)
         for a in range(PASSES):
             wa_raw[1, a] = late[:, 4 * a : 4 * a + 4, :]
             load_wa(1, a)
@@ -169,14 +168,14 @@ def tile_list_rgg_relu_kernel(
         wc_w.append(keep.tile([P, PASSES, WIDE], I32, name="wc_w1", tag="src", align_bytes=64))
         load_wc(1)
 
-        wgo_bank = psum.tile([P, HALF], F32, name="wgo_bank", tag="za1")
+        wgo_bank = psum.tile([P, HALF], F32, name="wgo_bank", tag="bank2")
         nc.tensor.transpose(wgo_bank[:, 0:P], wgo_rows[:], ident[:])
         wgo_cols = keep.tile([P, J // P], F32, name="wgo_cols")
         nc.scalar.copy(wgo_cols[:], wgo_bank[:, 0 : J // P])
 
-        def half_unit(u, t, h, weighted):
+        def sum_message(t, h, bank, positive):
             g, own = divmod(t * P, WIDE)
-            ms_bank = psum.tile([P, HALF], F32, name="ms_bank", tag=f"ms{u % 2}")
+            ms_bank = psum.tile([P, HALF], F32, name="ms_bank", tag=bank)
             for a in reversed(range(PASSES)):
                 for b in range(BLOCKS):
                     nc.tensor.matmul_mx(
@@ -188,20 +187,25 @@ def tile_list_rgg_relu_kernel(
                         start=(a == PASSES - 1 and b == 0),
                         stop=(a == 0 and b == BLOCKS - 1),
                     )
-            if u == 0:
-                positive = keep.tile([P, HALF], F32, name="positive0", tag="early1", align_bytes=64)
-            elif u == 2:
-                positive = keep.tile([P, HALF], F32, name="positive2", tag="first1", align_bytes=64)
-            else:
-                positive = ring.tile([P, HALF], F32, name="positive")
             nc.scalar.activation(positive[:], ms_bank[:], ACT.Relu)
+
+        def weigh(h, positive, weighted):
             for b in range(BLOCKS):
                 c = h * BLOCKS + b
                 nc.scalar.activation(
                     weighted[:, b * P : (b + 1) * P], positive[:, b * P : (b + 1) * P], ACT.Copy,
                     scale=wgo_cols[:, c : c + 1],
                 )
-            za_bank = psum.tile([P, HALF], F32, name="za_bank", tag=f"za{u % 2}")
+
+        def turn(t, h, bank, weighted):
+            turned = psum.tile([P, HALF], F32, name="turned", tag=bank)
+            for b in range(BLOCKS):
+                nc.tensor.transpose(turned[:, b * P : (b + 1) * P], weighted[:, b * P : (b + 1) * P], ident[:])
+            nc.scalar.copy(messages[t][:, h * HALF : (h + 1) * HALF], turned[:])
+
+        def sum_gate(t, h, bank):
+            g, own = divmod(t * P, WIDE)
+            za_bank = psum.tile([P, HALF], F32, name="za_bank", tag=bank)
             for a in reversed(range(PASSES)):
                 nc.tensor.matmul_mx(
                     out=za_bank[:],
@@ -212,6 +216,7 @@ def tile_list_rgg_relu_kernel(
                     start=(a == PASSES - 1),
                     stop=False,
                 )
+            for a in range(PASSES):
                 nc.tensor.matmul_mx(
                     out=za_bank[:],
                     lhsT=wa_w[g][:, a * WIDE + own : a * WIDE + own + P].bitcast(FP8X4),
@@ -219,17 +224,12 @@ def tile_list_rgg_relu_kernel(
                     rhs=parted[1, h][:, a, :].bitcast(FP4X4),
                     rhs_scale=scales_of(h, a, HALF, HALF),
                     start=False,
-                    stop=(a == 0),
+                    stop=(a == PASSES - 1),
                 )
-            turned = psum.tile([P, HALF], F32, name="turned", tag=f"ms{u % 2}")
-            for b in range(BLOCKS):
-                nc.tensor.transpose(turned[:, b * P : (b + 1) * P], weighted[:, b * P : (b + 1) * P], ident[:])
-            edges = slice(h * HALF, (h + 1) * HALF)
-            nc.scalar.activation(gates[t][:, edges], za_bank[:], ACT.Sigmoid)
-            nc.scalar.copy(messages[t][:, edges], turned[:])
+            nc.scalar.activation(gates[t][:, h * HALF : (h + 1) * HALF], za_bank[:], ACT.Sigmoid)
 
         def place(t, first, last):
-            page = pages[t % 2]
+            page = pages[t % 3]
             nc.vector.tensor_tensor(
                 page[:].indirect(dst_list[:, first // 16 : last // 16]), gates[t][:, first:last], messages[t][:, first:last], MULT
             )
@@ -238,18 +238,39 @@ def tile_list_rgg_relu_kernel(
 
         gates = [keep.tile([P, J], F32, name=f"gate{t}") for t in range(N // P)]
         messages = [keep.tile([P, J], F32, name=f"message{t}") for t in range(N // P)]
-        units = [(0, 0, 0, HALF), (1, 0, 0, SPLIT), (0, 1, HALF, J), (1, 1, SPLIT, J)]
-        units = units + [(2, 0, 0, 0), (2, 1, 0, J), (3, 0, 0, 0), (3, 1, 0, J)]
-        for u, (t, h, first, last) in enumerate(units):
+
+        positive0 = keep.tile([P, HALF], F32, name="positive0", tag="early1", align_bytes=64)
+        weighted0 = ring.tile([P, HALF], F32, name="weighted")
+        positive1 = ring.tile([P, HALF], F32, name="positive")
+        weighted1 = keep.tile([P, HALF], F32, name="weighted1", tag="stage1", align_bytes=64)
+        sum_message(0, 0, "bank0", positive0)
+        weigh(0, positive0, weighted0)
+        turn(0, 0, "bank0", weighted0)
+        sum_gate(0, 0, "bank2")
+        place(0, 0, HALF)
+        sum_message(1, 0, "bank1", positive1)
+        weigh(0, positive1, weighted1)
+        turn(1, 0, "bank1", weighted1)
+        sum_gate(1, 0, "bank0")
+        place(1, 0, HALF)
+
+        rounded = keep.tile([P, PASSES * WIDE, 4], BF16, name="rounded1", tag="stage1", align_bytes=64)
+        for a in range(PASSES):
+            round_wa(1, a, rounded[:, a * WIDE : (a + 1) * WIDE, :])
+        quantise_wa(1, 0, rounded[:])
+        pages.append(keep.tile([P, T], F32, name="page2", tag="stage1", align_bytes=64))
+        nc.gpsimd.memset(pages[2][:], 0.0)
+
+        units = [(0, 1), (1, 1), (2, 0), (3, 0), (2, 1), (3, 1)]
+        for u, (t, h) in enumerate(units):
             if u == 0:
-                weighted = keep.tile([P, HALF], F32, name="weighted0", tag="stage1", align_bytes=64)
+                positive = behind.tile([P, HALF], F32, name="positive2", align_bytes=64, offset=4 * HALF)
             else:
-                weighted = ring.tile([P, HALF], F32, name="weighted")
-            half_unit(u, t, h, weighted)
-            if last > first:
-                place(t, first, last)
-            if u == 1:
-                rounded = keep.tile([P, PASSES * WIDE, 4], BF16, name="rounded1", tag="stage1", align_bytes=64)
-                for a in range(PASSES):
-                    round_wa(1, a, rounded[:, a * WIDE : (a + 1) * WIDE, :])
-                quantise_wa(1, 0, rounded[:])
+                positive = ring.tile([P, HALF], F32, name="positive")
+            weighted = ring.tile([P, HALF], F32, name="weighted")
+            bank = f"bank{1 - u % 2}"
+            sum_message(t, h, bank, positive)
+            weigh(h, positive, weighted)
+            sum_gate(t, h, "bank2")
+            turn(t, h, bank, weighted)
+            place(t, h * HALF, (h + 1) * HALF)

@@ -26,6 +26,7 @@ WB_AT = 2 * HALF
 WC_AT = WB_AT + N
 PLANE = WC_AT + N
 WIDE = N // 2
+SHORT = 3 * J // 8
 
 
 def tile_list_rgg_relu_kernel(
@@ -37,6 +38,7 @@ def tile_list_rgg_relu_kernel(
         ring = ctx.enter_context(tc.tile_pool(name="ring", bufs=2))
         shared = ctx.enter_context(tc.tile_pool(name="shared", bufs=1))
         behind = ctx.enter_context(tc.tile_pool(name="behind", bufs=1))
+        first = ctx.enter_context(tc.tile_pool(name="first", bufs=1))
         psum = ctx.enter_context(tc.psum_pool(name="psum", bufs=1))
 
         src_list = keep.tile([P, J // 16], U16, name="src_list")
@@ -46,13 +48,13 @@ def tile_list_rgg_relu_kernel(
         tab_s = keep.tile([P, T // 4], I32, name="tab_s", align_bytes=64)
         planes = {(0, a): keep.tile([P, PLANE // 4], I32, name=f"plane0{a}", align_bytes=64) for a in range(PASSES)}
         rows_s = planes[0, 0]
-        wa_raw = {(0, a): keep.tile([P, 4, WIDE], F32, name=f"wa_raw{a}", tag=f"early{a}", align_bytes=64) for a in range(PASSES)}
+        wa_raw = {(0, a): first.tile([P, 4, WIDE], F32, name=f"wa_raw{a}", align_bytes=64, offset=a * 16 * WIDE) for a in range(PASSES)}
         wc_w = [keep.tile([P, PASSES, WIDE], I32, name="wc_w0", align_bytes=64)]
         wa_w = [keep.tile([P, PASSES * WIDE], U32, name=f"wa_w{g}", align_bytes=64) for g in range(2)]
         wa_s = [keep.tile([P, PASSES * WIDE], U8, name=f"wa_s{g}", align_bytes=64) for g in range(2)]
         pages = []
         wgo_rows = keep.tile([P, P], F32, name="wgo_rows")
-        warm = keep.tile([P, 1], F32, name="warm", tag="to_ident")
+        warm = keep.tile([P, 1], F32, name="warm", tag="to_page")
 
         nc.vector.memset(tab_s[32:64, :], 0)
         nc.vector.memset(tab_s[64:128, :], 0)
@@ -62,8 +64,8 @@ def tile_list_rgg_relu_kernel(
         nc.gpsimd.memset(wgo_rows[:], 0.0)
         nc.scalar.dma_start(out=tab_s[0:ROWS, :], in_=tab_scales.rearrange("a q n -> (a q) n").bitcast(I32))
         nc.scalar.activation(warm[:], wgo_rows[:, 0:1], ACT.Sigmoid)
-        ident = keep.tile([P, P], F32, name="ident", tag="to_ident")
-        make_identity(nc, ident[:])
+        pages.append(keep.tile([P, T], F32, name="page0", tag="to_page"))
+        nc.gpsimd.memset(pages[0][:], 0.0)
 
         def load_wa(g, a):
             rows = wa[512 * a : 512 * (a + 1), g * WIDE : (g + 1) * WIDE]
@@ -104,8 +106,12 @@ def tile_list_rgg_relu_kernel(
         spread_rows(0, rows_s[:], 1)
         wb_w = shared.tile([P, PASSES, N // 2], I32, name="wb_w", align_bytes=64, offset=0)
         nc.sync.dma_start(out=wb_w[:], in_=wb_words.rearrange("a p n -> p a n").bitcast(I32))
-        pages.append(shared.tile([P, T], F32, name="page0", align_bytes=64, offset=4 * N))
-        nc.gpsimd.memset(pages[0][:], 0.0)
+        ident = shared.tile([P, P], F32, name="ident", align_bytes=64, offset=4 * N)
+        make_identity(nc, ident[:])
+        late_planes = shared.tile([P, PASSES * WB_AT // 4], I32, name="late_planes", align_bytes=64, offset=5 * N)
+        nc.gpsimd.memset(late_planes[:], 0)
+        for a in range(PASSES):
+            planes[1, a] = late_planes[:, a * WB_AT // 4 : (a + 1) * WB_AT // 4]
 
         def scales_of(h, a, first, width):
             return planes[h, a][:].bitcast(U8)[:, first : first + width]
@@ -134,20 +140,15 @@ def tile_list_rgg_relu_kernel(
                 out=wa_w[g][:, cols].bitcast(FP8X4), scales=wa_s[g][:, cols], in_=rounded.rearrange("p n i -> p (n i)")
             )
 
-        at = 4 * N + 8 * T
+        at = 9 * N + 4 * T
         both_src = keep.tile([P, HALF], U32, name="both_src", tag="src", align_bytes=64)
-        both_dst = behind.tile([P, HALF], U32, name="both_dst", align_bytes=64, offset=4 * HALF - 64)
+        both_dst = behind.tile([P, HALF], U32, name="both_dst", align_bytes=64, offset=6 * HALF)
         pick_words(0, 0, both_src)
         pick_words(1, 0, both_dst)
         part_words(0, 0, both_src)
         part_words(1, 0, both_dst)
-        late_planes = behind.tile([P, PASSES * WB_AT // 4], I32, name="late_planes", align_bytes=64, offset=0)
-        nc.gpsimd.memset(late_planes[:], 0)
         for a in range(PASSES):
-            planes[1, a] = late_planes[:, a * WB_AT // 4 : (a + 1) * WB_AT // 4]
-        late = behind.tile([P, PASSES * 4, WIDE], F32, name="wa_late", align_bytes=64, offset=4 * HALF)
-        for a in range(PASSES):
-            wa_raw[1, a] = late[:, 4 * a : 4 * a + 4, :]
+            wa_raw[1, a] = behind.tile([P, 4, WIDE], F32, name=f"wa_late{a}", align_bytes=64, offset=(1 - a) * 8 * HALF)
             load_wa(1, a)
         next_src = keep.tile([P, HALF], U32, name="next_src", tag="src", align_bytes=64)
         pick_words(0, 1, next_src)
@@ -157,8 +158,8 @@ def tile_list_rgg_relu_kernel(
         quantise_wa(0, 0, early[:])
         pages.append(shared.tile([P, T], F32, name="page1", align_bytes=64, offset=at - 4 * T + 64))
         nc.gpsimd.memset(pages[1][:], 0.0)
-        picked1 = shared.tile([P, 2 * HALF], U8, name="picked1", align_bytes=64, offset=at + 64)
-        next_dst = shared.tile([P, HALF], U32, name="next_dst", align_bytes=64, offset=at + 6 * HALF + 64)
+        picked1 = first.tile([P, 2 * HALF], U8, name="picked1", align_bytes=64, offset=16 * WIDE + 4 * HALF)
+        next_dst = first.tile([P, HALF], U32, name="next_dst", align_bytes=64, offset=16 * WIDE + 6 * HALF)
         pick_scales(0, 1, picked1[:, 0:HALF])
         pick_scales(1, 1, picked1[:, HALF : 2 * HALF])
         spread_rows(1, picked1[:].bitcast(I32), 0)
@@ -168,7 +169,7 @@ def tile_list_rgg_relu_kernel(
         wc_w.append(keep.tile([P, PASSES, WIDE], I32, name="wc_w1", tag="src", align_bytes=64))
         load_wc(1)
 
-        wgo_bank = psum.tile([P, HALF], F32, name="wgo_bank", tag="bank2")
+        wgo_bank = psum.tile([P, HALF], F32, name="wgo_bank", tag="bank3")
         nc.tensor.transpose(wgo_bank[:, 0:P], wgo_rows[:], ident[:])
         wgo_cols = keep.tile([P, J // P], F32, name="wgo_cols")
         nc.scalar.copy(wgo_cols[:], wgo_bank[:, 0 : J // P])
@@ -239,38 +240,34 @@ def tile_list_rgg_relu_kernel(
         gates = [keep.tile([P, J], F32, name=f"gate{t}") for t in range(N // P)]
         messages = [keep.tile([P, J], F32, name=f"message{t}") for t in range(N // P)]
 
-        positive0 = keep.tile([P, HALF], F32, name="positive0", tag="early1", align_bytes=64)
-        weighted0 = ring.tile([P, HALF], F32, name="weighted")
-        positive1 = ring.tile([P, HALF], F32, name="positive")
-        weighted1 = keep.tile([P, HALF], F32, name="weighted1", tag="stage1", align_bytes=64)
-        sum_message(0, 0, "bank0", positive0)
-        weigh(0, positive0, weighted0)
-        turn(0, 0, "bank0", weighted0)
-        sum_gate(0, 0, "bank2")
-        place(0, 0, HALF)
-        sum_message(1, 0, "bank1", positive1)
-        weigh(0, positive1, weighted1)
-        turn(1, 0, "bank1", weighted1)
-        sum_gate(1, 0, "bank0")
-        place(1, 0, HALF)
+        def late_columns(a):
+            rounded = keep.tile([P, WIDE, 4], BF16, name=f"rounded{a}", tag=f"stage{a}", align_bytes=64)
+            round_wa(1, a, rounded[:])
+            quantise_wa(1, a * WIDE, rounded[:])
 
-        rounded = keep.tile([P, PASSES * WIDE, 4], BF16, name="rounded1", tag="stage1", align_bytes=64)
-        for a in range(PASSES):
-            round_wa(1, a, rounded[:, a * WIDE : (a + 1) * WIDE, :])
-        quantise_wa(1, 0, rounded[:])
-        pages.append(keep.tile([P, T], F32, name="page2", tag="stage1", align_bytes=64))
-        nc.gpsimd.memset(pages[2][:], 0.0)
-
-        units = [(0, 1), (1, 1), (2, 0), (3, 0), (2, 1), (3, 1)]
+        units = [(0, 0), (1, 0), (0, 1), (1, 1), (2, 0), (3, 0), (2, 1), (3, 1)]
         for u, (t, h) in enumerate(units):
             if u == 0:
-                positive = behind.tile([P, HALF], F32, name="positive2", align_bytes=64, offset=4 * HALF)
+                positive = first.tile([P, HALF], F32, name="positive0", align_bytes=64, offset=16 * WIDE)
             else:
                 positive = ring.tile([P, HALF], F32, name="positive")
-            weighted = ring.tile([P, HALF], F32, name="weighted")
-            bank = f"bank{1 - u % 2}"
-            sum_message(t, h, bank, positive)
+            if u in (1, 2):
+                weighted = keep.tile([P, HALF], F32, name=f"weighted{u}", tag=f"stage{u - 1}", align_bytes=64)
+            elif u == 3:
+                weighted = behind.tile([P, HALF], F32, name="weighted3", align_bytes=64, offset=0)
+            else:
+                weighted = ring.tile([P, HALF], F32, name="weighted")
+            message_bank, gate_bank, turn_bank = ("012", "012", "210", "210", "201", "210", "201", "210")[u]
+            sum_message(t, h, f"bank{message_bank}", positive)
             weigh(h, positive, weighted)
-            sum_gate(t, h, "bank2")
-            turn(t, h, bank, weighted)
-            place(t, h * HALF, (h + 1) * HALF)
+            sum_gate(t, h, f"bank{gate_bank}")
+            turn(t, h, f"bank{turn_bank}", weighted)
+            if t == 3:
+                place(t, h * SHORT, SHORT + h * (J - SHORT))
+            else:
+                place(t, h * HALF, (h + 1) * HALF)
+            if u in (1, 2):
+                late_columns(u - 1)
+            if u == 1:
+                pages.append(keep.tile([P, T], F32, name="page2", tag="stage0", align_bytes=64))
+                nc.gpsimd.memset(pages[2][:], 0.0)

@@ -126,7 +126,10 @@ def tile_list_rgg_relu_kernel(
                 parted[e, h] = shared.tile([P, PASSES, HALF], U16, name="parted01", align_bytes=64, offset=at + 2 * HALF + 64)
             else:
                 parted[e, h] = keep.tile([P, PASSES, HALF], U16, name=f"parted{e}{h}", align_bytes=64)
-            nc.vector.tensor_copy(parted[e, h][:], both[:].bitcast(U16).rearrange("p (j d) -> p d j", d=PASSES))
+            nc.vector.tensor_copy(
+                parted[e, h][:].rearrange("p d (s j) -> p s d j", s=2),
+                both[:].bitcast(U16).rearrange("p (s j d) -> p s d j", s=2, d=PASSES),
+            )
 
         def round_wa(g, a, rounded):
             nc.scalar.copy(

@@ -46,7 +46,7 @@ def tile_list_rgg_relu_kernel(
         lists = (src_list, dst_list)
         tab_w = keep.tile([P, T], I32, name="tab_w", align_bytes=64)
         tab_s = keep.tile([P, T // 4], I32, name="tab_s", align_bytes=64)
-        planes = {(0, a): keep.tile([P, PLANE // 4], I32, name=f"plane0{a}", align_bytes=64) for a in range(PASSES)}
+        planes = {(0, 0): keep.tile([P, PLANE // 4], I32, name="plane00", align_bytes=64)}
         rows_s = planes[0, 0]
         wa_raw = {(0, a): first.tile([P, 4, WIDE], F32, name=f"wa_raw{a}", align_bytes=64, offset=a * 16 * WIDE) for a in range(PASSES)}
         wc_w = [keep.tile([P, PASSES, WIDE], I32, name="wc_w0", align_bytes=64)]
@@ -54,18 +54,19 @@ def tile_list_rgg_relu_kernel(
         wa_s = [keep.tile([P, PASSES * WIDE], U8, name=f"wa_s{g}", align_bytes=64) for g in range(2)]
         pages = []
         wgo_rows = keep.tile([P, P], F32, name="wgo_rows")
-        warm = keep.tile([P, 1], F32, name="warm", tag="to_page")
+        warm = keep.tile([P, 1], F32, name="warm", tag="to_plane", align_bytes=64)
+        ident = keep.tile([P, P], F32, name="ident", align_bytes=64)
 
         nc.vector.memset(tab_s[32:64, :], 0)
         nc.vector.memset(tab_s[64:128, :], 0)
         nc.vector.memset(rows_s[32:64, WB_AT // 4 :], 0)
         nc.vector.memset(rows_s[64:128, WB_AT // 4 :], 0)
-        nc.vector.memset(planes[0, 1][:], 0)
         nc.gpsimd.memset(wgo_rows[:], 0.0)
+        make_identity(nc, ident[:])
         nc.scalar.dma_start(out=tab_s[0:ROWS, :], in_=tab_scales.rearrange("a q n -> (a q) n").bitcast(I32))
         nc.scalar.activation(warm[:], wgo_rows[:, 0:1], ACT.Sigmoid)
-        pages.append(keep.tile([P, T], F32, name="page0", tag="to_page"))
-        nc.gpsimd.memset(pages[0][:], 0.0)
+        planes[0, 1] = keep.tile([P, PLANE // 4], I32, name="plane01", tag="to_plane", align_bytes=64)
+        nc.gpsimd.memset(planes[0, 1][:], 0)
 
         def load_wa(g, a):
             rows = wa[512 * a : 512 * (a + 1), g * WIDE : (g + 1) * WIDE]
@@ -106,8 +107,6 @@ def tile_list_rgg_relu_kernel(
         spread_rows(0, rows_s[:], 1)
         wb_w = shared.tile([P, PASSES, N // 2], I32, name="wb_w", align_bytes=64, offset=0)
         nc.sync.dma_start(out=wb_w[:], in_=wb_words.rearrange("a p n -> p a n").bitcast(I32))
-        ident = shared.tile([P, P], F32, name="ident", align_bytes=64, offset=4 * N)
-        make_identity(nc, ident[:])
         late_planes = shared.tile([P, PASSES * WB_AT // 4], I32, name="late_planes", align_bytes=64, offset=5 * N)
         nc.gpsimd.memset(late_planes[:], 0)
         for a in range(PASSES):
@@ -159,8 +158,8 @@ def tile_list_rgg_relu_kernel(
         for a in range(PASSES):
             round_wa(0, a, early[:, a * WIDE : (a + 1) * WIDE, :])
         quantise_wa(0, 0, early[:])
-        pages.append(shared.tile([P, T], F32, name="page1", align_bytes=64, offset=at - 4 * T + 64))
-        nc.gpsimd.memset(pages[1][:], 0.0)
+        pages.append(shared.tile([P, T], F32, name="page0", align_bytes=64, offset=at - 4 * T + 64))
+        nc.gpsimd.memset(pages[0][:], 0.0)
         picked1 = first.tile([P, 2 * HALF], U8, name="picked1", align_bytes=64, offset=16 * WIDE + 4 * HALF)
         next_dst = first.tile([P, HALF], U32, name="next_dst", align_bytes=64, offset=16 * WIDE + 6 * HALF)
         pick_scales(0, 1, picked1[:, 0:HALF])
@@ -169,6 +168,8 @@ def tile_list_rgg_relu_kernel(
         pick_words(1, 1, next_dst)
         part_words(0, 1, next_src)
         part_words(1, 1, next_dst)
+        pages.append(first.tile([P, T], F32, name="page1", align_bytes=64, offset=16 * WIDE + 10 * HALF - 64))
+        nc.gpsimd.memset(pages[1][:], 0.0)
         wc_w.append(keep.tile([P, PASSES, WIDE], I32, name="wc_w1", tag="src", align_bytes=64))
         load_wc(1)
 

@@ -21,12 +21,25 @@ P = 128
 PASSES = K // 512
 HALF = J // 2
 BLOCKS = HALF // P
-ROWS = K // 32
+ROW_TILES = N // P
+SCALE_ROWS = K // 32
+SRC, DST = 0, 1
+
 WB_AT = 2 * HALF
 WC_AT = WB_AT + N
 PLANE = WC_AT + N
+
 WIDE = N // 2
+PAGES = 3
 SHORT = 3 * J // 8
+
+ALIGN = 64
+WB_BYTES = PASSES * N * 2
+IDENT_BYTES = P * 4
+PAGE_BYTES = T * 4
+RAW_BYTES = 4 * WIDE * 4
+WORD_BYTES = HALF * 4
+PICKED_BYTES = 2 * HALF
 
 
 def tile_list_rgg_relu_kernel(
@@ -36,37 +49,40 @@ def tile_list_rgg_relu_kernel(
     with ExitStack() as ctx:
         keep = ctx.enter_context(tc.tile_pool(name="keep", bufs=1))
         ring = ctx.enter_context(tc.tile_pool(name="ring", bufs=2))
-        shared = ctx.enter_context(tc.tile_pool(name="shared", bufs=1))
-        behind = ctx.enter_context(tc.tile_pool(name="behind", bufs=1))
-        first = ctx.enter_context(tc.tile_pool(name="first", bufs=1))
+        after_picks = ctx.enter_context(tc.tile_pool(name="after_picks", bufs=1))
+        after_words = ctx.enter_context(tc.tile_pool(name="after_words", bufs=1))
+        after_raw = ctx.enter_context(tc.tile_pool(name="after_raw", bufs=1))
         psum = ctx.enter_context(tc.psum_pool(name="psum", bufs=1))
 
         src_list = keep.tile([P, J // 16], U16, name="src_list")
         dst_list = keep.tile([P, J // 16], U16, name="dst_list")
         lists = (src_list, dst_list)
-        tab_w = keep.tile([P, T], I32, name="tab_w", align_bytes=64)
-        tab_s = keep.tile([P, T // 4], I32, name="tab_s", align_bytes=64)
-        planes = {(0, 0): keep.tile([P, PLANE // 4], I32, name="plane00", align_bytes=64)}
-        rows_s = planes[0, 0]
-        wa_raw = {(0, a): first.tile([P, 4, WIDE], F32, name=f"wa_raw{a}", align_bytes=64, offset=a * 16 * WIDE) for a in range(PASSES)}
-        wc_w = [keep.tile([P, PASSES, WIDE], I32, name="wc_w0", align_bytes=64)]
-        wa_w = [keep.tile([P, PASSES * WIDE], U32, name=f"wa_w{g}", align_bytes=64) for g in range(2)]
-        wa_s = [keep.tile([P, PASSES * WIDE], U8, name=f"wa_s{g}", align_bytes=64) for g in range(2)]
+        tab_w = keep.tile([P, T], I32, name="tab_w", align_bytes=ALIGN)
+        tab_s = keep.tile([P, T // 4], I32, name="tab_s", align_bytes=ALIGN)
+        planes = {(0, 0): keep.tile([P, PLANE // 4], I32, name="plane00", align_bytes=ALIGN)}
+        compact = planes[0, 0]
+        wa_raw = {
+            (0, a): after_raw.tile([P, 4, WIDE], F32, name=f"wa_raw{a}", align_bytes=ALIGN, offset=a * RAW_BYTES)
+            for a in range(PASSES)
+        }
+        wc_w = [keep.tile([P, PASSES, WIDE], I32, name="wc_w0", align_bytes=ALIGN)]
+        wa_w = [keep.tile([P, PASSES * WIDE], U32, name=f"wa_w{g}", align_bytes=ALIGN) for g in range(2)]
+        wa_s = [keep.tile([P, PASSES * WIDE], U8, name=f"wa_s{g}", align_bytes=ALIGN) for g in range(2)]
         pages = []
         wgo_rows = keep.tile([P, P], F32, name="wgo_rows")
-        warm = keep.tile([P, 1], F32, name="warm", tag="to_plane", align_bytes=64)
-        ident = keep.tile([P, P], F32, name="ident", align_bytes=64)
+        warm = keep.tile([P, 1], F32, name="warm")
 
         nc.vector.memset(tab_s[32:64, :], 0)
         nc.vector.memset(tab_s[64:128, :], 0)
-        nc.vector.memset(rows_s[32:64, WB_AT // 4 :], 0)
-        nc.vector.memset(rows_s[64:128, WB_AT // 4 :], 0)
+        nc.vector.memset(compact[32:64, WB_AT // 4 :], 0)
+        nc.vector.memset(compact[64:128, WB_AT // 4 :], 0)
         nc.gpsimd.memset(wgo_rows[:], 0.0)
-        make_identity(nc, ident[:])
-        nc.scalar.dma_start(out=tab_s[0:ROWS, :], in_=tab_scales.rearrange("a q n -> (a q) n").bitcast(I32))
+
+        def scale_rows(scales):
+            return scales.rearrange("a q n -> (a q) n").bitcast(I32)
+
+        nc.scalar.dma_start(out=tab_s[0:SCALE_ROWS, :], in_=scale_rows(tab_scales))
         nc.scalar.activation(warm[:], wgo_rows[:, 0:1], ACT.Sigmoid)
-        planes[0, 1] = keep.tile([P, PLANE // 4], I32, name="plane01", tag="to_plane", align_bytes=64)
-        nc.gpsimd.memset(planes[0, 1][:], 0)
 
         def load_wa(g, a):
             rows = wa[512 * a : 512 * (a + 1), g * WIDE : (g + 1) * WIDE]
@@ -76,14 +92,11 @@ def tile_list_rgg_relu_kernel(
             cols = wc_words[:, :, g * WIDE : (g + 1) * WIDE, :]
             nc.sync.dma_start(out=wc_w[g][:], in_=cols.rearrange("a p n i -> p a (n i)").bitcast(I32))
 
-        def scale_rows(scales):
-            return scales.rearrange("a q n -> (a q) n").bitcast(I32)
-
         nc.sync.dma_start(src_list[:], offs)
         nc.sync.dma_start(dst_list[:], offs2)
         nc.sync.dma_start(out=tab_w[:], in_=tab_words[0].rearrange("p t b -> p (t b)").bitcast(I32))
-        nc.sync.dma_start(out=rows_s[0:ROWS, WB_AT // 4 : WC_AT // 4], in_=scale_rows(wb_scales))
-        nc.sync.dma_start(out=rows_s[0:ROWS, WC_AT // 4 : PLANE // 4], in_=scale_rows(wc_scales))
+        nc.sync.dma_start(out=compact[0:SCALE_ROWS, WB_AT // 4 : WC_AT // 4], in_=scale_rows(wb_scales))
+        nc.sync.dma_start(out=compact[0:SCALE_ROWS, WC_AT // 4 : PLANE // 4], in_=scale_rows(wc_scales))
         nc.gpsimd.dma_start(out=wgo_rows[0 : J // P, :], in_=wgo[0:1, :].rearrange("o (c p) -> (o c) p", p=P))
         load_wa(0, 0)
         load_wc(0)
@@ -92,43 +105,44 @@ def tile_list_rgg_relu_kernel(
         def half_list(e, h):
             return lists[e][:, h * HALF // 16 : (h + 1) * HALF // 16]
 
-        def pick_scales(e, h, picked):
-            nc.vector.tensor_copy(picked, tab_s[:].bitcast(U8).indirect(half_list(e, h)))
+        def pick_scales(h, picked):
+            for e in (SRC, DST):
+                nc.vector.tensor_copy(picked[:, e * HALF : (e + 1) * HALF], tab_s[:].bitcast(U8).indirect(half_list(e, h)))
 
-        def spread_rows(h, rows, first):
-            for r in range(first, ROWS // 4):
-                a, q = divmod(r, 4)
-                nc.sync.dma_start(out=planes[h, a][32 * q : 32 * q + 4, :], in_=rows[4 * r : 4 * r + 4, :])
+        def spread_rows(h, rows, first_run):
+            for run in range(first_run, SCALE_ROWS // 4):
+                a, q = divmod(run, 4)
+                nc.sync.dma_start(out=planes[h, a][32 * q : 32 * q + 4, :], in_=rows[4 * run : 4 * run + 4, :])
 
-        picked0 = shared.tile([P, 2 * HALF], U8, name="picked0", align_bytes=64, offset=4 * N - 64)
-        pick_scales(0, 0, picked0[:, 0:HALF])
-        pick_scales(1, 0, picked0[:, HALF : 2 * HALF])
-        nc.vector.tensor_copy(rows_s[:, 0 : WB_AT // 4], picked0[:].bitcast(I32))
-        spread_rows(0, rows_s[:], 1)
-        wb_w = shared.tile([P, PASSES, N // 2], I32, name="wb_w", align_bytes=64, offset=0)
+        picked0 = after_picks.tile([P, PICKED_BYTES], U8, name="picked0", align_bytes=ALIGN, offset=WB_BYTES - ALIGN)
+        pick_scales(0, picked0)
+        nc.vector.tensor_copy(compact[:, 0 : WB_AT // 4], picked0[:].bitcast(I32))
+        plane_at = WB_BYTES + IDENT_BYTES
+        planes[0, 1] = after_picks.tile([P, PLANE // 4], I32, name="plane01", align_bytes=ALIGN, offset=plane_at)
+        nc.gpsimd.memset(planes[0, 1][:], 0)
+        spread_rows(0, compact[:], 1)
+        wb_w = after_picks.tile([P, PASSES, N // 2], I32, name="wb_w", align_bytes=ALIGN, offset=0)
         nc.sync.dma_start(out=wb_w[:], in_=wb_words.rearrange("a p n -> p a n").bitcast(I32))
-        late_planes = shared.tile([P, PASSES * WB_AT // 4], I32, name="late_planes", align_bytes=64, offset=5 * N)
-        nc.gpsimd.memset(late_planes[:], 0)
-        for a in range(PASSES):
-            planes[1, a] = late_planes[:, a * WB_AT // 4 : (a + 1) * WB_AT // 4]
+        ident = after_picks.tile([P, P], F32, name="ident", align_bytes=ALIGN, offset=WB_BYTES)
+        make_identity(nc, ident[:])
 
-        def scales_of(h, a, first, width):
-            return planes[h, a][:].bitcast(U8)[:, first : first + width]
+        def scales_of(h, a, at, width):
+            return planes[h, a][:].bitcast(U8)[:, at : at + width]
 
         parted = {}
 
         def pick_words(e, h, both):
             nc.vector.tensor_copy(both[:], tab_w[:].bitcast(U32).indirect(half_list(e, h)))
 
-        def part_words(e, h, both):
-            if (e, h) == (0, 1):
-                parted[e, h] = shared.tile([P, PASSES, HALF], U16, name="parted01", align_bytes=64, offset=at + 2 * HALF + 64)
-            else:
-                parted[e, h] = keep.tile([P, PASSES, HALF], U16, name=f"parted{e}{h}", align_bytes=64)
+        def part_words(e, h, both, words):
+            parted[e, h] = words
             nc.vector.tensor_copy(
-                parted[e, h][:].rearrange("p d (s j) -> p s d j", s=2),
-                both[:].bitcast(U16).rearrange("p (s j d) -> p s d j", s=2, d=PASSES),
+                words[:].rearrange("p a (s j) -> p s a j", s=2),
+                both[:].bitcast(U16).rearrange("p (s j a) -> p s a j", s=2, a=PASSES),
             )
+
+        def own_words(e, h):
+            return keep.tile([P, PASSES, HALF], U16, name=f"parted{e}{h}", align_bytes=ALIGN)
 
         def round_wa(g, a, rounded):
             nc.scalar.copy(
@@ -136,41 +150,60 @@ def tile_list_rgg_relu_kernel(
                 wa_raw[g, a][:].rearrange("p i (c u) -> p c i u", u=4),
             )
 
-        def quantise_wa(g, first, rounded):
-            cols = slice(first, first + rounded.shape[1])
+        def quantise_wa(g, at, rounded):
+            cols = slice(at, at + rounded.shape[1])
             nc.vector.quantize_mx(
                 out=wa_w[g][:, cols].bitcast(FP8X4), scales=wa_s[g][:, cols], in_=rounded.rearrange("p n i -> p (n i)")
             )
 
-        at = 9 * N + 4 * T
-        both_src = keep.tile([P, HALF], U32, name="both_src", tag="src", align_bytes=64)
-        both_dst = behind.tile([P, HALF], U32, name="both_dst", align_bytes=64, offset=6 * HALF)
-        pick_words(0, 0, both_src)
-        pick_words(1, 0, both_dst)
-        part_words(0, 0, both_src)
-        part_words(1, 0, both_dst)
+        both_src = keep.tile([P, HALF], U32, name="both_src", tag="src", align_bytes=ALIGN)
+        both_dst = after_words.tile(
+            [P, HALF], U32, name="both_dst", align_bytes=ALIGN, offset=RAW_BYTES - WORD_BYTES // 2
+        )
+        pick_words(SRC, 0, both_src)
+        pick_words(DST, 0, both_dst)
+        part_words(SRC, 0, both_src, own_words(SRC, 0))
+        part_words(DST, 0, both_dst, own_words(DST, 0))
         for a in range(PASSES):
-            wa_raw[1, a] = behind.tile([P, 4, WIDE], F32, name=f"wa_late{a}", align_bytes=64, offset=(1 - a) * 8 * HALF)
+            wa_raw[1, a] = after_words.tile(
+                [P, 4, WIDE], F32, name=f"wa_late{a}", align_bytes=ALIGN, offset=(1 - a) * RAW_BYTES
+            )
             load_wa(1, a)
-        next_src = keep.tile([P, HALF], U32, name="next_src", tag="src", align_bytes=64)
-        pick_words(0, 1, next_src)
-        early = shared.tile([P, PASSES * WIDE, 4], BF16, name="early", align_bytes=64, offset=at)
+        next_src = keep.tile([P, HALF], U32, name="next_src", tag="src", align_bytes=ALIGN)
+        pick_words(SRC, 1, next_src)
+
+        early_at = plane_at + PLANE + PAGE_BYTES
+        early = after_picks.tile([P, PASSES * WIDE, 4], BF16, name="early", align_bytes=ALIGN, offset=early_at)
         for a in range(PASSES):
             round_wa(0, a, early[:, a * WIDE : (a + 1) * WIDE, :])
         quantise_wa(0, 0, early[:])
-        pages.append(shared.tile([P, T], F32, name="page0", align_bytes=64, offset=at - 4 * T + 64))
+        late_words_at = early_at + WORD_BYTES // 2 + ALIGN
+        late_planes = after_picks.tile(
+            [P, PASSES * WB_AT // 4], I32, name="late_planes", align_bytes=ALIGN, offset=late_words_at + WORD_BYTES
+        )
+        nc.gpsimd.memset(late_planes[:], 0)
+        for a in range(PASSES):
+            planes[1, a] = late_planes[:, a * WB_AT // 4 : (a + 1) * WB_AT // 4]
+        pages.append(
+            after_picks.tile([P, T], F32, name="page0", align_bytes=ALIGN, offset=early_at - PAGE_BYTES + ALIGN)
+        )
         nc.gpsimd.memset(pages[0][:], 0.0)
-        picked1 = first.tile([P, 2 * HALF], U8, name="picked1", align_bytes=64, offset=16 * WIDE + 4 * HALF)
-        next_dst = first.tile([P, HALF], U32, name="next_dst", align_bytes=64, offset=16 * WIDE + 6 * HALF)
-        pick_scales(0, 1, picked1[:, 0:HALF])
-        pick_scales(1, 1, picked1[:, HALF : 2 * HALF])
+
+        picked1_at = RAW_BYTES + WORD_BYTES
+        next_dst_at = picked1_at + PICKED_BYTES
+        picked1 = after_raw.tile([P, PICKED_BYTES], U8, name="picked1", align_bytes=ALIGN, offset=picked1_at)
+        next_dst = after_raw.tile([P, HALF], U32, name="next_dst", align_bytes=ALIGN, offset=next_dst_at)
+        pick_scales(1, picked1)
         spread_rows(1, picked1[:].bitcast(I32), 0)
-        pick_words(1, 1, next_dst)
-        part_words(0, 1, next_src)
-        part_words(1, 1, next_dst)
-        pages.append(first.tile([P, T], F32, name="page1", align_bytes=64, offset=16 * WIDE + 10 * HALF - 64))
+        pick_words(DST, 1, next_dst)
+        late_words = after_picks.tile([P, PASSES, HALF], U16, name="parted01", align_bytes=ALIGN, offset=late_words_at)
+        part_words(SRC, 1, next_src, late_words)
+        part_words(DST, 1, next_dst, own_words(DST, 1))
+        pages.append(
+            after_raw.tile([P, T], F32, name="page1", align_bytes=ALIGN, offset=next_dst_at + WORD_BYTES - ALIGN)
+        )
         nc.gpsimd.memset(pages[1][:], 0.0)
-        wc_w.append(keep.tile([P, PASSES, WIDE], I32, name="wc_w1", tag="src", align_bytes=64))
+        wc_w.append(keep.tile([P, PASSES, WIDE], I32, name="wc_w1", tag="src", align_bytes=ALIGN))
         load_wc(1)
 
         wgo_bank = psum.tile([P, HALF], F32, name="wgo_bank", tag="bank3")
@@ -185,7 +218,7 @@ def tile_list_rgg_relu_kernel(
                 for b in range(BLOCKS):
                     nc.tensor.matmul_mx(
                         out=ms_bank[:, b * P : (b + 1) * P],
-                        lhsT=parted[0, h][:, a, b * P : (b + 1) * P].bitcast(FP4X4),
+                        lhsT=parted[SRC, h][:, a, b * P : (b + 1) * P].bitcast(FP4X4),
                         lhsT_scale=scales_of(h, a, b * P, P),
                         rhs=wc_w[g][:, a, own : own + P].bitcast(FP8X4),
                         rhs_scale=scales_of(0, a, WC_AT + t * P, P),
@@ -216,8 +249,8 @@ def tile_list_rgg_relu_kernel(
                     out=za_bank[:],
                     lhsT=wb_w[:, a, t * P // 2 : (t + 1) * P // 2].bitcast(FP4X4),
                     lhsT_scale=scales_of(0, a, WB_AT + t * P, P),
-                    rhs=parted[0, h][:, a, :].bitcast(FP4X4),
-                    rhs_scale=scales_of(h, a, 0, HALF),
+                    rhs=parted[SRC, h][:, a, :].bitcast(FP4X4),
+                    rhs_scale=scales_of(h, a, SRC * HALF, HALF),
                     start=(a == PASSES - 1),
                     stop=False,
                 )
@@ -226,52 +259,57 @@ def tile_list_rgg_relu_kernel(
                     out=za_bank[:],
                     lhsT=wa_w[g][:, a * WIDE + own : a * WIDE + own + P].bitcast(FP8X4),
                     lhsT_scale=wa_s[g][:, a * WIDE + own : a * WIDE + own + P],
-                    rhs=parted[1, h][:, a, :].bitcast(FP4X4),
-                    rhs_scale=scales_of(h, a, HALF, HALF),
+                    rhs=parted[DST, h][:, a, :].bitcast(FP4X4),
+                    rhs_scale=scales_of(h, a, DST * HALF, HALF),
                     start=False,
                     stop=(a == PASSES - 1),
                 )
             nc.scalar.activation(gates[t][:, h * HALF : (h + 1) * HALF], za_bank[:], ACT.Sigmoid)
 
         def place(t, first, last):
-            page = pages[t % 3]
+            page = pages[t % PAGES]
             nc.vector.tensor_tensor(
                 page[:].indirect(dst_list[:, first // 16 : last // 16]), gates[t][:, first:last], messages[t][:, first:last], MULT
             )
             if last == J:
                 nc.sync.dma_start(out=out[t * P : (t + 1) * P, :], in_=page[:])
 
-        gates = [keep.tile([P, J], F32, name=f"gate{t}") for t in range(N // P)]
-        messages = [keep.tile([P, J], F32, name=f"message{t}") for t in range(N // P)]
+        gates = [keep.tile([P, J], F32, name=f"gate{t}") for t in range(ROW_TILES)]
+        messages = [keep.tile([P, J], F32, name=f"message{t}") for t in range(ROW_TILES)]
 
-        def late_columns(a):
-            rounded = keep.tile([P, WIDE, 4], BF16, name=f"rounded{a}", tag=f"stage{a}", align_bytes=64)
+        def late_pass(a):
+            rounded = keep.tile([P, WIDE, 4], BF16, name=f"rounded{a}", tag=f"stage{a}", align_bytes=ALIGN)
             round_wa(1, a, rounded[:])
             quantise_wa(1, a * WIDE, rounded[:])
 
-        units = [(0, 0), (1, 0), (0, 1), (1, 1), (2, 0), (3, 0), (2, 1), (3, 1)]
+        units = [(2 * g + s, h) for g in range(2) for h in range(2) for s in range(2)]
+        message_bank, gate_bank, turn_bank = "bank0", "bank1", "bank2"
         for u, (t, h) in enumerate(units):
+            if (t, h) == (0, 1):
+                message_bank, turn_bank = turn_bank, message_bank
+            if t * P >= WIDE:
+                gate_bank, turn_bank = turn_bank, gate_bank
+
             if u == 0:
-                positive = first.tile([P, HALF], F32, name="positive0", align_bytes=64, offset=16 * WIDE)
+                positive = after_raw.tile([P, HALF], F32, name="positive0", align_bytes=ALIGN, offset=RAW_BYTES)
             else:
                 positive = ring.tile([P, HALF], F32, name="positive")
-            if u in (1, 2):
-                weighted = keep.tile([P, HALF], F32, name=f"weighted{u}", tag=f"stage{u - 1}", align_bytes=64)
-            elif u == 3:
-                weighted = behind.tile([P, HALF], F32, name="weighted3", align_bytes=64, offset=0)
+            late_a = u - 1
+            if 0 <= late_a < PASSES:
+                weighted = keep.tile([P, HALF], F32, name=f"weighted{u}", tag=f"stage{late_a}", align_bytes=ALIGN)
+            elif late_a == PASSES:
+                weighted = after_words.tile([P, HALF], F32, name=f"weighted{u}", align_bytes=ALIGN, offset=0)
             else:
                 weighted = ring.tile([P, HALF], F32, name="weighted")
-            message_bank, gate_bank, turn_bank = ("012", "012", "210", "210", "201", "210", "201", "210")[u]
-            sum_message(t, h, f"bank{message_bank}", positive)
+
+            sum_message(t, h, message_bank, positive)
             weigh(h, positive, weighted)
-            sum_gate(t, h, f"bank{gate_bank}")
-            turn(t, h, f"bank{turn_bank}", weighted)
-            if t == 3:
-                place(t, h * SHORT, SHORT + h * (J - SHORT))
-            else:
-                place(t, h * HALF, (h + 1) * HALF)
-            if u in (1, 2):
-                late_columns(u - 1)
-            if u == 1:
-                pages.append(keep.tile([P, T], F32, name="page2", tag="stage0", align_bytes=64))
+            sum_gate(t, h, gate_bank)
+            turn(t, h, turn_bank, weighted)
+            split = SHORT if t == ROW_TILES - 1 else HALF
+            place(t, h * split, split + h * (J - split))
+            if 0 <= late_a < PASSES:
+                late_pass(late_a)
+            if late_a == 0:
+                pages.append(keep.tile([P, T], F32, name="page2", tag="stage0", align_bytes=ALIGN))
                 nc.gpsimd.memset(pages[2][:], 0.0)

@@ -19,27 +19,20 @@ MULT = mybir.AluOpType.mult
 
 P = 128
 PASSES = K // 512
-HALF = J // 2
-BLOCKS = HALF // P
 ROW_TILES = N // P
 SCALE_ROWS = K // 32
+TOP = P - SCALE_ROWS
 SRC, DST = 0, 1
-
-WB_AT = 2 * HALF
-WC_AT = WB_AT + N
-PLANE = WC_AT + N
-
+WB, WC = 0, 1
 WIDE = N // 2
-PAGES = 3
-SHORT = 3 * J // 8
-
+EARLY = J // 2
+GROUPS = ((0, EARLY), (EARLY, J))
+SPLITS = (2 * P, 3 * P, EARLY, EARLY)
+BANKS = 3
 ALIGN = 64
-WB_BYTES = PASSES * N * 2
-IDENT_BYTES = P * 4
-PAGE_BYTES = T * 4
-RAW_BYTES = 4 * WIDE * 4
-WORD_BYTES = HALF * 4
-PICKED_BYTES = 2 * HALF
+RAW_BYTES = 4 * N * 4
+RAW_AT = PASSES * (2 * J + 4 * WIDE + 2 * N)
+LATE_BYTES = (J - EARLY) * 4
 
 
 def tile_list_rgg_relu_kernel(
@@ -49,8 +42,6 @@ def tile_list_rgg_relu_kernel(
     with ExitStack() as ctx:
         keep = ctx.enter_context(tc.tile_pool(name="keep", bufs=1))
         ring = ctx.enter_context(tc.tile_pool(name="ring", bufs=2))
-        after_picks = ctx.enter_context(tc.tile_pool(name="after_picks", bufs=1))
-        after_words = ctx.enter_context(tc.tile_pool(name="after_words", bufs=1))
         after_raw = ctx.enter_context(tc.tile_pool(name="after_raw", bufs=1))
         psum = ctx.enter_context(tc.psum_pool(name="psum", bufs=1))
 
@@ -59,80 +50,91 @@ def tile_list_rgg_relu_kernel(
         lists = (src_list, dst_list)
         tab_w = keep.tile([P, T], I32, name="tab_w", align_bytes=ALIGN)
         tab_s = keep.tile([P, T // 4], I32, name="tab_s", align_bytes=ALIGN)
-        planes = {(0, 0): keep.tile([P, PLANE // 4], I32, name="plane00", align_bytes=ALIGN)}
-        compact = planes[0, 0]
-        wa_raw = {
-            (0, a): after_raw.tile([P, 4, WIDE], F32, name=f"wa_raw{a}", align_bytes=ALIGN, offset=a * RAW_BYTES)
-            for a in range(PASSES)
-        }
-        wc_w = [keep.tile([P, PASSES, WIDE], I32, name="wc_w0", align_bytes=ALIGN)]
+        staged = keep.tile([SCALE_ROWS, 2 * N // 4], I32, name="staged", align_bytes=ALIGN)
+        weight_planes = keep.tile([P, PASSES, 2 * N // 4], I32, name="weight_planes", align_bytes=ALIGN)
+        first_raw = keep.tile([P, 4, N], F32, name="first_raw", tag="raw", align_bytes=ALIGN)
+        wc_w = []
         wa_w = [keep.tile([P, PASSES * WIDE], U32, name=f"wa_w{g}", align_bytes=ALIGN) for g in range(2)]
         wa_s = [keep.tile([P, PASSES * WIDE], U8, name=f"wa_s{g}", align_bytes=ALIGN) for g in range(2)]
-        pages = []
-        wgo_rows = keep.tile([P, P], F32, name="wgo_rows")
+        rounded = [keep.tile([P, PASSES * WIDE, 4], BF16, name=f"rounded{g}", align_bytes=ALIGN) for g in range(2)]
+        pages = [keep.tile([P, T], F32, name=f"page{s}", align_bytes=ALIGN) for s in range(2)]
+        wgo_rows = after_raw.tile([P, P], F32, name="wgo_rows", align_bytes=ALIGN, offset=RAW_AT - 2 * P)
+        ident = keep.tile([P, P], F32, name="ident", align_bytes=ALIGN)
         warm = keep.tile([P, 1], F32, name="warm")
 
-        nc.vector.memset(tab_s[32:64, :], 0)
-        nc.vector.memset(tab_s[64:128, :], 0)
-        nc.vector.memset(compact[32:64, WB_AT // 4 :], 0)
-        nc.vector.memset(compact[64:128, WB_AT // 4 :], 0)
-        nc.gpsimd.memset(wgo_rows[:], 0.0)
-
         def scale_rows(scales):
-            return scales.rearrange("a q n -> (a q) n").bitcast(I32)
+            return scales.rearrange("a m n -> m a n").bitcast(I32)
 
-        nc.scalar.dma_start(out=tab_s[0:SCALE_ROWS, :], in_=scale_rows(tab_scales))
-        nc.scalar.activation(warm[:], wgo_rows[:, 0:1], ACT.Sigmoid)
+        nc.gpsimd.memset(wgo_rows[0:TOP, :], 0.0)
+        nc.gpsimd.memset(ident[:], 0.0)
+        nc.gpsimd.memset(tab_s[0:TOP, :], 0)
+        nc.gpsimd.memset(weight_planes[:], 0)
+        make_identity(nc, ident[:], nomemset=True)
+        nc.scalar.dma_start(out=tab_s[TOP:P, :], in_=scale_rows(tab_scales))
+        nc.scalar.activation(warm[0:64, :], wgo_rows[0:64, 0:1], ACT.Sigmoid)
+        for page in pages:
+            nc.gpsimd.memset(page[:], 0.0)
 
-        def load_wa(g, a):
-            rows = wa[512 * a : 512 * (a + 1), g * WIDE : (g + 1) * WIDE]
-            nc.sync.dma_start(out=wa_raw[g, a][:], in_=rows.rearrange("(p i) n -> p i n", i=4))
+        def wa_rows(a):
+            return wa[512 * a : 512 * (a + 1), :].rearrange("(p i) n -> p i n", i=4)
 
         def load_wc(g):
             cols = wc_words[:, :, g * WIDE : (g + 1) * WIDE, :]
-            nc.sync.dma_start(out=wc_w[g][:], in_=cols.rearrange("a p n i -> p a (n i)").bitcast(I32))
+            nc.sync.dma_start(out=wc_w[g][:, :, :], in_=cols.rearrange("a p n i -> p a (n i)").bitcast(I32))
 
         nc.sync.dma_start(src_list[:], offs)
         nc.sync.dma_start(dst_list[:], offs2)
+        for w, scales in ((WB, wb_scales), (WC, wc_scales)):
+            nc.sync.dma_start(out=staged[:, w * N // 4 : (w + 1) * N // 4], in_=scale_rows(scales))
+        nc.sync.dma_start(out=wgo_rows[TOP:P, :], in_=wgo[0:4, :].rearrange("o (c p) -> (o c) p", p=P))
+        nc.sync.dma_start(out=first_raw[:], in_=wa_rows(0))
         nc.sync.dma_start(out=tab_w[:], in_=tab_words[0].rearrange("p t b -> p (t b)").bitcast(I32))
-        nc.sync.dma_start(out=compact[0:SCALE_ROWS, WB_AT // 4 : WC_AT // 4], in_=scale_rows(wb_scales))
-        nc.sync.dma_start(out=compact[0:SCALE_ROWS, WC_AT // 4 : PLANE // 4], in_=scale_rows(wc_scales))
-        nc.gpsimd.dma_start(out=wgo_rows[0 : J // P, :], in_=wgo[0:1, :].rearrange("o (c p) -> (o c) p", p=P))
-        load_wa(0, 0)
+
+        def spread_rows(queue, planes, rows):
+            for q in range(4):
+                queue.dma_start(out=planes[32 * q : 32 * q + 4, :, :], in_=rows[8 * q : 8 * q + 8, :])
+
+        spread_rows(nc.sync, weight_planes, staged[:])
+        wgo_bank = psum.tile([P, 512], F32, name="wgo_bank")
+        nc.tensor.transpose(wgo_bank[:, 0:P], wgo_rows[:], ident[:])
+        held = after_raw.tile([P, RAW_AT // 4], I32, name="held", align_bytes=ALIGN, offset=0)
+        edge_planes = held[:, 0 : PASSES * 2 * J // 4].rearrange("p (a w) -> p a w", a=PASSES)
+        wc_w.append(held[:, PASSES * 2 * J // 4 : RAW_AT // 4 - N].rearrange("p (a w) -> p a w", a=PASSES))
+        wb_w = held[:, RAW_AT // 4 - N :].rearrange("p (a w) -> p a w", a=PASSES)
+        nc.gpsimd.memset(edge_planes, 0)
+        second_raw = after_raw.tile([P, 4, N], F32, name="second_raw", align_bytes=ALIGN, offset=RAW_AT)
+        nc.sync.dma_start(out=second_raw[:], in_=wa_rows(1))
         load_wc(0)
-        load_wa(0, 1)
+        nc.sync.dma_start(out=wb_w, in_=wb_words.rearrange("a p n -> p a n").bitcast(I32))
 
-        def half_list(e, h):
-            return lists[e][:, h * HALF // 16 : (h + 1) * HALF // 16]
+        picked = keep.tile([P, 2 * J], U8, name="picked", tag="picked", align_bytes=ALIGN)
+        for e in (SRC, DST):
+            nc.vector.tensor_copy(picked[:, e * J : (e + 1) * J], tab_s[:].bitcast(U8).indirect(lists[e][:]))
+        spread_rows(nc.sync, edge_planes, picked[TOP:P, :].bitcast(I32))
 
-        def pick_scales(h, picked):
-            for e in (SRC, DST):
-                nc.vector.tensor_copy(picked[:, e * HALF : (e + 1) * HALF], tab_s[:].bitcast(U8).indirect(half_list(e, h)))
+        wc_w.append(keep.tile([P, PASSES, WIDE], I32, name="wc_w1", tag="picked", align_bytes=ALIGN))
+        load_wc(1)
 
-        def spread_rows(h, rows, first_run):
-            for run in range(first_run, SCALE_ROWS // 4):
-                a, q = divmod(run, 4)
-                nc.sync.dma_start(out=planes[h, a][32 * q : 32 * q + 4, :], in_=rows[4 * run : 4 * run + 4, :])
+        def round_wa(g, a, raw):
+            nc.scalar.copy(
+                rounded[g][:, a * WIDE : (a + 1) * WIDE, :].rearrange("p (c u) i -> p c i u", u=4),
+                raw.rearrange("p i (c u) -> p c i u", u=4),
+            )
 
-        picked0 = after_picks.tile([P, PICKED_BYTES], U8, name="picked0", align_bytes=ALIGN, offset=WB_BYTES - ALIGN)
-        pick_scales(0, picked0)
-        nc.vector.tensor_copy(compact[:, 0 : WB_AT // 4], picked0[:].bitcast(I32))
-        plane_at = WB_BYTES + IDENT_BYTES
-        planes[0, 1] = after_picks.tile([P, PLANE // 4], I32, name="plane01", align_bytes=ALIGN, offset=plane_at)
-        nc.gpsimd.memset(planes[0, 1][:], 0)
-        spread_rows(0, compact[:], 1)
-        wb_w = after_picks.tile([P, PASSES, N // 2], I32, name="wb_w", align_bytes=ALIGN, offset=0)
-        nc.sync.dma_start(out=wb_w[:], in_=wb_words.rearrange("a p n -> p a n").bitcast(I32))
-        ident = after_picks.tile([P, P], F32, name="ident", align_bytes=ALIGN, offset=WB_BYTES)
-        make_identity(nc, ident[:])
+        def quantise_wa(g):
+            nc.vector.quantize_mx(
+                out=wa_w[g][:].bitcast(FP8X4), scales=wa_s[g][:], in_=rounded[g][:].rearrange("p n i -> p (n i)")
+            )
 
-        def scales_of(h, a, at, width):
-            return planes[h, a][:].bitcast(U8)[:, at : at + width]
+        for a, raw in enumerate((first_raw, second_raw)):
+            for g in range(2):
+                round_wa(g, a, raw[:, :, g * WIDE : (g + 1) * WIDE])
 
         parted = {}
 
         def pick_words(e, h, both):
-            nc.vector.tensor_copy(both[:], tab_w[:].bitcast(U32).indirect(half_list(e, h)))
+            first, last = GROUPS[h]
+            nc.vector.tensor_copy(both[:], tab_w[:].bitcast(U32).indirect(lists[e][:, first // 16 : last // 16]))
 
         def part_words(e, h, both, words):
             parted[e, h] = words
@@ -142,174 +144,117 @@ def tile_list_rgg_relu_kernel(
             )
 
         def own_words(e, h):
-            return keep.tile([P, PASSES, HALF], U16, name=f"parted{e}{h}", align_bytes=ALIGN)
+            first, last = GROUPS[h]
+            return keep.tile([P, PASSES, last - first], U16, name=f"parted{e}{h}", align_bytes=ALIGN)
 
-        def round_wa(g, a, rounded):
-            nc.scalar.copy(
-                rounded.rearrange("p (c u) i -> p c i u", u=4),
-                wa_raw[g, a][:].rearrange("p i (c u) -> p c i u", u=4),
-            )
+        early_src = keep.tile([P, EARLY], U32, name="early_src", tag="src", align_bytes=ALIGN)
+        early_dst = keep.tile([P, EARLY], U32, name="early_dst", align_bytes=ALIGN)
+        pick_words(SRC, 0, early_src)
+        pick_words(DST, 0, early_dst)
+        part_words(SRC, 0, early_src, own_words(SRC, 0))
+        part_words(DST, 0, early_dst, own_words(DST, 0))
+        late_src = keep.tile([P, J - EARLY], U32, name="late_src", tag="src", align_bytes=ALIGN)
+        pick_words(SRC, 1, late_src)
+        quantise_wa(0)
+        late_dst = after_raw.tile([P, J - EARLY], U32, name="late_dst", align_bytes=ALIGN, offset=RAW_AT + RAW_BYTES - LATE_BYTES)
+        pick_words(DST, 1, late_dst)
+        quantise_wa(1)
+        late_words = after_raw.tile([P, PASSES, J - EARLY], U16, name="parted01", align_bytes=ALIGN, offset=RAW_AT)
+        part_words(SRC, 1, late_src, late_words)
+        part_words(DST, 1, late_dst, own_words(DST, 1))
+        pages.append(after_raw.tile([P, T], F32, name="page2", align_bytes=ALIGN, offset=RAW_AT + RAW_BYTES - ALIGN))
+        nc.gpsimd.memset(pages[2][:], 0.0)
+        pages.append(keep.tile([P, T], F32, name="page3", tag="src", align_bytes=ALIGN))
+        nc.gpsimd.memset(pages[3][:], 0.0)
 
-        def quantise_wa(g, at, rounded):
-            cols = slice(at, at + rounded.shape[1])
-            nc.vector.quantize_mx(
-                out=wa_w[g][:, cols].bitcast(FP8X4), scales=wa_s[g][:, cols], in_=rounded.rearrange("p n i -> p (n i)")
-            )
+        wgo_cols = keep.tile([P, J // P], F32, name="wgo_cols", tag="raw", align_bytes=ALIGN)
+        nc.scalar.copy(wgo_cols[:], wgo_bank[:, TOP : TOP + J // P])
 
-        both_src = keep.tile([P, HALF], U32, name="both_src", tag="src", align_bytes=ALIGN)
-        both_dst = after_words.tile(
-            [P, HALF], U32, name="both_dst", align_bytes=ALIGN, offset=RAW_BYTES - WORD_BYTES // 2
-        )
-        pick_words(SRC, 0, both_src)
-        pick_words(DST, 0, both_dst)
-        part_words(SRC, 0, both_src, own_words(SRC, 0))
-        part_words(DST, 0, both_dst, own_words(DST, 0))
-        for a in range(PASSES):
-            wa_raw[1, a] = after_words.tile(
-                [P, 4, WIDE], F32, name=f"wa_late{a}", align_bytes=ALIGN, offset=(1 - a) * RAW_BYTES
-            )
-            load_wa(1, a)
-        next_src = keep.tile([P, HALF], U32, name="next_src", tag="src", align_bytes=ALIGN)
-        pick_words(SRC, 1, next_src)
+        def words_of(e, a, first, last):
+            h = int(first >= EARLY)
+            at = GROUPS[h][0]
+            return parted[e, h][:, a, first - at : last - at].bitcast(FP4X4)
 
-        early_at = plane_at + PLANE + PAGE_BYTES
-        early = after_picks.tile([P, PASSES * WIDE, 4], BF16, name="early", align_bytes=ALIGN, offset=early_at)
-        for a in range(PASSES):
-            round_wa(0, a, early[:, a * WIDE : (a + 1) * WIDE, :])
-        quantise_wa(0, 0, early[:])
-        late_words_at = early_at + WORD_BYTES // 2 + ALIGN
-        late_planes = after_picks.tile(
-            [P, PASSES * WB_AT // 4], I32, name="late_planes", align_bytes=ALIGN, offset=late_words_at + WORD_BYTES
-        )
-        nc.gpsimd.memset(late_planes[:], 0)
-        for a in range(PASSES):
-            planes[1, a] = late_planes[:, a * WB_AT // 4 : (a + 1) * WB_AT // 4]
-        pages.append(
-            after_picks.tile([P, T], F32, name="page0", align_bytes=ALIGN, offset=early_at - PAGE_BYTES + ALIGN)
-        )
-        nc.gpsimd.memset(pages[0][:], 0.0)
+        def edge_scales(e, a, first, last):
+            return edge_planes[:, a, :].bitcast(U8)[:, e * J + first : e * J + last]
 
-        picked1_at = RAW_BYTES + WORD_BYTES
-        next_dst_at = picked1_at + PICKED_BYTES
-        picked1 = after_raw.tile([P, PICKED_BYTES], U8, name="picked1", align_bytes=ALIGN, offset=picked1_at)
-        next_dst = after_raw.tile([P, HALF], U32, name="next_dst", align_bytes=ALIGN, offset=next_dst_at)
-        pick_scales(1, picked1)
-        spread_rows(1, picked1[:].bitcast(I32), 0)
-        pick_words(DST, 1, next_dst)
-        late_words = after_picks.tile([P, PASSES, HALF], U16, name="parted01", align_bytes=ALIGN, offset=late_words_at)
-        part_words(SRC, 1, next_src, late_words)
-        part_words(DST, 1, next_dst, own_words(DST, 1))
-        pages.append(
-            after_raw.tile([P, T], F32, name="page1", align_bytes=ALIGN, offset=next_dst_at + WORD_BYTES - ALIGN)
-        )
-        nc.gpsimd.memset(pages[1][:], 0.0)
-        wc_w.append(keep.tile([P, PASSES, WIDE], I32, name="wc_w1", tag="src", align_bytes=ALIGN))
-        load_wc(1)
+        def weight_scales(w, a, t):
+            return weight_planes[:, a, :].bitcast(U8)[:, w * N + t * P : w * N + (t + 1) * P]
 
-        wgo_bank = psum.tile([P, HALF], F32, name="wgo_bank", tag="bank3")
-        nc.tensor.transpose(wgo_bank[:, 0:P], wgo_rows[:], ident[:])
-        wgo_cols = keep.tile([P, J // P], F32, name="wgo_cols")
-        nc.scalar.copy(wgo_cols[:], wgo_bank[:, 0 : J // P])
+        gates = [keep.tile([P, J], F32, name=f"gate{t}") for t in range(ROW_TILES)]
+        messages = [keep.tile([P, J], F32, name=f"message{t}") for t in range(ROW_TILES)]
 
-        def sum_message(t, h, bank, positive):
+        taken = []
+
+        def next_bank():
+            taken.append(psum.tile([P, 512], F32, name=f"bank{len(taken)}", tag=f"bank{len(taken) % BANKS}"))
+            return taken[-1]
+
+        def unit(t, first, last):
+            width = last - first
+            blocks = range(width // P)
             g, own = divmod(t * P, WIDE)
-            ms_bank = psum.tile([P, HALF], F32, name="ms_bank", tag=bank)
-            for a in reversed(range(PASSES)):
-                for b in range(BLOCKS):
-                    nc.tensor.matmul_mx(
-                        out=ms_bank[:, b * P : (b + 1) * P],
-                        lhsT=parted[SRC, h][:, a, b * P : (b + 1) * P].bitcast(FP4X4),
-                        lhsT_scale=scales_of(h, a, b * P, P),
-                        rhs=wc_w[g][:, a, own : own + P].bitcast(FP8X4),
-                        rhs_scale=scales_of(0, a, WC_AT + t * P, P),
-                        start=(a == PASSES - 1 and b == 0),
-                        stop=(a == 0 and b == BLOCKS - 1),
-                    )
-            nc.scalar.activation(positive[:], ms_bank[:], ACT.Relu)
-
-        def weigh(h, positive, weighted):
-            for b in range(BLOCKS):
-                c = h * BLOCKS + b
+            ms_bank = next_bank()
+            steps = [(a, b) for a in range(PASSES) for b in blocks]
+            for s, (a, b) in enumerate(steps):
+                lo = first + b * P
+                nc.tensor.matmul_mx(
+                    out=ms_bank[:, b * P : (b + 1) * P],
+                    lhsT=words_of(SRC, a, lo, lo + P),
+                    lhsT_scale=edge_scales(SRC, a, lo, lo + P),
+                    rhs=wc_w[g][:, a, own : own + P].bitcast(FP8X4),
+                    rhs_scale=weight_scales(WC, a, t),
+                    start=(s == 0),
+                    stop=(s == len(steps) - 1),
+                )
+            positive = ring.tile([P, EARLY], F32, name="positive")
+            nc.scalar.activation(positive[:, 0:width], ms_bank[:, 0:width], ACT.Relu)
+            weighted = ring.tile([P, EARLY], F32, name="weighted")
+            for b in blocks:
+                c = first // P + b
                 nc.scalar.activation(
                     weighted[:, b * P : (b + 1) * P], positive[:, b * P : (b + 1) * P], ACT.Copy,
                     scale=wgo_cols[:, c : c + 1],
                 )
-
-        def turn(t, h, bank, weighted):
-            turned = psum.tile([P, HALF], F32, name="turned", tag=bank)
-            for b in range(BLOCKS):
+            za_bank = psum.tile([P, 512], F32, name="za_bank")
+            pieces = [(lo, min(lo + 2 * P, last)) for lo in range(first, last, 2 * P)]
+            steps = [(e, a, piece) for e in (SRC, DST) for a in range(PASSES) for piece in pieces]
+            for s, (e, a, (lo, hi)) in enumerate(steps):
+                if e == SRC:
+                    codes = wb_w[:, a, t * P // 2 : (t + 1) * P // 2].bitcast(FP4X4)
+                    scales = weight_scales(WB, a, t)
+                else:
+                    cols = slice(a * WIDE + own, a * WIDE + own + P)
+                    codes = wa_w[g][:, cols].bitcast(FP8X4)
+                    scales = wa_s[g][:, cols]
+                nc.tensor.matmul_mx(
+                    out=za_bank[:, lo - first : hi - first],
+                    lhsT=codes,
+                    lhsT_scale=scales,
+                    rhs=words_of(e, a, lo, hi),
+                    rhs_scale=edge_scales(e, a, lo, hi),
+                    start=(s == 0),
+                    stop=(s == len(steps) - 1),
+                )
+            nc.scalar.activation(gates[t][:, first:last], za_bank[:, 0:width], ACT.Sigmoid)
+            turned = next_bank()
+            for b in blocks:
                 nc.tensor.transpose(turned[:, b * P : (b + 1) * P], weighted[:, b * P : (b + 1) * P], ident[:])
-            nc.scalar.copy(messages[t][:, h * HALF : (h + 1) * HALF], turned[:])
-
-        def sum_gate(t, h, bank):
-            g, own = divmod(t * P, WIDE)
-            za_bank = psum.tile([P, HALF], F32, name="za_bank", tag=bank)
-            for a in reversed(range(PASSES)):
-                nc.tensor.matmul_mx(
-                    out=za_bank[:],
-                    lhsT=wb_w[:, a, t * P // 2 : (t + 1) * P // 2].bitcast(FP4X4),
-                    lhsT_scale=scales_of(0, a, WB_AT + t * P, P),
-                    rhs=parted[SRC, h][:, a, :].bitcast(FP4X4),
-                    rhs_scale=scales_of(h, a, SRC * HALF, HALF),
-                    start=(a == PASSES - 1),
-                    stop=False,
-                )
-            for a in range(PASSES):
-                nc.tensor.matmul_mx(
-                    out=za_bank[:],
-                    lhsT=wa_w[g][:, a * WIDE + own : a * WIDE + own + P].bitcast(FP8X4),
-                    lhsT_scale=wa_s[g][:, a * WIDE + own : a * WIDE + own + P],
-                    rhs=parted[DST, h][:, a, :].bitcast(FP4X4),
-                    rhs_scale=scales_of(h, a, DST * HALF, HALF),
-                    start=False,
-                    stop=(a == PASSES - 1),
-                )
-            nc.scalar.activation(gates[t][:, h * HALF : (h + 1) * HALF], za_bank[:], ACT.Sigmoid)
+            nc.scalar.copy(messages[t][:, first:last], turned[:, 0:width])
 
         def place(t, first, last):
-            page = pages[t % PAGES]
+            page = pages[t]
             nc.vector.tensor_tensor(
                 page[:].indirect(dst_list[:, first // 16 : last // 16]), gates[t][:, first:last], messages[t][:, first:last], MULT
             )
             if last == J:
                 nc.sync.dma_start(out=out[t * P : (t + 1) * P, :], in_=page[:])
 
-        gates = [keep.tile([P, J], F32, name=f"gate{t}") for t in range(ROW_TILES)]
-        messages = [keep.tile([P, J], F32, name=f"message{t}") for t in range(ROW_TILES)]
-
-        def late_pass(a):
-            rounded = keep.tile([P, WIDE, 4], BF16, name=f"rounded{a}", tag=f"stage{a}", align_bytes=ALIGN)
-            round_wa(1, a, rounded[:])
-            quantise_wa(1, a * WIDE, rounded[:])
-
-        units = [(2 * g + s, h) for g in range(2) for h in range(2) for s in range(2)]
-        message_bank, gate_bank, turn_bank = "bank0", "bank1", "bank2"
-        for u, (t, h) in enumerate(units):
-            if (t, h) == (0, 1):
-                message_bank, turn_bank = turn_bank, message_bank
-            if t * P >= WIDE:
-                gate_bank, turn_bank = turn_bank, gate_bank
-
-            if u == 0:
-                positive = after_raw.tile([P, HALF], F32, name="positive0", align_bytes=ALIGN, offset=RAW_BYTES)
-            else:
-                positive = ring.tile([P, HALF], F32, name="positive")
-            late_a = u - 1
-            if 0 <= late_a < PASSES:
-                weighted = keep.tile([P, HALF], F32, name=f"weighted{u}", tag=f"stage{late_a}", align_bytes=ALIGN)
-            elif late_a == PASSES:
-                weighted = after_words.tile([P, HALF], F32, name=f"weighted{u}", align_bytes=ALIGN, offset=0)
-            else:
-                weighted = ring.tile([P, HALF], F32, name="weighted")
-
-            sum_message(t, h, message_bank, positive)
-            weigh(h, positive, weighted)
-            sum_gate(t, h, gate_bank)
-            turn(t, h, turn_bank, weighted)
-            split = SHORT if t == ROW_TILES - 1 else HALF
-            place(t, h * split, split + h * (J - split))
-            if 0 <= late_a < PASSES:
-                late_pass(late_a)
-            if late_a == 0:
-                pages.append(keep.tile([P, T], F32, name="page2", tag="stage0", align_bytes=ALIGN))
-                nc.gpsimd.memset(pages[2][:], 0.0)
+        for t, split in enumerate(SPLITS):
+            unit(t, 0, split)
+            place(t, 0, split)
+        for t in (2, 3, 1, 0):
+            if SPLITS[t] < EARLY:
+                unit(t, SPLITS[t], EARLY)
+            unit(t, EARLY, J)
+            place(t, SPLITS[t], J)

@@ -19,20 +19,22 @@ MULT = mybir.AluOpType.mult
 
 P = 128
 PASSES = K // 512
+HALF = J // 2
+BLOCKS = HALF // P
 ROW_TILES = N // P
 SCALE_ROWS = K // 32
 TOP = P - SCALE_ROWS
 SRC, DST = 0, 1
-WB, WC = 0, 1
+
 WIDE = N // 2
-EARLY = J // 2
-GROUPS = ((0, EARLY), (EARLY, J))
-SPLITS = (2 * P, 3 * P, EARLY, EARLY)
-BANKS = 3
+PAGES = 3
+SHORT = 3 * J // 8
+
 ALIGN = 64
-RAW_BYTES = 4 * N * 4
-RAW_AT = PASSES * (2 * J + 4 * WIDE + 2 * N)
-LATE_BYTES = (J - EARLY) * 4
+PAGE_BYTES = T * 4
+RAW_BYTES = 4 * WIDE * 4
+WORD_BYTES = HALF * 4
+PICKED_BYTES = 2 * HALF
 
 
 def tile_list_rgg_relu_kernel(
@@ -42,6 +44,8 @@ def tile_list_rgg_relu_kernel(
     with ExitStack() as ctx:
         keep = ctx.enter_context(tc.tile_pool(name="keep", bufs=1))
         ring = ctx.enter_context(tc.tile_pool(name="ring", bufs=2))
+        after_picks = ctx.enter_context(tc.tile_pool(name="after_picks", bufs=1))
+        after_words = ctx.enter_context(tc.tile_pool(name="after_words", bufs=1))
         after_raw = ctx.enter_context(tc.tile_pool(name="after_raw", bufs=1))
         psum = ctx.enter_context(tc.psum_pool(name="psum", bufs=1))
 
@@ -52,31 +56,33 @@ def tile_list_rgg_relu_kernel(
         tab_s = keep.tile([P, T // 4], I32, name="tab_s", align_bytes=ALIGN)
         staged = keep.tile([SCALE_ROWS, 2 * N // 4], I32, name="staged", align_bytes=ALIGN)
         weight_planes = keep.tile([P, PASSES, 2 * N // 4], I32, name="weight_planes", align_bytes=ALIGN)
-        first_raw = keep.tile([P, 4, N], F32, name="first_raw", tag="raw", align_bytes=ALIGN)
+        planes = [keep.tile([P, PASSES, 2 * HALF // 4], I32, name="planes0", align_bytes=ALIGN)]
+        wa_raw = {(0, 0): keep.tile([P, 4, WIDE], F32, name="wa_raw0", align_bytes=ALIGN)}
         wc_w = []
+        wgo_row = after_raw.tile([J // P, P], F32, name="wgo_row", align_bytes=ALIGN, offset=RAW_BYTES - 2 * P)
+        ident = keep.tile([P, P], F32, name="ident", align_bytes=ALIGN)
         wa_w = [keep.tile([P, PASSES * WIDE], U32, name=f"wa_w{g}", align_bytes=ALIGN) for g in range(2)]
         wa_s = [keep.tile([P, PASSES * WIDE], U8, name=f"wa_s{g}", align_bytes=ALIGN) for g in range(2)]
-        rounded = [keep.tile([P, PASSES * WIDE, 4], BF16, name=f"rounded{g}", align_bytes=ALIGN) for g in range(2)]
-        pages = [keep.tile([P, T], F32, name=f"page{s}", align_bytes=ALIGN) for s in range(2)]
-        wgo_rows = after_raw.tile([P, P], F32, name="wgo_rows", align_bytes=ALIGN, offset=RAW_AT - 2 * P)
-        ident = keep.tile([P, P], F32, name="ident", align_bytes=ALIGN)
+        pages = []
+        wgo_rows = keep.tile([P, P], F32, name="wgo_rows")
         warm = keep.tile([P, 1], F32, name="warm")
+
+        nc.gpsimd.memset(wgo_rows[:], 0.0)
+        nc.gpsimd.memset(ident[:], 0.0)
+        nc.gpsimd.memset(tab_s[0:TOP, :], 0)
+        nc.gpsimd.memset(weight_planes[:], 0)
+        nc.gpsimd.memset(planes[0][:], 0)
+        make_identity(nc, ident[:], nomemset=True)
 
         def scale_rows(scales):
             return scales.rearrange("a m n -> m a n").bitcast(I32)
 
-        nc.gpsimd.memset(wgo_rows[0:TOP, :], 0.0)
-        nc.gpsimd.memset(ident[:], 0.0)
-        nc.gpsimd.memset(tab_s[0:TOP, :], 0)
-        nc.gpsimd.memset(weight_planes[:], 0)
-        make_identity(nc, ident[:], nomemset=True)
         nc.scalar.dma_start(out=tab_s[TOP:P, :], in_=scale_rows(tab_scales))
-        nc.scalar.activation(warm[0:64, :], wgo_rows[0:64, 0:1], ACT.Sigmoid)
-        for page in pages:
-            nc.gpsimd.memset(page[:], 0.0)
+        nc.scalar.activation(warm[:], wgo_rows[:, 0:1], ACT.Sigmoid)
 
-        def wa_rows(a):
-            return wa[512 * a : 512 * (a + 1), :].rearrange("(p i) n -> p i n", i=4)
+        def load_wa(g, a):
+            rows = wa[512 * a : 512 * (a + 1), g * WIDE : (g + 1) * WIDE]
+            nc.sync.dma_start(out=wa_raw[g, a][:], in_=rows.rearrange("(p i) n -> p i n", i=4))
 
         def load_wc(g):
             cols = wc_words[:, :, g * WIDE : (g + 1) * WIDE, :]
@@ -84,57 +90,47 @@ def tile_list_rgg_relu_kernel(
 
         nc.sync.dma_start(src_list[:], offs)
         nc.sync.dma_start(dst_list[:], offs2)
-        for w, scales in ((WB, wb_scales), (WC, wc_scales)):
+        for w, scales in enumerate((wb_scales, wc_scales)):
             nc.sync.dma_start(out=staged[:, w * N // 4 : (w + 1) * N // 4], in_=scale_rows(scales))
-        nc.sync.dma_start(out=wgo_rows[TOP:P, :], in_=wgo[0:4, :].rearrange("o (c p) -> (o c) p", p=P))
-        nc.sync.dma_start(out=first_raw[:], in_=wa_rows(0))
+        nc.sync.dma_start(out=wgo_row[:], in_=wgo[0:1, :].rearrange("o (c p) -> (o c) p", p=P))
         nc.sync.dma_start(out=tab_w[:], in_=tab_words[0].rearrange("p t b -> p (t b)").bitcast(I32))
+        load_wa(0, 0)
 
-        def spread_rows(queue, planes, rows):
+        def spread_rows(plane_pair, rows):
             for q in range(4):
-                queue.dma_start(out=planes[32 * q : 32 * q + 4, :, :], in_=rows[8 * q : 8 * q + 8, :])
+                nc.sync.dma_start(out=plane_pair[32 * q : 32 * q + 4, :, :], in_=rows[8 * q : 8 * q + 8, :])
 
-        spread_rows(nc.sync, weight_planes, staged[:])
-        wgo_bank = psum.tile([P, 512], F32, name="wgo_bank")
-        nc.tensor.transpose(wgo_bank[:, 0:P], wgo_rows[:], ident[:])
-        held = after_raw.tile([P, RAW_AT // 4], I32, name="held", align_bytes=ALIGN, offset=0)
-        edge_planes = held[:, 0 : PASSES * 2 * J // 4].rearrange("p (a w) -> p a w", a=PASSES)
-        wc_w.append(held[:, PASSES * 2 * J // 4 : RAW_AT // 4 - N].rearrange("p (a w) -> p a w", a=PASSES))
-        wb_w = held[:, RAW_AT // 4 - N :].rearrange("p (a w) -> p a w", a=PASSES)
-        nc.gpsimd.memset(edge_planes, 0)
-        second_raw = after_raw.tile([P, 4, N], F32, name="second_raw", align_bytes=ALIGN, offset=RAW_AT)
-        nc.sync.dma_start(out=second_raw[:], in_=wa_rows(1))
+        spread_rows(weight_planes, staged[:])
+        nc.scalar.copy(wgo_rows[0 : J // P, :], wgo_row[:])
+        held = after_raw.tile([P, RAW_BYTES // 4], I32, name="held", align_bytes=ALIGN, offset=0)
+        wc_w.append(held[:, 0 : PASSES * WIDE].rearrange("p (a w) -> p a w", a=PASSES))
+        wb_w = held[:, PASSES * WIDE :].rearrange("p (a w) -> p a w", a=PASSES)
+        wa_raw[0, 1] = after_raw.tile([P, 4, WIDE], F32, name="wa_raw1", align_bytes=ALIGN, offset=RAW_BYTES)
+        load_wa(0, 1)
         load_wc(0)
         nc.sync.dma_start(out=wb_w, in_=wb_words.rearrange("a p n -> p a n").bitcast(I32))
 
-        picked = keep.tile([P, 2 * J], U8, name="picked", tag="picked", align_bytes=ALIGN)
-        for e in (SRC, DST):
-            nc.vector.tensor_copy(picked[:, e * J : (e + 1) * J], tab_s[:].bitcast(U8).indirect(lists[e][:]))
-        spread_rows(nc.sync, edge_planes, picked[TOP:P, :].bitcast(I32))
+        def half_list(e, h):
+            return lists[e][:, h * HALF // 16 : (h + 1) * HALF // 16]
 
-        wc_w.append(keep.tile([P, PASSES, WIDE], I32, name="wc_w1", tag="picked", align_bytes=ALIGN))
-        load_wc(1)
+        def pick_scales(h, picked):
+            for e in (SRC, DST):
+                nc.vector.tensor_copy(picked[:, e * HALF : (e + 1) * HALF], tab_s[:].bitcast(U8).indirect(half_list(e, h)))
 
-        def round_wa(g, a, raw):
-            nc.scalar.copy(
-                rounded[g][:, a * WIDE : (a + 1) * WIDE, :].rearrange("p (c u) i -> p c i u", u=4),
-                raw.rearrange("p i (c u) -> p c i u", u=4),
-            )
+        picked0 = keep.tile([P, PICKED_BYTES], U8, name="picked0", align_bytes=ALIGN)
+        pick_scales(0, picked0)
+        spread_rows(planes[0], picked0[TOP:P, :].bitcast(I32))
 
-        def quantise_wa(g):
-            nc.vector.quantize_mx(
-                out=wa_w[g][:].bitcast(FP8X4), scales=wa_s[g][:], in_=rounded[g][:].rearrange("p n i -> p (n i)")
-            )
+        def scales_of(h, a, at, width):
+            return planes[h][:, a, :].bitcast(U8)[:, at : at + width]
 
-        for a, raw in enumerate((first_raw, second_raw)):
-            for g in range(2):
-                round_wa(g, a, raw[:, :, g * WIDE : (g + 1) * WIDE])
+        def weight_scales(a, at, width):
+            return weight_planes[:, a, :].bitcast(U8)[:, at : at + width]
 
         parted = {}
 
         def pick_words(e, h, both):
-            first, last = GROUPS[h]
-            nc.vector.tensor_copy(both[:], tab_w[:].bitcast(U32).indirect(lists[e][:, first // 16 : last // 16]))
+            nc.vector.tensor_copy(both[:], tab_w[:].bitcast(U32).indirect(half_list(e, h)))
 
         def part_words(e, h, both, words):
             parted[e, h] = words
@@ -144,117 +140,173 @@ def tile_list_rgg_relu_kernel(
             )
 
         def own_words(e, h):
-            first, last = GROUPS[h]
-            return keep.tile([P, PASSES, last - first], U16, name=f"parted{e}{h}", align_bytes=ALIGN)
+            return keep.tile([P, PASSES, HALF], U16, name=f"parted{e}{h}", align_bytes=ALIGN)
 
-        early_src = keep.tile([P, EARLY], U32, name="early_src", tag="src", align_bytes=ALIGN)
-        early_dst = keep.tile([P, EARLY], U32, name="early_dst", align_bytes=ALIGN)
-        pick_words(SRC, 0, early_src)
-        pick_words(DST, 0, early_dst)
-        part_words(SRC, 0, early_src, own_words(SRC, 0))
-        part_words(DST, 0, early_dst, own_words(DST, 0))
-        late_src = keep.tile([P, J - EARLY], U32, name="late_src", tag="src", align_bytes=ALIGN)
-        pick_words(SRC, 1, late_src)
-        quantise_wa(0)
-        late_dst = after_raw.tile([P, J - EARLY], U32, name="late_dst", align_bytes=ALIGN, offset=RAW_AT + RAW_BYTES - LATE_BYTES)
-        pick_words(DST, 1, late_dst)
-        quantise_wa(1)
-        late_words = after_raw.tile([P, PASSES, J - EARLY], U16, name="parted01", align_bytes=ALIGN, offset=RAW_AT)
-        part_words(SRC, 1, late_src, late_words)
-        part_words(DST, 1, late_dst, own_words(DST, 1))
-        pages.append(after_raw.tile([P, T], F32, name="page2", align_bytes=ALIGN, offset=RAW_AT + RAW_BYTES - ALIGN))
-        nc.gpsimd.memset(pages[2][:], 0.0)
-        pages.append(keep.tile([P, T], F32, name="page3", tag="src", align_bytes=ALIGN))
-        nc.gpsimd.memset(pages[3][:], 0.0)
+        def round_wa(g, a, rounded):
+            nc.scalar.copy(
+                rounded.rearrange("p (c u) i -> p c i u", u=4),
+                wa_raw[g, a][:].rearrange("p i (c u) -> p c i u", u=4),
+            )
 
-        wgo_cols = keep.tile([P, J // P], F32, name="wgo_cols", tag="raw", align_bytes=ALIGN)
-        nc.scalar.copy(wgo_cols[:], wgo_bank[:, TOP : TOP + J // P])
+        def quantise_wa(g, at, rounded):
+            cols = slice(at, at + rounded.shape[1])
+            nc.vector.quantize_mx(
+                out=wa_w[g][:, cols].bitcast(FP8X4), scales=wa_s[g][:, cols], in_=rounded.rearrange("p n i -> p (n i)")
+            )
 
-        def words_of(e, a, first, last):
-            h = int(first >= EARLY)
-            at = GROUPS[h][0]
-            return parted[e, h][:, a, first - at : last - at].bitcast(FP4X4)
+        both_src = keep.tile([P, HALF], U32, name="both_src", tag="src", align_bytes=ALIGN)
+        both_dst = after_words.tile(
+            [P, HALF], U32, name="both_dst", align_bytes=ALIGN, offset=RAW_BYTES - WORD_BYTES // 2
+        )
+        pick_words(SRC, 0, both_src)
+        pick_words(DST, 0, both_dst)
+        part_words(SRC, 0, both_src, own_words(SRC, 0))
+        part_words(DST, 0, both_dst, own_words(DST, 0))
+        for a in range(PASSES):
+            wa_raw[1, a] = after_words.tile(
+                [P, 4, WIDE], F32, name=f"wa_late{a}", align_bytes=ALIGN, offset=(1 - a) * RAW_BYTES
+            )
+            load_wa(1, a)
+        next_src = keep.tile([P, HALF], U32, name="next_src", tag="src", align_bytes=ALIGN)
+        pick_words(SRC, 1, next_src)
 
-        def edge_scales(e, a, first, last):
-            return edge_planes[:, a, :].bitcast(U8)[:, e * J + first : e * J + last]
+        early_at = PAGE_BYTES
+        early = after_picks.tile([P, PASSES * WIDE, 4], BF16, name="early", align_bytes=ALIGN, offset=early_at)
+        for a in range(PASSES):
+            round_wa(0, a, early[:, a * WIDE : (a + 1) * WIDE, :])
+        quantise_wa(0, 0, early[:])
+        late_words_at = early_at + WORD_BYTES // 2 + ALIGN
+        late_planes = after_picks.tile(
+            [P, PASSES, 2 * HALF // 4], I32, name="late_planes", align_bytes=ALIGN, offset=late_words_at + WORD_BYTES
+        )
+        nc.gpsimd.memset(late_planes[:], 0)
+        planes.append(late_planes)
+        pages.append(
+            after_picks.tile([P, T], F32, name="page0", align_bytes=ALIGN, offset=early_at - PAGE_BYTES + ALIGN)
+        )
+        nc.gpsimd.memset(pages[0][:], 0.0)
 
-        def weight_scales(w, a, t):
-            return weight_planes[:, a, :].bitcast(U8)[:, w * N + t * P : w * N + (t + 1) * P]
+        picked1_at = RAW_BYTES + WORD_BYTES
+        next_dst_at = picked1_at + PICKED_BYTES
+        picked1 = after_raw.tile([P, PICKED_BYTES], U8, name="picked1", align_bytes=ALIGN, offset=picked1_at)
+        next_dst = after_raw.tile([P, HALF], U32, name="next_dst", align_bytes=ALIGN, offset=next_dst_at)
+        pick_scales(1, picked1)
+        spread_rows(planes[1], picked1[TOP:P, :].bitcast(I32))
+        pick_words(DST, 1, next_dst)
+        late_words = after_picks.tile([P, PASSES, HALF], U16, name="parted01", align_bytes=ALIGN, offset=late_words_at)
+        part_words(SRC, 1, next_src, late_words)
+        part_words(DST, 1, next_dst, own_words(DST, 1))
+        pages.append(
+            after_raw.tile([P, T], F32, name="page1", align_bytes=ALIGN, offset=next_dst_at + WORD_BYTES - ALIGN)
+        )
+        nc.gpsimd.memset(pages[1][:], 0.0)
+        wc_w.append(keep.tile([P, PASSES, WIDE], I32, name="wc_w1", tag="src", align_bytes=ALIGN))
+        load_wc(1)
 
-        gates = [keep.tile([P, J], F32, name=f"gate{t}") for t in range(ROW_TILES)]
-        messages = [keep.tile([P, J], F32, name=f"message{t}") for t in range(ROW_TILES)]
+        wgo_bank = psum.tile([P, HALF], F32, name="wgo_bank", tag="bank3")
+        nc.tensor.transpose(wgo_bank[:, 0:P], wgo_rows[:], ident[:])
+        wgo_cols = keep.tile([P, J // P], F32, name="wgo_cols")
+        nc.scalar.copy(wgo_cols[:], wgo_bank[:, 0 : J // P])
 
-        taken = []
-
-        def next_bank():
-            taken.append(psum.tile([P, 512], F32, name=f"bank{len(taken)}", tag=f"bank{len(taken) % BANKS}"))
-            return taken[-1]
-
-        def unit(t, first, last):
-            width = last - first
-            blocks = range(width // P)
+        def sum_message(t, h, bank, positive):
             g, own = divmod(t * P, WIDE)
-            ms_bank = next_bank()
-            steps = [(a, b) for a in range(PASSES) for b in blocks]
-            for s, (a, b) in enumerate(steps):
-                lo = first + b * P
-                nc.tensor.matmul_mx(
-                    out=ms_bank[:, b * P : (b + 1) * P],
-                    lhsT=words_of(SRC, a, lo, lo + P),
-                    lhsT_scale=edge_scales(SRC, a, lo, lo + P),
-                    rhs=wc_w[g][:, a, own : own + P].bitcast(FP8X4),
-                    rhs_scale=weight_scales(WC, a, t),
-                    start=(s == 0),
-                    stop=(s == len(steps) - 1),
-                )
-            positive = ring.tile([P, EARLY], F32, name="positive")
-            nc.scalar.activation(positive[:, 0:width], ms_bank[:, 0:width], ACT.Relu)
-            weighted = ring.tile([P, EARLY], F32, name="weighted")
-            for b in blocks:
-                c = first // P + b
+            ms_bank = psum.tile([P, HALF], F32, name="ms_bank", tag=bank)
+            for a in reversed(range(PASSES)):
+                for b in range(BLOCKS):
+                    nc.tensor.matmul_mx(
+                        out=ms_bank[:, b * P : (b + 1) * P],
+                        lhsT=parted[SRC, h][:, a, b * P : (b + 1) * P].bitcast(FP4X4),
+                        lhsT_scale=scales_of(h, a, b * P, P),
+                        rhs=wc_w[g][:, a, own : own + P].bitcast(FP8X4),
+                        rhs_scale=weight_scales(a, N + t * P, P),
+                        start=(a == PASSES - 1 and b == 0),
+                        stop=(a == 0 and b == BLOCKS - 1),
+                    )
+            nc.scalar.activation(positive[:], ms_bank[:], ACT.Relu)
+
+        def weigh(h, positive, weighted):
+            for b in range(BLOCKS):
+                c = h * BLOCKS + b
                 nc.scalar.activation(
                     weighted[:, b * P : (b + 1) * P], positive[:, b * P : (b + 1) * P], ACT.Copy,
                     scale=wgo_cols[:, c : c + 1],
                 )
-            za_bank = psum.tile([P, 512], F32, name="za_bank")
-            pieces = [(lo, min(lo + 2 * P, last)) for lo in range(first, last, 2 * P)]
-            steps = [(e, a, piece) for e in (SRC, DST) for a in range(PASSES) for piece in pieces]
-            for s, (e, a, (lo, hi)) in enumerate(steps):
-                if e == SRC:
-                    codes = wb_w[:, a, t * P // 2 : (t + 1) * P // 2].bitcast(FP4X4)
-                    scales = weight_scales(WB, a, t)
-                else:
-                    cols = slice(a * WIDE + own, a * WIDE + own + P)
-                    codes = wa_w[g][:, cols].bitcast(FP8X4)
-                    scales = wa_s[g][:, cols]
-                nc.tensor.matmul_mx(
-                    out=za_bank[:, lo - first : hi - first],
-                    lhsT=codes,
-                    lhsT_scale=scales,
-                    rhs=words_of(e, a, lo, hi),
-                    rhs_scale=edge_scales(e, a, lo, hi),
-                    start=(s == 0),
-                    stop=(s == len(steps) - 1),
-                )
-            nc.scalar.activation(gates[t][:, first:last], za_bank[:, 0:width], ACT.Sigmoid)
-            turned = next_bank()
-            for b in blocks:
+
+        def turn(t, h, bank, weighted):
+            turned = psum.tile([P, HALF], F32, name="turned", tag=bank)
+            for b in range(BLOCKS):
                 nc.tensor.transpose(turned[:, b * P : (b + 1) * P], weighted[:, b * P : (b + 1) * P], ident[:])
-            nc.scalar.copy(messages[t][:, first:last], turned[:, 0:width])
+            nc.scalar.copy(messages[t][:, h * HALF : (h + 1) * HALF], turned[:])
+
+        def sum_gate(t, h, bank):
+            g, own = divmod(t * P, WIDE)
+            za_bank = psum.tile([P, HALF], F32, name="za_bank", tag=bank)
+            for a in reversed(range(PASSES)):
+                nc.tensor.matmul_mx(
+                    out=za_bank[:],
+                    lhsT=wb_w[:, a, t * P // 2 : (t + 1) * P // 2].bitcast(FP4X4),
+                    lhsT_scale=weight_scales(a, t * P, P),
+                    rhs=parted[SRC, h][:, a, :].bitcast(FP4X4),
+                    rhs_scale=scales_of(h, a, SRC * HALF, HALF),
+                    start=(a == PASSES - 1),
+                    stop=False,
+                )
+            for a in range(PASSES):
+                nc.tensor.matmul_mx(
+                    out=za_bank[:],
+                    lhsT=wa_w[g][:, a * WIDE + own : a * WIDE + own + P].bitcast(FP8X4),
+                    lhsT_scale=wa_s[g][:, a * WIDE + own : a * WIDE + own + P],
+                    rhs=parted[DST, h][:, a, :].bitcast(FP4X4),
+                    rhs_scale=scales_of(h, a, DST * HALF, HALF),
+                    start=False,
+                    stop=(a == PASSES - 1),
+                )
+            nc.scalar.activation(gates[t][:, h * HALF : (h + 1) * HALF], za_bank[:], ACT.Sigmoid)
 
         def place(t, first, last):
-            page = pages[t]
+            page = pages[t % PAGES]
             nc.vector.tensor_tensor(
                 page[:].indirect(dst_list[:, first // 16 : last // 16]), gates[t][:, first:last], messages[t][:, first:last], MULT
             )
             if last == J:
                 nc.sync.dma_start(out=out[t * P : (t + 1) * P, :], in_=page[:])
 
-        for t, split in enumerate(SPLITS):
-            unit(t, 0, split)
-            place(t, 0, split)
-        for t in (2, 3, 1, 0):
-            if SPLITS[t] < EARLY:
-                unit(t, SPLITS[t], EARLY)
-            unit(t, EARLY, J)
-            place(t, SPLITS[t], J)
+        gates = [keep.tile([P, J], F32, name=f"gate{t}") for t in range(ROW_TILES)]
+        messages = [keep.tile([P, J], F32, name=f"message{t}") for t in range(ROW_TILES)]
+
+        def late_pass(a):
+            rounded = keep.tile([P, WIDE, 4], BF16, name=f"rounded{a}", tag=f"stage{a}", align_bytes=ALIGN)
+            round_wa(1, a, rounded[:])
+            quantise_wa(1, a * WIDE, rounded[:])
+
+        units = [(2 * g + s, h) for g in range(2) for h in range(2) for s in range(2)]
+        message_bank, gate_bank, turn_bank = "bank0", "bank1", "bank2"
+        for u, (t, h) in enumerate(units):
+            if (t, h) == (0, 1):
+                message_bank, turn_bank = turn_bank, message_bank
+            if t * P >= WIDE:
+                gate_bank, turn_bank = turn_bank, gate_bank
+
+            if u == 0:
+                positive = after_raw.tile([P, HALF], F32, name="positive0", align_bytes=ALIGN, offset=RAW_BYTES)
+            else:
+                positive = ring.tile([P, HALF], F32, name="positive")
+            late_a = u - 1
+            if 0 <= late_a < PASSES:
+                weighted = keep.tile([P, HALF], F32, name=f"weighted{u}", tag=f"stage{late_a}", align_bytes=ALIGN)
+            elif late_a == PASSES:
+                weighted = after_words.tile([P, HALF], F32, name=f"weighted{u}", align_bytes=ALIGN, offset=0)
+            else:
+                weighted = ring.tile([P, HALF], F32, name="weighted")
+
+            sum_message(t, h, message_bank, positive)
+            weigh(h, positive, weighted)
+            sum_gate(t, h, gate_bank)
+            turn(t, h, turn_bank, weighted)
+            split = SHORT if t == ROW_TILES - 1 else HALF
+            place(t, h * split, split + h * (J - split))
+            if 0 <= late_a < PASSES:
+                late_pass(late_a)
+            if late_a == 0:
+                pages.append(keep.tile([P, T], F32, name="page2", tag="stage0", align_bytes=ALIGN))
+                nc.gpsimd.memset(pages[2][:], 0.0)

@@ -27,11 +27,14 @@ TOP = P - SCALE_ROWS
 SRC, DST = 0, 1
 
 WIDE = N // 2
+RANGES = ((0, P), (P, WIDE), (WIDE, N))
+WC_RANGES = ((0, P), (P, N))
 PAGES = 3
 SHORT = 3 * J // 8
 
 ALIGN = 64
 PAGE_BYTES = T * 4
+HELD_BYTES = PASSES * (2 * N + 4 * (N - P))
 RAW_BYTES = 4 * WIDE * 4
 WORD_BYTES = HALF * 4
 PICKED_BYTES = 2 * HALF
@@ -45,6 +48,7 @@ def tile_list_rgg_relu_kernel(
         keep = ctx.enter_context(tc.tile_pool(name="keep", bufs=1))
         ring = ctx.enter_context(tc.tile_pool(name="ring", bufs=2))
         after_picks = ctx.enter_context(tc.tile_pool(name="after_picks", bufs=1))
+        after_src = ctx.enter_context(tc.tile_pool(name="after_src", bufs=1))
         after_words = ctx.enter_context(tc.tile_pool(name="after_words", bufs=1))
         after_raw = ctx.enter_context(tc.tile_pool(name="after_raw", bufs=1))
         psum = ctx.enter_context(tc.psum_pool(name="psum", bufs=1))
@@ -54,15 +58,17 @@ def tile_list_rgg_relu_kernel(
         lists = (src_list, dst_list)
         tab_w = keep.tile([P, T], I32, name="tab_w", align_bytes=ALIGN)
         tab_s = keep.tile([P, T // 4], I32, name="tab_s", align_bytes=ALIGN)
-        staged = keep.tile([SCALE_ROWS, 2 * N // 4], I32, name="staged", align_bytes=ALIGN)
+        staged = keep.tile([SCALE_ROWS // PASSES, PASSES, 2 * N // 4], I32, name="staged", align_bytes=ALIGN)
         weight_planes = keep.tile([P, PASSES, 2 * N // 4], I32, name="weight_planes", align_bytes=ALIGN)
         planes = [keep.tile([P, PASSES, 2 * HALF // 4], I32, name="planes0", align_bytes=ALIGN)]
-        wa_raw = {(0, 0): keep.tile([P, 4, WIDE], F32, name="wa_raw0", align_bytes=ALIGN)}
-        wc_w = []
-        wgo_row = after_raw.tile([J // P, P], F32, name="wgo_row", align_bytes=ALIGN, offset=RAW_BYTES - 2 * P)
+        wa_raw = {
+            (0, 0): after_words.tile([P, 4, P], F32, name="wa_raw0", align_bytes=ALIGN, offset=HELD_BYTES - WORD_BYTES // 2),
+            (0, 1): after_raw.tile([P, 4, P], F32, name="wa_raw1", align_bytes=ALIGN, offset=WORD_BYTES - ALIGN),
+        }
+        wc_w = [keep.tile([P, PASSES, P], I32, name="wc_w0", align_bytes=ALIGN)]
         ident = keep.tile([P, P], F32, name="ident", align_bytes=ALIGN)
-        wa_w = [keep.tile([P, PASSES * WIDE], U32, name=f"wa_w{g}", align_bytes=ALIGN) for g in range(2)]
-        wa_s = [keep.tile([P, PASSES * WIDE], U8, name=f"wa_s{g}", align_bytes=ALIGN) for g in range(2)]
+        wa_w = [keep.tile([P, PASSES * (hi - lo)], U32, name=f"wa_w{lo}", align_bytes=ALIGN) for lo, hi in RANGES]
+        wa_s = [keep.tile([P, PASSES * (hi - lo)], U8, name=f"wa_s{lo}", align_bytes=ALIGN) for lo, hi in RANGES]
         pages = []
         wgo_rows = keep.tile([P, P], F32, name="wgo_rows")
         warm = keep.tile([P, 1], F32, name="warm")
@@ -73,42 +79,39 @@ def tile_list_rgg_relu_kernel(
         nc.gpsimd.memset(weight_planes[:], 0)
         nc.gpsimd.memset(planes[0][:], 0)
         make_identity(nc, ident[:], nomemset=True)
+        nc.gpsimd.dma_start(out=wgo_rows[0 : J // P, :], in_=wgo[0:1, :].rearrange("o (c p) -> (o c) p", p=P))
+        pages.append(keep.tile([P, T], F32, name="page0", align_bytes=ALIGN))
+        nc.gpsimd.memset(pages[0][:], 0.0)
 
         def scale_rows(scales):
             return scales.rearrange("a m n -> m a n").bitcast(I32)
 
         nc.scalar.dma_start(out=tab_s[TOP:P, :], in_=scale_rows(tab_scales))
-        nc.scalar.activation(warm[:], wgo_rows[:, 0:1], ACT.Sigmoid)
+        for w, scales in enumerate((wb_scales, wc_scales)):
+            nc.scalar.dma_start(out=staged[:, :, w * N // 4 : (w + 1) * N // 4], in_=scale_rows(scales))
+        nc.scalar.activation(warm[64:P, :], wgo_rows[64:P, 0:1], ACT.Sigmoid)
 
         def load_wa(g, a):
-            rows = wa[512 * a : 512 * (a + 1), g * WIDE : (g + 1) * WIDE]
-            nc.sync.dma_start(out=wa_raw[g, a][:], in_=rows.rearrange("(p i) n -> p i n", i=4))
+            rows = wa[512 * a : 512 * (a + 1), RANGES[g][0] : RANGES[g][1]]
+            nc.sync.dma_start(out=wa_raw[g, a][:, :, :], in_=rows.rearrange("(p i) n -> p i n", i=4))
 
         def load_wc(g):
-            cols = wc_words[:, :, g * WIDE : (g + 1) * WIDE, :]
+            cols = wc_words[:, :, WC_RANGES[g][0] : WC_RANGES[g][1], :]
             nc.sync.dma_start(out=wc_w[g][:, :, :], in_=cols.rearrange("a p n i -> p a (n i)").bitcast(I32))
 
         nc.sync.dma_start(src_list[:], offs)
         nc.sync.dma_start(dst_list[:], offs2)
-        for w, scales in enumerate((wb_scales, wc_scales)):
-            nc.sync.dma_start(out=staged[:, w * N // 4 : (w + 1) * N // 4], in_=scale_rows(scales))
-        nc.sync.dma_start(out=wgo_row[:], in_=wgo[0:1, :].rearrange("o (c p) -> (o c) p", p=P))
         nc.sync.dma_start(out=tab_w[:], in_=tab_words[0].rearrange("p t b -> p (t b)").bitcast(I32))
         load_wa(0, 0)
+        load_wa(0, 1)
+        load_wc(0)
 
         def spread_rows(plane_pair, rows):
             for q in range(4):
                 nc.sync.dma_start(out=plane_pair[32 * q : 32 * q + 4, :, :], in_=rows[8 * q : 8 * q + 8, :])
 
-        spread_rows(weight_planes, staged[:])
-        nc.scalar.copy(wgo_rows[0 : J // P, :], wgo_row[:])
-        held = after_raw.tile([P, RAW_BYTES // 4], I32, name="held", align_bytes=ALIGN, offset=0)
-        wc_w.append(held[:, 0 : PASSES * WIDE].rearrange("p (a w) -> p a w", a=PASSES))
-        wb_w = held[:, PASSES * WIDE :].rearrange("p (a w) -> p a w", a=PASSES)
-        wa_raw[0, 1] = after_raw.tile([P, 4, WIDE], F32, name="wa_raw1", align_bytes=ALIGN, offset=RAW_BYTES)
-        load_wa(0, 1)
-        load_wc(0)
-        nc.sync.dma_start(out=wb_w, in_=wb_words.rearrange("a p n -> p a n").bitcast(I32))
+        for q in range(4):
+            nc.sync.dma_start(out=weight_planes[32 * q : 32 * q + 4, :, :], in_=staged[4 * q : 4 * q + 4, :, :])
 
         def half_list(e, h):
             return lists[e][:, h * HALF // 16 : (h + 1) * HALF // 16]
@@ -145,7 +148,7 @@ def tile_list_rgg_relu_kernel(
         def round_wa(g, a, rounded):
             nc.scalar.copy(
                 rounded.rearrange("p (c u) i -> p c i u", u=4),
-                wa_raw[g, a][:].rearrange("p i (c u) -> p c i u", u=4),
+                wa_raw[g, a][:, :, :].rearrange("p i (c u) -> p c i u", u=4),
             )
 
         def quantise_wa(g, at, rounded):
@@ -154,39 +157,38 @@ def tile_list_rgg_relu_kernel(
                 out=wa_w[g][:, cols].bitcast(FP8X4), scales=wa_s[g][:, cols], in_=rounded.rearrange("p n i -> p (n i)")
             )
 
-        both_src = keep.tile([P, HALF], U32, name="both_src", tag="src", align_bytes=ALIGN)
-        both_dst = after_words.tile(
-            [P, HALF], U32, name="both_dst", align_bytes=ALIGN, offset=RAW_BYTES - WORD_BYTES // 2
-        )
+        both_src = after_src.tile([P, HALF], U32, name="both_src", align_bytes=ALIGN, offset=WORD_BYTES)
+        both_dst = keep.tile([P, HALF], U32, name="both_dst", align_bytes=ALIGN)
         pick_words(SRC, 0, both_src)
         pick_words(DST, 0, both_dst)
         part_words(SRC, 0, both_src, own_words(SRC, 0))
         part_words(DST, 0, both_dst, own_words(DST, 0))
-        for a in range(PASSES):
-            wa_raw[1, a] = after_words.tile(
-                [P, 4, WIDE], F32, name=f"wa_late{a}", align_bytes=ALIGN, offset=(1 - a) * RAW_BYTES
-            )
-            load_wa(1, a)
-        next_src = keep.tile([P, HALF], U32, name="next_src", tag="src", align_bytes=ALIGN)
+        next_src = after_src.tile([P, HALF], U32, name="next_src", align_bytes=ALIGN, offset=ALIGN)
         pick_words(SRC, 1, next_src)
 
-        early_at = PAGE_BYTES
-        early = after_picks.tile([P, PASSES * WIDE, 4], BF16, name="early", align_bytes=ALIGN, offset=early_at)
-        for a in range(PASSES):
-            round_wa(0, a, early[:, a * WIDE : (a + 1) * WIDE, :])
+        early_at = WORD_BYTES // 2
+        early = after_picks.tile([P, PASSES * P, 4], BF16, name="early", align_bytes=ALIGN, offset=early_at)
+        round_wa(0, 0, early[:, 0:P, :])
+        held = after_words.tile([P, HELD_BYTES // 4], I32, name="held", align_bytes=ALIGN, offset=0)
+        wb_w = held[:, 0:N].rearrange("p (a w) -> p a w", a=PASSES)
+        nc.sync.dma_start(out=wb_w, in_=wb_words.rearrange("a p n -> p a n").bitcast(I32))
+        wc_w.append(held[:, N:].rearrange("p (a w) -> p a w", a=PASSES))
+        load_wc(1)
+        rest_raw = after_words.tile([P, PASSES, 4, N - P], F32, name="rest_raw", align_bytes=ALIGN, offset=HELD_BYTES)
+        for g in (1, 2):
+            for a in range(PASSES):
+                wa_raw[g, a] = rest_raw[:, a, :, RANGES[g][0] - P : RANGES[g][1] - P]
+                load_wa(g, a)
+        round_wa(0, 1, early[:, P : 2 * P, :])
         quantise_wa(0, 0, early[:])
-        late_words_at = early_at + WORD_BYTES // 2 + ALIGN
+        late_words_at = early_at - WORD_BYTES // 2
         late_planes = after_picks.tile(
             [P, PASSES, 2 * HALF // 4], I32, name="late_planes", align_bytes=ALIGN, offset=late_words_at + WORD_BYTES
         )
         nc.gpsimd.memset(late_planes[:], 0)
         planes.append(late_planes)
-        pages.append(
-            after_picks.tile([P, T], F32, name="page0", align_bytes=ALIGN, offset=early_at - PAGE_BYTES + ALIGN)
-        )
-        nc.gpsimd.memset(pages[0][:], 0.0)
 
-        picked1_at = RAW_BYTES + WORD_BYTES
+        picked1_at = WORD_BYTES
         next_dst_at = picked1_at + PICKED_BYTES
         picked1 = after_raw.tile([P, PICKED_BYTES], U8, name="picked1", align_bytes=ALIGN, offset=picked1_at)
         next_dst = after_raw.tile([P, HALF], U32, name="next_dst", align_bytes=ALIGN, offset=next_dst_at)
@@ -200,8 +202,10 @@ def tile_list_rgg_relu_kernel(
             after_raw.tile([P, T], F32, name="page1", align_bytes=ALIGN, offset=next_dst_at + WORD_BYTES - ALIGN)
         )
         nc.gpsimd.memset(pages[1][:], 0.0)
-        wc_w.append(keep.tile([P, PASSES, WIDE], I32, name="wc_w1", tag="src", align_bytes=ALIGN))
-        load_wc(1)
+        middle = keep.tile([P, PASSES * P, 4], BF16, name="middle", align_bytes=ALIGN)
+        for a in range(PASSES):
+            round_wa(1, a, middle[:, a * P : (a + 1) * P, :])
+        quantise_wa(1, 0, middle[:])
 
         wgo_bank = psum.tile([P, HALF], F32, name="wgo_bank", tag="bank3")
         nc.tensor.transpose(wgo_bank[:, 0:P], wgo_rows[:], ident[:])
@@ -209,7 +213,8 @@ def tile_list_rgg_relu_kernel(
         nc.scalar.copy(wgo_cols[:], wgo_bank[:, 0 : J // P])
 
         def sum_message(t, h, bank, positive):
-            g, own = divmod(t * P, WIDE)
+            g = min(t, 1)
+            own = t * P - WC_RANGES[g][0]
             ms_bank = psum.tile([P, HALF], F32, name="ms_bank", tag=bank)
             for a in reversed(range(PASSES)):
                 for b in range(BLOCKS):
@@ -239,7 +244,9 @@ def tile_list_rgg_relu_kernel(
             nc.scalar.copy(messages[t][:, h * HALF : (h + 1) * HALF], turned[:])
 
         def sum_gate(t, h, bank):
-            g, own = divmod(t * P, WIDE)
+            g = min(t, 2)
+            own = t * P - RANGES[g][0]
+            wide = RANGES[g][1] - RANGES[g][0]
             za_bank = psum.tile([P, HALF], F32, name="za_bank", tag=bank)
             for a in reversed(range(PASSES)):
                 nc.tensor.matmul_mx(
@@ -254,8 +261,8 @@ def tile_list_rgg_relu_kernel(
             for a in range(PASSES):
                 nc.tensor.matmul_mx(
                     out=za_bank[:],
-                    lhsT=wa_w[g][:, a * WIDE + own : a * WIDE + own + P].bitcast(FP8X4),
-                    lhsT_scale=wa_s[g][:, a * WIDE + own : a * WIDE + own + P],
+                    lhsT=wa_w[g][:, a * wide + own : a * wide + own + P].bitcast(FP8X4),
+                    lhsT_scale=wa_s[g][:, a * wide + own : a * wide + own + P],
                     rhs=parted[DST, h][:, a, :].bitcast(FP4X4),
                     rhs_scale=scales_of(h, a, DST * HALF, HALF),
                     start=False,
@@ -276,8 +283,8 @@ def tile_list_rgg_relu_kernel(
 
         def late_pass(a):
             rounded = keep.tile([P, WIDE, 4], BF16, name=f"rounded{a}", tag=f"stage{a}", align_bytes=ALIGN)
-            round_wa(1, a, rounded[:])
-            quantise_wa(1, a * WIDE, rounded[:])
+            round_wa(2, a, rounded[:])
+            quantise_wa(2, a * WIDE, rounded[:])
 
         units = [(2 * g + s, h) for g in range(2) for h in range(2) for s in range(2)]
         message_bank, gate_bank, turn_bank = "bank0", "bank1", "bank2"
@@ -288,14 +295,14 @@ def tile_list_rgg_relu_kernel(
                 gate_bank, turn_bank = turn_bank, gate_bank
 
             if u == 0:
-                positive = after_raw.tile([P, HALF], F32, name="positive0", align_bytes=ALIGN, offset=RAW_BYTES)
+                positive = after_raw.tile([P, HALF], F32, name="positive0", align_bytes=ALIGN, offset=0)
             else:
                 positive = ring.tile([P, HALF], F32, name="positive")
             late_a = u - 1
             if 0 <= late_a < PASSES:
                 weighted = keep.tile([P, HALF], F32, name=f"weighted{u}", tag=f"stage{late_a}", align_bytes=ALIGN)
             elif late_a == PASSES:
-                weighted = after_words.tile([P, HALF], F32, name=f"weighted{u}", align_bytes=ALIGN, offset=0)
+                weighted = after_words.tile([P, HALF], F32, name=f"weighted{u}", align_bytes=ALIGN, offset=HELD_BYTES)
             else:
                 weighted = ring.tile([P, HALF], F32, name="weighted")
 

@@ -31,6 +31,8 @@ RANGES = ((0, P), (P, WIDE), (WIDE, N))
 WC_RANGES = ((0, P), (P, N))
 PAGES = 3
 SHORT = 3 * J // 8
+LEAD = 3 * J // 4
+SOURCES = ((0, LEAD), (LEAD, J))
 
 ALIGN = 64
 PAGE_BYTES = T * 4
@@ -60,7 +62,7 @@ def tile_list_rgg_relu_kernel(
         tab_s = keep.tile([P, T // 4], I32, name="tab_s", align_bytes=ALIGN)
         staged = keep.tile([SCALE_ROWS // PASSES, PASSES, 2 * N // 4], I32, name="staged", align_bytes=ALIGN)
         weight_planes = keep.tile([P, PASSES, 2 * N // 4], I32, name="weight_planes", align_bytes=ALIGN)
-        planes = [keep.tile([P, PASSES, 2 * HALF // 4], I32, name="planes0", align_bytes=ALIGN)]
+        planes = [keep.tile([P, PASSES, (LEAD + HALF) // 4], I32, name="planes0", align_bytes=ALIGN)]
         wa_raw = {
             (0, 0): after_words.tile([P, 4, P], F32, name="wa_raw0", align_bytes=ALIGN, offset=HELD_BYTES - WORD_BYTES // 2),
             (0, 1): after_raw.tile([P, 4, P], F32, name="wa_raw1", align_bytes=ALIGN, offset=WORD_BYTES - ALIGN),
@@ -117,15 +119,24 @@ def tile_list_rgg_relu_kernel(
             return lists[e][:, h * HALF // 16 : (h + 1) * HALF // 16]
 
         def pick_scales(h, picked):
-            for e in (SRC, DST):
-                nc.vector.tensor_copy(picked[:, e * HALF : (e + 1) * HALF], tab_s[:].bitcast(U8).indirect(half_list(e, h)))
+            first, last = SOURCES[h]
+            width = last - first
+            rows = tab_s[:].bitcast(U8)
+            nc.vector.tensor_copy(picked[:, 0:width], rows.indirect(src_list[:, first // 16 : last // 16]))
+            nc.vector.tensor_copy(picked[:, width:], rows.indirect(half_list(DST, h)))
 
-        picked0 = keep.tile([P, PICKED_BYTES], U8, name="picked0", align_bytes=ALIGN)
+        picked0 = keep.tile([P, LEAD + HALF], U8, name="picked0", align_bytes=ALIGN)
         pick_scales(0, picked0)
         spread_rows(planes[0], picked0[TOP:P, :].bitcast(I32))
 
-        def scales_of(h, a, at, width):
+        def source_scales(a, first, width):
+            h = int(first >= LEAD)
+            at = first - SOURCES[h][0]
             return planes[h][:, a, :].bitcast(U8)[:, at : at + width]
+
+        def target_scales(h, a):
+            at = SOURCES[h][1] - SOURCES[h][0]
+            return planes[h][:, a, :].bitcast(U8)[:, at : at + HALF]
 
         def weight_scales(a, at, width):
             return weight_planes[:, a, :].bitcast(U8)[:, at : at + width]
@@ -171,26 +182,27 @@ def tile_list_rgg_relu_kernel(
         round_wa(0, 0, early[:, 0:P, :])
         held = after_words.tile([P, HELD_BYTES // 4], I32, name="held", align_bytes=ALIGN, offset=0)
         wb_w = held[:, 0:N].rearrange("p (a w) -> p a w", a=PASSES)
-        nc.sync.dma_start(out=wb_w, in_=wb_words.rearrange("a p n -> p a n").bitcast(I32))
         wc_w.append(held[:, N:].rearrange("p (a w) -> p a w", a=PASSES))
-        load_wc(1)
         rest_raw = after_words.tile([P, PASSES, 4, N - P], F32, name="rest_raw", align_bytes=ALIGN, offset=HELD_BYTES)
         for g in (1, 2):
             for a in range(PASSES):
                 wa_raw[g, a] = rest_raw[:, a, :, RANGES[g][0] - P : RANGES[g][1] - P]
                 load_wa(g, a)
+            if g == 1:
+                nc.sync.dma_start(out=wb_w, in_=wb_words.rearrange("a p n -> p a n").bitcast(I32))
+                load_wc(1)
         round_wa(0, 1, early[:, P : 2 * P, :])
         quantise_wa(0, 0, early[:])
         late_words_at = early_at - WORD_BYTES // 2
         late_planes = after_picks.tile(
-            [P, PASSES, 2 * HALF // 4], I32, name="late_planes", align_bytes=ALIGN, offset=late_words_at + WORD_BYTES
+            [P, PASSES, (J - LEAD + HALF) // 4], I32, name="late_planes", align_bytes=ALIGN, offset=late_words_at + WORD_BYTES
         )
         nc.gpsimd.memset(late_planes[:], 0)
         planes.append(late_planes)
 
         picked1_at = WORD_BYTES
         next_dst_at = picked1_at + PICKED_BYTES
-        picked1 = after_raw.tile([P, PICKED_BYTES], U8, name="picked1", align_bytes=ALIGN, offset=picked1_at)
+        picked1 = after_raw.tile([P, J - LEAD + HALF], U8, name="picked1", align_bytes=ALIGN, offset=picked1_at)
         next_dst = after_raw.tile([P, HALF], U32, name="next_dst", align_bytes=ALIGN, offset=next_dst_at)
         pick_scales(1, picked1)
         spread_rows(planes[1], picked1[TOP:P, :].bitcast(I32))
@@ -221,7 +233,7 @@ def tile_list_rgg_relu_kernel(
                     nc.tensor.matmul_mx(
                         out=ms_bank[:, b * P : (b + 1) * P],
                         lhsT=parted[SRC, h][:, a, b * P : (b + 1) * P].bitcast(FP4X4),
-                        lhsT_scale=scales_of(h, a, b * P, P),
+                        lhsT_scale=source_scales(a, h * HALF + b * P, P),
                         rhs=wc_w[g][:, a, own : own + P].bitcast(FP8X4),
                         rhs_scale=weight_scales(a, N + t * P, P),
                         start=(a == PASSES - 1 and b == 0),
@@ -248,25 +260,28 @@ def tile_list_rgg_relu_kernel(
             own = t * P - RANGES[g][0]
             wide = RANGES[g][1] - RANGES[g][0]
             za_bank = psum.tile([P, HALF], F32, name="za_bank", tag=bank)
-            for a in reversed(range(PASSES)):
-                nc.tensor.matmul_mx(
-                    out=za_bank[:],
-                    lhsT=wb_w[:, a, t * P // 2 : (t + 1) * P // 2].bitcast(FP4X4),
-                    lhsT_scale=weight_scales(a, t * P, P),
-                    rhs=parted[SRC, h][:, a, :].bitcast(FP4X4),
-                    rhs_scale=scales_of(h, a, SRC * HALF, HALF),
-                    start=(a == PASSES - 1),
-                    stop=False,
+            cuts = (0, HALF) if h == 0 else (0, LEAD - HALF, HALF)
+            by_source = [
+                (
+                    wb_w[:, a, t * P // 2 : (t + 1) * P // 2].bitcast(FP4X4), weight_scales(a, t * P, P),
+                    parted[SRC, h][:, a, lo:hi], source_scales(a, h * HALF + lo, hi - lo), lo, hi,
                 )
-            for a in range(PASSES):
+                for a in reversed(range(PASSES))
+                for lo, hi in zip(cuts, cuts[1:])
+            ]
+            by_target = [
+                (
+                    wa_w[g][:, a * wide + own : a * wide + own + P].bitcast(FP8X4),
+                    wa_s[g][:, a * wide + own : a * wide + own + P],
+                    parted[DST, h][:, a, :], target_scales(h, a), 0, HALF,
+                )
+                for a in range(PASSES)
+            ]
+            steps = by_target + by_source if g == 0 else by_source + by_target
+            for s, (codes, scales, words, word_scales, lo, hi) in enumerate(steps):
                 nc.tensor.matmul_mx(
-                    out=za_bank[:],
-                    lhsT=wa_w[g][:, a * wide + own : a * wide + own + P].bitcast(FP8X4),
-                    lhsT_scale=wa_s[g][:, a * wide + own : a * wide + own + P],
-                    rhs=parted[DST, h][:, a, :].bitcast(FP4X4),
-                    rhs_scale=scales_of(h, a, DST * HALF, HALF),
-                    start=False,
-                    stop=(a == PASSES - 1),
+                    out=za_bank[:, lo:hi], lhsT=codes, lhsT_scale=scales, rhs=words.bitcast(FP4X4),
+                    rhs_scale=word_scales, start=(s == 0), stop=(s == len(steps) - 1),
                 )
             nc.scalar.activation(gates[t][:, h * HALF : (h + 1) * HALF], za_bank[:], ACT.Sigmoid)
 

@@ -49,8 +49,6 @@ def tile_list_rgg_relu_kernel(
     with ExitStack() as ctx:
         keep = ctx.enter_context(tc.tile_pool(name="keep", bufs=1))
         ring = ctx.enter_context(tc.tile_pool(name="ring", bufs=2))
-        after_picks = ctx.enter_context(tc.tile_pool(name="after_picks", bufs=1))
-        after_src = ctx.enter_context(tc.tile_pool(name="after_src", bufs=1))
         after_words = ctx.enter_context(tc.tile_pool(name="after_words", bufs=1))
         after_raw = ctx.enter_context(tc.tile_pool(name="after_raw", bufs=1))
         psum = ctx.enter_context(tc.psum_pool(name="psum", bufs=1))
@@ -78,10 +76,10 @@ def tile_list_rgg_relu_kernel(
         nc.gpsimd.memset(wgo_rows[:], 0.0)
         nc.gpsimd.memset(ident[:], 0.0)
         nc.gpsimd.memset(tab_s[0:TOP, :], 0)
+        nc.gpsimd.dma_start(out=wgo_rows[0 : J // P, :], in_=wgo[0:1, :].rearrange("o (c p) -> (o c) p", p=P))
         nc.gpsimd.memset(weight_planes[:], 0)
         nc.gpsimd.memset(planes[0][:], 0)
         make_identity(nc, ident[:], nomemset=True)
-        nc.gpsimd.dma_start(out=wgo_rows[0 : J // P, :], in_=wgo[0:1, :].rearrange("o (c p) -> (o c) p", p=P))
         pages.append(keep.tile([P, T], F32, name="page0", align_bytes=ALIGN))
         nc.gpsimd.memset(pages[0][:], 0.0)
 
@@ -144,7 +142,7 @@ def tile_list_rgg_relu_kernel(
         parted = {}
 
         def pick_words(e, h, both):
-            nc.vector.tensor_copy(both[:], tab_w[:].bitcast(U32).indirect(half_list(e, h)))
+            nc.vector.tensor_copy(both[:, :], tab_w[:].bitcast(U32).indirect(half_list(e, h)))
 
         def part_words(e, h, both, words):
             parted[e, h] = words
@@ -168,17 +166,14 @@ def tile_list_rgg_relu_kernel(
                 out=wa_w[g][:, cols].bitcast(FP8X4), scales=wa_s[g][:, cols], in_=rounded.rearrange("p n i -> p (n i)")
             )
 
-        both_src = after_src.tile([P, HALF], U32, name="both_src", align_bytes=ALIGN, offset=WORD_BYTES)
+        both_src = keep.tile([P, HALF], U32, name="both_src", align_bytes=ALIGN)
         both_dst = keep.tile([P, HALF], U32, name="both_dst", align_bytes=ALIGN)
         pick_words(SRC, 0, both_src)
         pick_words(DST, 0, both_dst)
         part_words(SRC, 0, both_src, own_words(SRC, 0))
         part_words(DST, 0, both_dst, own_words(DST, 0))
-        next_src = after_src.tile([P, HALF], U32, name="next_src", align_bytes=ALIGN, offset=ALIGN)
-        pick_words(SRC, 1, next_src)
 
-        early_at = WORD_BYTES // 2
-        early = after_picks.tile([P, PASSES * P, 4], BF16, name="early", align_bytes=ALIGN, offset=early_at)
+        early = keep.tile([P, PASSES * P, 4], BF16, name="early", tag="early", align_bytes=ALIGN)
         round_wa(0, 0, early[:, 0:P, :])
         held = after_words.tile([P, HELD_BYTES // 4], I32, name="held", align_bytes=ALIGN, offset=0)
         wb_w = held[:, 0:N].rearrange("p (a w) -> p a w", a=PASSES)
@@ -193,31 +188,29 @@ def tile_list_rgg_relu_kernel(
                 load_wc(1)
         round_wa(0, 1, early[:, P : 2 * P, :])
         quantise_wa(0, 0, early[:])
-        late_words_at = early_at - WORD_BYTES // 2
-        late_planes = after_picks.tile(
-            [P, PASSES, (J - LEAD + HALF) // 4], I32, name="late_planes", align_bytes=ALIGN, offset=late_words_at + WORD_BYTES
+        late_planes = keep.tile(
+            [P, PASSES, (J - LEAD + HALF) // 4], I32, name="late_planes", tag="early", align_bytes=ALIGN
         )
         nc.gpsimd.memset(late_planes[:], 0)
         planes.append(late_planes)
 
         picked1_at = WORD_BYTES
-        next_dst_at = picked1_at + PICKED_BYTES
         picked1 = after_raw.tile([P, J - LEAD + HALF], U8, name="picked1", align_bytes=ALIGN, offset=picked1_at)
-        next_dst = after_raw.tile([P, HALF], U32, name="next_dst", align_bytes=ALIGN, offset=next_dst_at)
+        next_both = after_raw.tile([P, 2 * HALF], U32, name="next_both", align_bytes=ALIGN, offset=picked1_at + PICKED_BYTES)
+        for e in (SRC, DST):
+            pick_words(e, 1, next_both[:, e * HALF : (e + 1) * HALF])
         pick_scales(1, picked1)
         spread_rows(planes[1], picked1[TOP:P, :].bitcast(I32))
-        pick_words(DST, 1, next_dst)
-        late_words = after_picks.tile([P, PASSES, HALF], U16, name="parted01", align_bytes=ALIGN, offset=late_words_at)
-        part_words(SRC, 1, next_src, late_words)
-        part_words(DST, 1, next_dst, own_words(DST, 1))
-        pages.append(
-            after_raw.tile([P, T], F32, name="page1", align_bytes=ALIGN, offset=next_dst_at + WORD_BYTES - ALIGN)
-        )
-        nc.gpsimd.memset(pages[1][:], 0.0)
-        middle = keep.tile([P, PASSES * P, 4], BF16, name="middle", align_bytes=ALIGN)
+        late_words = keep.tile([P, 2, PASSES, HALF], U16, name="late_words", align_bytes=ALIGN)
+        nc.vector.tensor_copy(late_words[:], next_both[:].bitcast(U16).rearrange("p (e j a) -> p e a j", e=2, a=PASSES))
+        for e in (SRC, DST):
+            parted[e, 1] = late_words[:, e, :, :]
+        middle = keep.tile([P, PASSES * P, 4], BF16, name="middle", tag="middle", align_bytes=ALIGN)
         for a in range(PASSES):
             round_wa(1, a, middle[:, a * P : (a + 1) * P, :])
         quantise_wa(1, 0, middle[:])
+        pages.append(keep.tile([P, T], F32, name="page1", tag="middle", align_bytes=ALIGN))
+        nc.gpsimd.memset(pages[1][:], 0.0)
 
         wgo_bank = psum.tile([P, HALF], F32, name="wgo_bank", tag="bank3")
         nc.tensor.transpose(wgo_bank[:, 0:P], wgo_rows[:], ident[:])

@@ -148,7 +148,7 @@ def tile_list_rgg_relu_kernel(
             parted[e, h] = words
             nc.vector.tensor_copy(
                 words[:].rearrange("p a (s j) -> p s a j", s=2),
-                both[:].bitcast(U16).rearrange("p (s j a) -> p s a j", s=2, a=PASSES),
+                both[:, :].bitcast(U16).rearrange("p (s j a) -> p s a j", s=2, a=PASSES),
             )
 
         def own_words(e, h):
@@ -197,14 +197,12 @@ def tile_list_rgg_relu_kernel(
         picked1_at = WORD_BYTES
         picked1 = after_raw.tile([P, J - LEAD + HALF], U8, name="picked1", align_bytes=ALIGN, offset=picked1_at)
         next_both = after_raw.tile([P, 2 * HALF], U32, name="next_both", align_bytes=ALIGN, offset=picked1_at + PICKED_BYTES)
-        for e in (SRC, DST):
-            pick_words(e, 1, next_both[:, e * HALF : (e + 1) * HALF])
         pick_scales(1, picked1)
         spread_rows(planes[1], picked1[TOP:P, :].bitcast(I32))
-        late_words = keep.tile([P, 2, PASSES, HALF], U16, name="late_words", align_bytes=ALIGN)
-        nc.vector.tensor_copy(late_words[:], next_both[:].bitcast(U16).rearrange("p (e j a) -> p e a j", e=2, a=PASSES))
         for e in (SRC, DST):
-            parted[e, 1] = late_words[:, e, :, :]
+            pick_words(e, 1, next_both[:, e * HALF : (e + 1) * HALF])
+        for e in (SRC, DST):
+            part_words(e, 1, next_both[:, e * HALF : (e + 1) * HALF], own_words(e, 1))
         middle = keep.tile([P, PASSES * P, 4], BF16, name="middle", tag="middle", align_bytes=ALIGN)
         for a in range(PASSES):
             round_wa(1, a, middle[:, a * P : (a + 1) * P, :])
@@ -299,7 +297,7 @@ def tile_list_rgg_relu_kernel(
         for u, (t, h) in enumerate(units):
             if (t, h) == (0, 1):
                 message_bank, turn_bank = turn_bank, message_bank
-            if t * P >= WIDE:
+            if (t, h) == (2, 0):
                 gate_bank, turn_bank = turn_bank, gate_bank
 
             if u == 0:

@@ -27,19 +27,14 @@ TOP = P - SCALE_ROWS
 SRC, DST = 0, 1
 
 WIDE = N // 2
-RANGES = ((0, P), (P, WIDE), (WIDE, N))
+WA_RANGES = ((0, P), (P, WIDE), (WIDE, N))
 WC_RANGES = ((0, P), (P, N))
 PAGES = 3
 SHORT = 3 * J // 8
-LEAD = 3 * J // 4
-SOURCES = ((0, LEAD), (LEAD, J))
 
 ALIGN = 64
-PAGE_BYTES = T * 4
-HELD_BYTES = PASSES * (2 * N + 4 * (N - P))
-RAW_BYTES = 4 * WIDE * 4
-WORD_BYTES = HALF * 4
-PICKED_BYTES = 2 * HALF
+LATER_BYTES = PASSES * (2 * N + 4 * (N - P))
+BANK_BYTES = HALF * 4
 
 
 def tile_list_rgg_relu_kernel(
@@ -49,8 +44,8 @@ def tile_list_rgg_relu_kernel(
     with ExitStack() as ctx:
         keep = ctx.enter_context(tc.tile_pool(name="keep", bufs=1))
         ring = ctx.enter_context(tc.tile_pool(name="ring", bufs=2))
-        after_words = ctx.enter_context(tc.tile_pool(name="after_words", bufs=1))
-        after_raw = ctx.enter_context(tc.tile_pool(name="after_raw", bufs=1))
+        after_raw0 = ctx.enter_context(tc.tile_pool(name="after_raw0", bufs=1))
+        after_raw1 = ctx.enter_context(tc.tile_pool(name="after_raw1", bufs=1))
         psum = ctx.enter_context(tc.psum_pool(name="psum", bufs=1))
 
         src_list = keep.tile([P, J // 16], U16, name="src_list")
@@ -60,15 +55,16 @@ def tile_list_rgg_relu_kernel(
         tab_s = keep.tile([P, T // 4], I32, name="tab_s", align_bytes=ALIGN)
         staged = keep.tile([SCALE_ROWS // PASSES, PASSES, 2 * N // 4], I32, name="staged", align_bytes=ALIGN)
         weight_planes = keep.tile([P, PASSES, 2 * N // 4], I32, name="weight_planes", align_bytes=ALIGN)
-        planes = [keep.tile([P, PASSES, (LEAD + HALF) // 4], I32, name="planes0", align_bytes=ALIGN)]
+        planes = [keep.tile([P, PASSES, (J + HALF) // 4], I32, name="planes0", align_bytes=ALIGN)]
+        raw0_at, raw1_at = LATER_BYTES - BANK_BYTES // 2, BANK_BYTES - ALIGN
         wa_raw = {
-            (0, 0): after_words.tile([P, 4, P], F32, name="wa_raw0", align_bytes=ALIGN, offset=HELD_BYTES - WORD_BYTES // 2),
-            (0, 1): after_raw.tile([P, 4, P], F32, name="wa_raw1", align_bytes=ALIGN, offset=WORD_BYTES - ALIGN),
+            (0, 0): after_raw0.tile([P, 4, P], F32, name="wa_raw0", align_bytes=ALIGN, offset=raw0_at),
+            (0, 1): after_raw1.tile([P, 4, P], F32, name="wa_raw1", align_bytes=ALIGN, offset=raw1_at),
         }
         wc_w = [keep.tile([P, PASSES, P], I32, name="wc_w0", align_bytes=ALIGN)]
         ident = keep.tile([P, P], F32, name="ident", align_bytes=ALIGN)
-        wa_w = [keep.tile([P, PASSES * (hi - lo)], U32, name=f"wa_w{lo}", align_bytes=ALIGN) for lo, hi in RANGES]
-        wa_s = [keep.tile([P, PASSES * (hi - lo)], U8, name=f"wa_s{lo}", align_bytes=ALIGN) for lo, hi in RANGES]
+        wa_w = [keep.tile([P, PASSES * (hi - lo)], U32, name=f"wa_w{lo}", align_bytes=ALIGN) for lo, hi in WA_RANGES]
+        wa_s = [keep.tile([P, PASSES * (hi - lo)], U8, name=f"wa_s{lo}", align_bytes=ALIGN) for lo, hi in WA_RANGES]
         pages = []
         wgo_rows = keep.tile([P, P], F32, name="wgo_rows")
         warm = keep.tile([P, 1], F32, name="warm")
@@ -92,7 +88,7 @@ def tile_list_rgg_relu_kernel(
         nc.scalar.activation(warm[64:P, :], wgo_rows[64:P, 0:1], ACT.Sigmoid)
 
         def load_wa(g, a):
-            rows = wa[512 * a : 512 * (a + 1), RANGES[g][0] : RANGES[g][1]]
+            rows = wa[512 * a : 512 * (a + 1), WA_RANGES[g][0] : WA_RANGES[g][1]]
             nc.sync.dma_start(out=wa_raw[g, a][:, :, :], in_=rows.rearrange("(p i) n -> p i n", i=4))
 
         def load_wc(g):
@@ -106,35 +102,30 @@ def tile_list_rgg_relu_kernel(
         load_wa(0, 1)
         load_wc(0)
 
-        def spread_rows(plane_pair, rows):
+        def spread_rows(pair, rows):
+            run = rows.shape[0] // 4
             for q in range(4):
-                nc.sync.dma_start(out=plane_pair[32 * q : 32 * q + 4, :, :], in_=rows[8 * q : 8 * q + 8, :])
+                nc.sync.dma_start(out=pair[32 * q : 32 * q + 4, :, :], in_=rows[run * q : run * (q + 1)])
 
-        for q in range(4):
-            nc.sync.dma_start(out=weight_planes[32 * q : 32 * q + 4, :, :], in_=staged[4 * q : 4 * q + 4, :, :])
+        spread_rows(weight_planes, staged[:])
 
         def half_list(e, h):
             return lists[e][:, h * HALF // 16 : (h + 1) * HALF // 16]
 
-        def pick_scales(h, picked):
-            first, last = SOURCES[h]
-            width = last - first
-            rows = tab_s[:].bitcast(U8)
-            nc.vector.tensor_copy(picked[:, 0:width], rows.indirect(src_list[:, first // 16 : last // 16]))
-            nc.vector.tensor_copy(picked[:, width:], rows.indirect(half_list(DST, h)))
+        def pick_scales(offsets, picked):
+            nc.vector.tensor_copy(picked, tab_s[:].bitcast(U8).indirect(offsets))
 
-        picked0 = keep.tile([P, LEAD + HALF], U8, name="picked0", align_bytes=ALIGN)
-        pick_scales(0, picked0)
+        picked0 = keep.tile([P, J + HALF], U8, name="picked0", align_bytes=ALIGN)
+        pick_scales(src_list[:], picked0[:, 0:J])
+        pick_scales(half_list(DST, 0), picked0[:, J:])
         spread_rows(planes[0], picked0[TOP:P, :].bitcast(I32))
 
         def source_scales(a, first, width):
-            h = int(first >= LEAD)
-            at = first - SOURCES[h][0]
-            return planes[h][:, a, :].bitcast(U8)[:, at : at + width]
+            return planes[0][:, a, :].bitcast(U8)[:, first : first + width]
 
         def target_scales(h, a):
-            at = SOURCES[h][1] - SOURCES[h][0]
-            return planes[h][:, a, :].bitcast(U8)[:, at : at + HALF]
+            plane = planes[h][:, a, :].bitcast(U8)
+            return plane[:, plane.shape[1] - HALF :]
 
         def weight_scales(a, at, width):
             return weight_planes[:, a, :].bitcast(U8)[:, at : at + width]
@@ -142,17 +133,14 @@ def tile_list_rgg_relu_kernel(
         parted = {}
 
         def pick_words(e, h, both):
-            nc.vector.tensor_copy(both[:, :], tab_w[:].bitcast(U32).indirect(half_list(e, h)))
+            nc.vector.tensor_copy(both, tab_w[:].bitcast(U32).indirect(half_list(e, h)))
 
-        def part_words(e, h, both, words):
-            parted[e, h] = words
+        def part_words(e, h, both):
+            parted[e, h] = keep.tile([P, PASSES, HALF], U16, name=f"parted{e}{h}", align_bytes=ALIGN)
             nc.vector.tensor_copy(
-                words[:].rearrange("p a (s j) -> p s a j", s=2),
-                both[:, :].bitcast(U16).rearrange("p (s j a) -> p s a j", s=2, a=PASSES),
+                parted[e, h][:].rearrange("p a (s j) -> p s a j", s=2),
+                both.bitcast(U16).rearrange("p (s j a) -> p s a j", s=2, a=PASSES),
             )
-
-        def own_words(e, h):
-            return keep.tile([P, PASSES, HALF], U16, name=f"parted{e}{h}", align_bytes=ALIGN)
 
         def round_wa(g, a, rounded):
             nc.scalar.copy(
@@ -166,43 +154,38 @@ def tile_list_rgg_relu_kernel(
                 out=wa_w[g][:, cols].bitcast(FP8X4), scales=wa_s[g][:, cols], in_=rounded.rearrange("p n i -> p (n i)")
             )
 
-        both_src = keep.tile([P, HALF], U32, name="both_src", align_bytes=ALIGN)
-        both_dst = keep.tile([P, HALF], U32, name="both_dst", align_bytes=ALIGN)
-        pick_words(SRC, 0, both_src)
-        pick_words(DST, 0, both_dst)
-        part_words(SRC, 0, both_src, own_words(SRC, 0))
-        part_words(DST, 0, both_dst, own_words(DST, 0))
+        first_both = [keep.tile([P, HALF], U32, name=f"first_both{e}", align_bytes=ALIGN) for e in (SRC, DST)]
+        for e in (SRC, DST):
+            pick_words(e, 0, first_both[e][:])
+        for e in (SRC, DST):
+            part_words(e, 0, first_both[e][:])
 
         early = keep.tile([P, PASSES * P, 4], BF16, name="early", tag="early", align_bytes=ALIGN)
         round_wa(0, 0, early[:, 0:P, :])
-        held = after_words.tile([P, HELD_BYTES // 4], I32, name="held", align_bytes=ALIGN, offset=0)
-        wb_w = held[:, 0:N].rearrange("p (a w) -> p a w", a=PASSES)
-        wc_w.append(held[:, N:].rearrange("p (a w) -> p a w", a=PASSES))
-        rest_raw = after_words.tile([P, PASSES, 4, N - P], F32, name="rest_raw", align_bytes=ALIGN, offset=HELD_BYTES)
+        later = after_raw0.tile([P, LATER_BYTES // 4], I32, name="later", align_bytes=ALIGN, offset=0)
+        wb_w = later[:, 0:N].rearrange("p (a w) -> p a w", a=PASSES)
+        wc_w.append(later[:, N:].rearrange("p (a w) -> p a w", a=PASSES))
+        rest_raw = after_raw0.tile([P, PASSES, 4, N - P], F32, name="rest_raw", align_bytes=ALIGN, offset=LATER_BYTES)
         for g in (1, 2):
             for a in range(PASSES):
-                wa_raw[g, a] = rest_raw[:, a, :, RANGES[g][0] - P : RANGES[g][1] - P]
+                wa_raw[g, a] = rest_raw[:, a, :, WA_RANGES[g][0] - P : WA_RANGES[g][1] - P]
                 load_wa(g, a)
             if g == 1:
                 nc.sync.dma_start(out=wb_w, in_=wb_words.rearrange("a p n -> p a n").bitcast(I32))
                 load_wc(1)
         round_wa(0, 1, early[:, P : 2 * P, :])
         quantise_wa(0, 0, early[:])
-        late_planes = keep.tile(
-            [P, PASSES, (J - LEAD + HALF) // 4], I32, name="late_planes", tag="early", align_bytes=ALIGN
-        )
-        nc.gpsimd.memset(late_planes[:], 0)
-        planes.append(late_planes)
+        planes.append(keep.tile([P, PASSES, HALF // 4], I32, name="planes1", tag="early", align_bytes=ALIGN))
+        nc.gpsimd.memset(planes[1][:], 0)
 
-        picked1_at = WORD_BYTES
-        picked1 = after_raw.tile([P, J - LEAD + HALF], U8, name="picked1", align_bytes=ALIGN, offset=picked1_at)
-        next_both = after_raw.tile([P, 2 * HALF], U32, name="next_both", align_bytes=ALIGN, offset=picked1_at + PICKED_BYTES)
-        pick_scales(1, picked1)
+        picked1 = after_raw1.tile([P, HALF], U8, name="picked1", align_bytes=ALIGN, offset=BANK_BYTES)
+        next_both = after_raw1.tile([P, 2 * HALF], U32, name="next_both", align_bytes=ALIGN, offset=3 * BANK_BYTES // 2)
+        pick_scales(half_list(DST, 1), picked1[:])
         spread_rows(planes[1], picked1[TOP:P, :].bitcast(I32))
         for e in (SRC, DST):
             pick_words(e, 1, next_both[:, e * HALF : (e + 1) * HALF])
         for e in (SRC, DST):
-            part_words(e, 1, next_both[:, e * HALF : (e + 1) * HALF], own_words(e, 1))
+            part_words(e, 1, next_both[:, e * HALF : (e + 1) * HALF])
         middle = keep.tile([P, PASSES * P, 4], BF16, name="middle", tag="middle", align_bytes=ALIGN)
         for a in range(PASSES):
             round_wa(1, a, middle[:, a * P : (a + 1) * P, :])
@@ -248,39 +231,36 @@ def tile_list_rgg_relu_kernel(
 
         def sum_gate(t, h, bank):
             g = min(t, 2)
-            own = t * P - RANGES[g][0]
-            wide = RANGES[g][1] - RANGES[g][0]
+            own = t * P - WA_RANGES[g][0]
+            wide = WA_RANGES[g][1] - WA_RANGES[g][0]
             za_bank = psum.tile([P, HALF], F32, name="za_bank", tag=bank)
-            cuts = (0, HALF) if h == 0 else (0, LEAD - HALF, HALF)
             by_source = [
                 (
                     wb_w[:, a, t * P // 2 : (t + 1) * P // 2].bitcast(FP4X4), weight_scales(a, t * P, P),
-                    parted[SRC, h][:, a, lo:hi], source_scales(a, h * HALF + lo, hi - lo), lo, hi,
+                    parted[SRC, h][:, a, :], source_scales(a, h * HALF, HALF),
                 )
                 for a in reversed(range(PASSES))
-                for lo, hi in zip(cuts, cuts[1:])
             ]
             by_target = [
                 (
                     wa_w[g][:, a * wide + own : a * wide + own + P].bitcast(FP8X4),
                     wa_s[g][:, a * wide + own : a * wide + own + P],
-                    parted[DST, h][:, a, :], target_scales(h, a), 0, HALF,
+                    parted[DST, h][:, a, :], target_scales(h, a),
                 )
                 for a in range(PASSES)
             ]
-            steps = by_target + by_source if g == 0 else by_source + by_target
-            for s, (codes, scales, words, word_scales, lo, hi) in enumerate(steps):
+            steps = by_target + by_source if t == 0 else by_source + by_target
+            for s, (codes, scales, words, word_scales) in enumerate(steps):
                 nc.tensor.matmul_mx(
-                    out=za_bank[:, lo:hi], lhsT=codes, lhsT_scale=scales, rhs=words.bitcast(FP4X4),
+                    out=za_bank[:], lhsT=codes, lhsT_scale=scales, rhs=words.bitcast(FP4X4),
                     rhs_scale=word_scales, start=(s == 0), stop=(s == len(steps) - 1),
                 )
             nc.scalar.activation(gates[t][:, h * HALF : (h + 1) * HALF], za_bank[:], ACT.Sigmoid)
 
         def place(t, first, last):
             page = pages[t % PAGES]
-            nc.vector.tensor_tensor(
-                page[:].indirect(dst_list[:, first // 16 : last // 16]), gates[t][:, first:last], messages[t][:, first:last], MULT
-            )
+            places = page[:].indirect(dst_list[:, first // 16 : last // 16])
+            nc.vector.tensor_tensor(places, gates[t][:, first:last], messages[t][:, first:last], MULT)
             if last == J:
                 nc.sync.dma_start(out=out[t * P : (t + 1) * P, :], in_=page[:])
 
@@ -301,14 +281,14 @@ def tile_list_rgg_relu_kernel(
                 gate_bank, turn_bank = turn_bank, gate_bank
 
             if u == 0:
-                positive = after_raw.tile([P, HALF], F32, name="positive0", align_bytes=ALIGN, offset=0)
+                positive = after_raw1.tile([P, HALF], F32, name="positive0", align_bytes=ALIGN, offset=0)
             else:
                 positive = ring.tile([P, HALF], F32, name="positive")
             late_a = u - 1
             if 0 <= late_a < PASSES:
                 weighted = keep.tile([P, HALF], F32, name=f"weighted{u}", tag=f"stage{late_a}", align_bytes=ALIGN)
             elif late_a == PASSES:
-                weighted = after_words.tile([P, HALF], F32, name=f"weighted{u}", align_bytes=ALIGN, offset=HELD_BYTES)
+                weighted = after_raw0.tile([P, HALF], F32, name=f"weighted{u}", align_bytes=ALIGN, offset=LATER_BYTES)
             else:
                 weighted = ring.tile([P, HALF], F32, name="weighted")
 

from contextlib import ExitStack

import concourse.mybir as mybir
from concourse.masks import make_identity

K, N, T, J = 1024, 512, 2048, 1024
FLOPS = 3 * 2 * K * N * J

F32 = mybir.dt.float32
BF16 = mybir.dt.bfloat16
I32 = mybir.dt.int32
U32 = mybir.dt.uint32
U16 = mybir.dt.uint16
U8 = mybir.dt.uint8
FP8X4 = mybir.dt.float8_e4m3fn_x4
FP4X4 = mybir.dt.float4_e2m1fn_x4
ACT = mybir.ActivationFunctionType
MULT = mybir.AluOpType.mult

P = 128
PASSES = K // 512
HALF = J // 2
BLOCKS = HALF // P
ROW_TILES = N // P
SCALE_ROWS = K // 32
TOP = P - SCALE_ROWS
SRC, DST = 0, 1

WIDE = N // 2
WA_RANGES = ((0, P), (P, WIDE), (WIDE, N))
WC_RANGES = ((0, P), (P, N))
PAGES = 3
SHORT = 3 * J // 8

ALIGN = 64
LATER_BYTES = PASSES * (2 * N + 4 * (N - P))
BANK_BYTES = HALF * 4


def tile_list_rgg_relu_kernel(
    tc, tab_words, tab_scales, wa, wb_words, wb_scales, wc_words, wc_scales, wgo, offs, offs2, out
):
    nc = tc.nc
    with ExitStack() as ctx:
        keep = ctx.enter_context(tc.tile_pool(name="keep", bufs=1))
        ring = ctx.enter_context(tc.tile_pool(name="ring", bufs=2))
        after_raw0 = ctx.enter_context(tc.tile_pool(name="after_raw0", bufs=1))
        after_raw1 = ctx.enter_context(tc.tile_pool(name="after_raw1", bufs=1))
        psum = ctx.enter_context(tc.psum_pool(name="psum", bufs=1))

        src_list = keep.tile([P, J // 16], U16, name="src_list")
        dst_list = keep.tile([P, J // 16], U16, name="dst_list")
        lists = (src_list, dst_list)
        tab_w = keep.tile([P, T], I32, name="tab_w", align_bytes=ALIGN)
        tab_s = keep.tile([P, T // 4], I32, name="tab_s", align_bytes=ALIGN)
        staged = keep.tile([SCALE_ROWS // PASSES, PASSES, 2 * N // 4], I32, name="staged", align_bytes=ALIGN)
        weight_planes = keep.tile([P, PASSES, 2 * N // 4], I32, name="weight_planes", align_bytes=ALIGN)
        planes = [keep.tile([P, PASSES, (J + HALF) // 4], I32, name="planes0", align_bytes=ALIGN)]
        raw0_at, raw1_at = LATER_BYTES - BANK_BYTES // 2, BANK_BYTES - ALIGN
        wa_raw = {
            (0, 0): after_raw0.tile([P, 4, P], F32, name="wa_raw0", align_bytes=ALIGN, offset=raw0_at),
            (0, 1): after_raw1.tile([P, 4, P], F32, name="wa_raw1", align_bytes=ALIGN, offset=raw1_at),
        }
        wc_w = [keep.tile([P, PASSES, P], I32, name="wc_w0", align_bytes=ALIGN)]
        ident = keep.tile([P, P], F32, name="ident", align_bytes=ALIGN)
        wa_w = [keep.tile([P, PASSES * (hi - lo)], U32, name=f"wa_w{lo}", align_bytes=ALIGN) for lo, hi in WA_RANGES]
        wa_s = [keep.tile([P, PASSES * (hi - lo)], U8, name=f"wa_s{lo}", align_bytes=ALIGN) for lo, hi in WA_RANGES]
        pages = []
        wgo_rows = keep.tile([P, P], F32, name="wgo_rows")
        warm = keep.tile([P, 1], F32, name="warm")

        nc.gpsimd.memset(wgo_rows[:], 0.0)
        nc.gpsimd.memset(ident[:], 0.0)
        nc.gpsimd.memset(tab_s[0:TOP, :], 0)
        nc.gpsimd.dma_start(out=wgo_rows[0 : J // P, :], in_=wgo[0:1, :].rearrange("o (c p) -> (o c) p", p=P))
        nc.gpsimd.memset(weight_planes[:], 0)
        nc.gpsimd.memset(planes[0][:], 0)
        make_identity(nc, ident[:], nomemset=True)
        pages.append(keep.tile([P, T], F32, name="page0", align_bytes=ALIGN))
        nc.gpsimd.memset(pages[0][:], 0.0)

        def scale_rows(scales):
            return scales.rearrange("a m n -> m a n").bitcast(I32)

        nc.scalar.dma_start(out=tab_s[TOP:P, :], in_=scale_rows(tab_scales))
        for w, scales in enumerate((wb_scales, wc_scales)):
            nc.scalar.dma_start(out=staged[:, :, w * N // 4 : (w + 1) * N // 4], in_=scale_rows(scales))
        nc.scalar.activation(warm[64:P, :], wgo_rows[64:P, 0:1], ACT.Sigmoid)

        def load_wa(g, a):
            rows = wa[512 * a : 512 * (a + 1), WA_RANGES[g][0] : WA_RANGES[g][1]]
            nc.sync.dma_start(out=wa_raw[g, a][:, :, :], in_=rows.rearrange("(p i) n -> p i n", i=4))

        def load_wc(g):
            cols = wc_words[:, :, WC_RANGES[g][0] : WC_RANGES[g][1], :]
            nc.sync.dma_start(out=wc_w[g][:, :, :], in_=cols.rearrange("a p n i -> p a (n i)").bitcast(I32))

        nc.sync.dma_start(src_list[:], offs)
        nc.sync.dma_start(dst_list[:], offs2)
        nc.sync.dma_start(out=tab_w[:], in_=tab_words[0].rearrange("p t b -> p (t b)").bitcast(I32))
        load_wa(0, 0)
        load_wa(0, 1)
        load_wc(0)

        def spread_rows(pair, rows):
            run = rows.shape[0] // 4
            for q in range(4):
                nc.sync.dma_start(out=pair[32 * q : 32 * q + 4, :, :], in_=rows[run * q : run * (q + 1)])

        spread_rows(weight_planes, staged[:])

        def half_list(e, h):
            return lists[e][:, h * HALF // 16 : (h + 1) * HALF // 16]

        def pick_scales(offsets, picked):
            nc.vector.tensor_copy(picked, tab_s[:].bitcast(U8).indirect(offsets))

        picked0 = keep.tile([P, J + HALF], U8, name="picked0", align_bytes=ALIGN)
        pick_scales(src_list[:], picked0[:, 0:J])
        pick_scales(half_list(DST, 0), picked0[:, J:])
        spread_rows(planes[0], picked0[TOP:P, :].bitcast(I32))

        def source_scales(a, first, width):
            return planes[0][:, a, :].bitcast(U8)[:, first : first + width]

        def target_scales(h, a):
            plane = planes[h][:, a, :].bitcast(U8)
            return plane[:, plane.shape[1] - HALF :]

        def weight_scales(a, at, width):
            return weight_planes[:, a, :].bitcast(U8)[:, at : at + width]

        parted = {}

        def pick_words(e, h, both):
            nc.vector.tensor_copy(both, tab_w[:].bitcast(U32).indirect(half_list(e, h)))

        def part_words(e, h, both):
            parted[e, h] = keep.tile([P, PASSES, HALF], U16, name=f"parted{e}{h}", align_bytes=ALIGN)
            nc.vector.tensor_copy(
                parted[e, h][:].rearrange("p a (s j) -> p s a j", s=2),
                both.bitcast(U16).rearrange("p (s j a) -> p s a j", s=2, a=PASSES),
            )

        def round_wa(g, a, rounded):
            nc.scalar.copy(
                rounded.rearrange("p (c u) i -> p c i u", u=4),
                wa_raw[g, a][:, :, :].rearrange("p i (c u) -> p c i u", u=4),
            )

        def quantise_wa(g, at, rounded):
            cols = slice(at, at + rounded.shape[1])
            nc.vector.quantize_mx(
                out=wa_w[g][:, cols].bitcast(FP8X4), scales=wa_s[g][:, cols], in_=rounded.rearrange("p n i -> p (n i)")
            )

        first_both = [keep.tile([P, HALF], U32, name=f"first_both{e}", align_bytes=ALIGN) for e in (SRC, DST)]
        for e in (SRC, DST):
            pick_words(e, 0, first_both[e][:])
        for e in (SRC, DST):
            part_words(e, 0, first_both[e][:])

        early = keep.tile([P, PASSES * P, 4], BF16, name="early", tag="early", align_bytes=ALIGN)
        round_wa(0, 0, early[:, 0:P, :])
        later = after_raw0.tile([P, LATER_BYTES // 4], I32, name="later", align_bytes=ALIGN, offset=0)
        wb_w = later[:, 0:N].rearrange("p (a w) -> p a w", a=PASSES)
        wc_w.append(later[:, N:].rearrange("p (a w) -> p a w", a=PASSES))
        rest_raw = after_raw0.tile([P, PASSES, 4, N - P], F32, name="rest_raw", align_bytes=ALIGN, offset=LATER_BYTES)
        for g in (1, 2):
            for a in range(PASSES):
                wa_raw[g, a] = rest_raw[:, a, :, WA_RANGES[g][0] - P : WA_RANGES[g][1] - P]
                load_wa(g, a)
            if g == 1:
                nc.sync.dma_start(out=wb_w, in_=wb_words.rearrange("a p n -> p a n").bitcast(I32))
                load_wc(1)
        round_wa(0, 1, early[:, P : 2 * P, :])
        quantise_wa(0, 0, early[:])
        planes.append(keep.tile([P, PASSES, HALF // 4], I32, name="planes1", tag="early", align_bytes=ALIGN))
        nc.gpsimd.memset(planes[1][:], 0)

        picked1 = after_raw1.tile([P, HALF], U8, name="picked1", align_bytes=ALIGN, offset=BANK_BYTES)
        next_both = after_raw1.tile([P, 2 * HALF], U32, name="next_both", align_bytes=ALIGN, offset=3 * BANK_BYTES // 2)
        pick_scales(half_list(DST, 1), picked1[:])
        spread_rows(planes[1], picked1[TOP:P, :].bitcast(I32))
        for e in (SRC, DST):
            pick_words(e, 1, next_both[:, e * HALF : (e + 1) * HALF])
        for e in (SRC, DST):
            part_words(e, 1, next_both[:, e * HALF : (e + 1) * HALF])
        middle = keep.tile([P, PASSES * P, 4], BF16, name="middle", tag="middle", align_bytes=ALIGN)
        for a in range(PASSES):
            round_wa(1, a, middle[:, a * P : (a + 1) * P, :])
        quantise_wa(1, 0, middle[:])
        pages.append(keep.tile([P, T], F32, name="page1", tag="middle", align_bytes=ALIGN))
        nc.gpsimd.memset(pages[1][:], 0.0)

        wgo_bank = psum.tile([P, HALF], F32, name="wgo_bank", tag="bank3")
        nc.tensor.transpose(wgo_bank[:, 0:P], wgo_rows[:], ident[:])
        wgo_cols = keep.tile([P, J // P], F32, name="wgo_cols")
        nc.scalar.copy(wgo_cols[:], wgo_bank[:, 0 : J // P])

        def sum_message(t, h, bank, positive):
            g = min(t, 1)
            own = t * P - WC_RANGES[g][0]
            ms_bank = psum.tile([P, HALF], F32, name="ms_bank", tag=bank)
            for a in reversed(range(PASSES)):
                for b in range(BLOCKS):
                    nc.tensor.matmul_mx(
                        out=ms_bank[:, b * P : (b + 1) * P],
                        lhsT=parted[SRC, h][:, a, b * P : (b + 1) * P].bitcast(FP4X4),
                        lhsT_scale=source_scales(a, h * HALF + b * P, P),
                        rhs=wc_w[g][:, a, own : own + P].bitcast(FP8X4),
                        rhs_scale=weight_scales(a, N + t * P, P),
                        start=(a == PASSES - 1 and b == 0),
                        stop=(a == 0 and b == BLOCKS - 1),
                    )
            nc.scalar.activation(positive[:], ms_bank[:], ACT.Relu)

        def weigh(h, positive, weighted):
            for b in range(BLOCKS):
                c = h * BLOCKS + b
                nc.scalar.activation(
                    weighted[:, b * P : (b + 1) * P], positive[:, b * P : (b + 1) * P], ACT.Copy,
                    scale=wgo_cols[:, c : c + 1],
                )

        def turn(t, h, bank, weighted):
            turned = psum.tile([P, HALF], F32, name="turned", tag=bank)
            for b in range(BLOCKS):
                nc.tensor.transpose(turned[:, b * P : (b + 1) * P], weighted[:, b * P : (b + 1) * P], ident[:])
            nc.scalar.copy(messages[t][:, h * HALF : (h + 1) * HALF], turned[:])

        def sum_gate(t, h, bank):
            g = min(t, 2)
            own = t * P - WA_RANGES[g][0]
            wide = WA_RANGES[g][1] - WA_RANGES[g][0]
            za_bank = psum.tile([P, HALF], F32, name="za_bank", tag=bank)
            by_source = [
                (
                    wb_w[:, a, t * P // 2 : (t + 1) * P // 2].bitcast(FP4X4), weight_scales(a, t * P, P),
                    parted[SRC, h][:, a, :], source_scales(a, h * HALF, HALF),
                )
                for a in reversed(range(PASSES))
            ]
            by_target = [
                (
                    wa_w[g][:, a * wide + own : a * wide + own + P].bitcast(FP8X4),
                    wa_s[g][:, a * wide + own : a * wide + own + P],
                    parted[DST, h][:, a, :], target_scales(h, a),
                )
                for a in range(PASSES)
            ]
            steps = by_target + by_source if t == 0 else by_source + by_target
            for s, (codes, scales, words, word_scales) in enumerate(steps):
                nc.tensor.matmul_mx(
                    out=za_bank[:], lhsT=codes, lhsT_scale=scales, rhs=words.bitcast(FP4X4),
                    rhs_scale=word_scales, start=(s == 0), stop=(s == len(steps) - 1),
                )
            nc.scalar.activation(gates[t][:, h * HALF : (h + 1) * HALF], za_bank[:], ACT.Sigmoid)

        def place(t, first, last):
            page = pages[t % PAGES]
            places = page[:].indirect(dst_list[:, first // 16 : last // 16])
            nc.vector.tensor_tensor(places, gates[t][:, first:last], messages[t][:, first:last], MULT)
            if last == J:
                nc.sync.dma_start(out=out[t * P : (t + 1) * P, :], in_=page[:])

        gates = [keep.tile([P, J], F32, name=f"gate{t}") for t in range(ROW_TILES)]
        messages = [keep.tile([P, J], F32, name=f"message{t}") for t in range(ROW_TILES)]

        def late_pass(a):
            rounded = keep.tile([P, WIDE, 4], BF16, name=f"rounded{a}", tag=f"stage{a}", align_bytes=ALIGN)
            round_wa(2, a, rounded[:])
            quantise_wa(2, a * WIDE, rounded[:])

        units = [(2 * g + s, h) for g in range(2) for h in range(2) for s in range(2)]
        message_bank, gate_bank, turn_bank = "bank0", "bank1", "bank2"
        for u, (t, h) in enumerate(units):
            if (t, h) == (0, 1):
                message_bank, turn_bank = turn_bank, message_bank
            if (t, h) == (2, 0):
                gate_bank, turn_bank = turn_bank, gate_bank

            if u == 0:
                positive = after_raw1.tile([P, HALF], F32, name="positive0", align_bytes=ALIGN, offset=0)
            else:
                positive = ring.tile([P, HALF], F32, name="positive")
            late_a = u - 1
            if 0 <= late_a < PASSES:
                weighted = keep.tile([P, HALF], F32, name=f"weighted{u}", tag=f"stage{late_a}", align_bytes=ALIGN)
            elif late_a == PASSES:
                weighted = after_raw0.tile([P, HALF], F32, name=f"weighted{u}", align_bytes=ALIGN, offset=LATER_BYTES)
            else:
                weighted = ring.tile([P, HALF], F32, name="weighted")

            sum_message(t, h, message_bank, positive)
            weigh(h, positive, weighted)
            sum_gate(t, h, gate_bank)
            turn(t, h, turn_bank, weighted)
            split = SHORT if t == ROW_TILES - 1 else HALF
            place(t, h * split, split + h * (J - split))
            if 0 <= late_a < PASSES:
                late_pass(late_a)
            if late_a == 0:
                pages.append(keep.tile([P, T], F32, name="page2", tag="stage0", align_bytes=ALIGN))
                nc.gpsimd.memset(pages[2][:], 0.0)
